import numpy as np, ml_dtypes
CORES = [16,17,18,19,32,33,34,35]
N = 8
BF = ml_dtypes.bfloat16
V, P, L, RO, Q, CAP = 2048, 4096, 224, 2, 2, 48
H, ST = 2048, 9
MS, PO = (7, 7, 8, 9, 10, 11, 12, 14), 20
def rings(rng, hole):
    pool = 1 + np.argsort(rng.random((8, 16, 255)), axis=-1)[..., :PO]
    ms = np.stack([rng.permutation(np.array(MS)) for r in range(N)])
    pal = np.take_along_axis(np.broadcast_to(pool, (N, 8, 16, PO)), np.argsort(rng.random((N, 8, 16, PO)), axis=-1), 3)
    k = np.take_along_axis(pal, (rng.random((N, 8, 16, V)) * ms[:, :, None, None]).astype(np.int64), 3)
    u = rng.random((N, 8, 16, V))
    return np.where(u < hole, 0, np.where(u < hole + 0.05, rng.integers(1, 256, (N, 8, 16, V)), k))
def parts(rng, hole=0.12):
    t = rng.choice(np.array([0, 300, 500, 700, 850]), (N, 8, 16, 1)) + rng.integers(0, 100, (N, 8, 16, 1))
    return rings(rng, hole), rng.integers(0, V, (N, 8, 16, V)), rng.integers(0, 256, (N, 8, 16, P)), rng.integers(0, 256, (N, 8, 16, L)), t
def pack(k, b, x, z, t):
    def bf(a): return np.ascontiguousarray(a.reshape(N, 128, -1)).astype(np.float32).astype(BF)
    return {"ring": bf(k), "nbr": np.ascontiguousarray(b.reshape(N, 128, V)).astype(np.int32), "mat": bf(x), "z0": bf(z), "thr": np.ascontiguousarray(t.reshape(N, 128, 1)).astype(np.int32)}
def setup_inputs(rng):
    return pack(*parts(rng))
def setup_inputs_spread(rng):
    k, b, x, z, t = parts(rng)
    e = rng.integers(5, 13, (N, 8, 1, 1)); ix = np.minimum((255 * rng.random((N, 8, 16, V)) ** e).astype(np.int64), 254)
    keys = 1 + np.argsort(rng.random((8, 16, 255)), axis=-1)
    k = np.take_along_axis(np.broadcast_to(keys, (N, 8, 16, 255)), ix, 3)
    k = np.where(rng.random((N, 8, 16, V)) < rng.random((N, 8, 1, V)) ** 3, 0, k)
    b[:, ::2] = np.minimum((V * rng.random((N, 4, 16, V)) ** 2).astype(np.int64), V - 1)
    x = np.minimum((np.exp2(8 * rng.random((N, 8, 1, P))) * rng.random((N, 8, 16, P))).astype(np.int64), 255)
    z = np.minimum((np.exp2(8 * rng.random((N, 8, 1, L))) * rng.random((N, 8, 16, L))).astype(np.int64), 255)
    t = np.minimum(np.exp2(12 * rng.random((N, 8, 16, 1))).astype(np.int64), 4095)
    return pack(k, b, x, z, t)
def setup_inputs_ends(rng):
    k, b, x, z, t = parts(rng)
    c = rng.random((N, 8, 1, V)); dens = rng.choice(np.array([0.25, 0.25, 0.5]), (N, 8, 1, V))
    k = np.where(c < 0.25, 255, np.where(c < 0.4, 0, np.where(c < 0.85, 255 * (rng.random((N, 8, 16, V)) < dens), k)))
    k[:, 6, :, 2 * ST:ST * (L - 4):ST] = 255
    b = np.where(rng.random((N, 8, 16, V)) < 0.7, (V - 1) * rng.integers(0, 2, (N, 8, 16, V)), b)
    share = np.array([0.5, 0, 0.5, 0, 0, 0, 0, 0]).reshape(8, 1, 1)
    x = np.where(rng.random((N, 8, 1, P)) < share + 0.05, 255 * rng.integers(0, 2, (N, 8, 1, P)), 255 * rng.integers(0, 2, (N, 8, 16, P)))
    z = np.where(rng.random((N, 8, 1, L)) < share, 255 * rng.integers(0, 2, (N, 8, 1, L)), 255 * rng.integers(0, 2, (N, 8, 16, L)))
    t = np.broadcast_to(4095 * (rng.random((1, 8, 16, 1)) < 0.25), (N, 8, 16, 1)); t = np.where(rng.random((N, 8, 16, 1)) < 0.05, 4095 - t, t)
    t[:, 0, 0] = 4095; t[:, 7, 14] = 0; t[:, 7, 15] = 4095
    k[..., V - 1] = 255; k[..., 0] = 255 * (np.argsort(np.argsort(rng.random((N, 8, 16)), axis=-1), axis=-1) < 5)
    x[..., 0] = 0; x[..., P - 1] = 255
    p = np.arange(16)
    for lane in (1, L - 1):
        v = ST * lane; z[..., lane] = 255; k[..., v] = 0; b[:, :, 0, v] = V - 1
        x[..., ((255 * (2 * v + 1) >> 2) + 811 * p) & (P - 1)] = 0 if lane == 1 else 255 * ((p + 1) & 1)
    z[..., 0] = 0; z[..., L - 2] = 0; k[..., ST * (L - 2)] = 0
    a = (15 + Q) >> 1; v = ST * (L - 4); z[..., L - 4] = 0
    k[..., v] = 255 * (p < a); k[..., V - 2] = 255 * (p >= 16 - a); b[:, :, 0, v] = V - 2
    k[..., V - 3] = 255; k[..., V - 4] = 255; b[:, :, 0, V - 2] = V - 2
    for i, u in ((1, V - 1), (14, V - 3), (15, V - 4)): b[:, :, i, V - 2] = u
    return pack(k, b, x, z, t)
def setup_inputs_corners(rng):
    k, b, x, z, t = parts(rng)
    code = rng.integers(1, 256, (N, 8, 16, 1)); code[:, ::2] = code[:1, ::2]; row = np.arange(16)[:, None]
    u = rng.random((N, 8, 1, V))
    k = np.where((row < Q) | (u < 0.33), code, np.where(u < 0.66, rng.integers(1, 256, (N, 8, 16, V)), 0))
    own = np.broadcast_to(np.arange(V), (16, V)); many = (0, 1, CAP - 1, CAP, CAP + 1, L, CAP, L >> 1)
    for r in range(N):
        for g in range(8):
            n = many[(g + r) & 7]; lanes = rng.permutation(L)[:n]; vf = ST * lanes
            if g & 3 == 1: b[r, g] = np.where(rng.random((16, V)) < 0.5, own, b[r, g])
            if g & 3 == 2: b[r, g] = np.where(rng.random((16, V)) < 0.3, (V - 1) * rng.integers(0, 2, (16, V)), b[r, g])
            if g & 3 == 3: b[r, g] = np.where(rng.random((16, V)) < 0.5, rng.integers(0, V, (1, V)), b[r, g])
            gone = np.zeros(V, bool); gone[vf] = True
            b[r, g] = b[r, g] + gone[b[r, g]]
            if g & 3 == 1: b[r, g][:, vf[::2]] = vf[::2]
            k[r, g][:, vf] = np.where((row < Q - 1) & (rng.random(n) < 0.5), code[r, g], 0)
    t = np.where(rng.random((N, 8, 16, 1)) < 0.5, rng.choice(np.array([0, 1, 15, 600, 1000, 4095]), (N, 8, 16, 1)), t); t[:, ::2, :Q] = 0; t[:, 1, 15] = 4095
    x = np.where(rng.random((N, 8, 1, P)) < 0.2, rng.choice(np.array([0, 128, 255]), (N, 8, 1, P)), x)
    z = np.where(rng.random((N, 8, 1, L)) < 0.3, rng.choice(np.array([0, 1, 254, 255]), (N, 8, 1, L)), z)
    return pack(k, b, x, z, t)
def setup_inputs_crowd(rng):
    k, b, x, z, t = parts(rng, 0.22)
    k = np.where(rng.random((N, 8, 1, V)) < 0.03, 0, k)
    hubs = np.argsort(rng.random((N, 8, V)), axis=-1)[..., :12]
    h = np.take_along_axis(hubs, rng.integers(0, 12, (N, 8, 16 * V)), 2).reshape(N, 8, 16, V)
    b = np.where(rng.random((N, 8, 16, V)) < 0.6, h, b)
    x[:, 1::2] = np.take_along_axis(x[:, 1::2], np.broadcast_to(rng.integers(0, 8, (N, 4, 1, P)), (N, 4, 16, P)), 3)
    z[..., 1::2] = z[..., ::2]
    return pack(k, b, x, z, t)
def setup_inputs_far(rng):
    k, b, x, z, t = parts(rng); a = (15 + Q) >> 1; kk = np.arange(16)[:, None]
    up = rng.integers(0, 2, (N, 8, 1, 1)); up[0, 0] = 0; up[N - 1, 7] = 1
    x = rng.integers(0, 48, (N, 8, 16, P)) + 208 * up; z = rng.integers(0, 48, (N, 8, 16, L)) + 208 * (1 - up)
    t = np.where(rng.random((N, 8, 16, 1)) < 0.4, rng.integers(3000, 3500, (N, 8, 16, 1)), t)
    first = ST * np.arange(L); rest = np.setdiff1d(np.arange(V), first)
    for r in range(N):
        for g in range(8):
            if (g + r) & 1: continue
            code = rng.integers(1, 256, (16, 1)); o = rng.permutation(16)[:, None]
            rare = 1 + (code - 1 + rng.integers(1, 255, (16, V))) % 255
            other = np.where(rng.random((16, V)) < 0.7, 0, rare)
            u = rng.permutation(rest); q = len(u) >> 2; near = u[:q]; full = u[q:2 * q]; right = u[2 * q:3 * q]
            kr = k[r, g]; br = b[r, g]
            kr[:, first] = np.where(o < a, code, other[:, first])
            kr[:, right] = np.where(o >= 16 - a, code, other[:, right])
            kr[:, full] = code
            kr[:, near] = np.where(o == rng.integers(a, 16, q), rare[:, near], code)
            e = ST * rng.permutation(L)[:L >> 4]
            kr[:, e[::2]] = 0; kr[:, e[1::2]] = code
            br[:, first] = rng.choice(right, (16, L))
            i = rng.integers(0, 15, q); m = i + 1 + (rng.random(q) * (15 - i)).astype(np.int64)
            pick = rng.random((16, q)); low = rng.choice(near, (16, q)); top = rng.choice(full, (16, q)); poor = rng.choice(np.concatenate([first, u[2 * q:]]), (16, q))
            late = np.where((kk == m) | (pick < 0.4), top, np.where(pick < 0.7, low, poor))
            early = np.where((kk == i) | ((kk > i) & (pick < 0.5)), low, poor)
            br[:, right] = np.where(kk < m, early, late)
    return pack(k, b, x, z, t)
def check_inputs(d):
    bad = []
    for k, lo, hi in (("ring", 0, 255), ("nbr", 0, V - 1), ("mat", 0, 255), ("z0", 0, 255), ("thr", 0, 4095)):
        a = np.asarray(d[k]).astype(np.float64)
        if not (np.min(a) >= lo and np.max(a) <= hi): bad.append("range of " + k)
        elif np.any(a != np.floor(a)): bad.append("whole numbers in " + k)
    return bad
def columns(a, ix):
    return np.take_along_axis(a, ix[:, :, None, :], 3)
def by_lane(a):
    return np.ascontiguousarray(a.transpose(0, 1, 3, 2)).reshape(N, 8, L * 16)
def reference(ring, nbr, mat, z0, thr):
    K = ring.astype(np.float32).astype(np.int64).reshape(N, 8, 16, V); B = nbr.astype(np.int64).reshape(N, 8, 16, V)
    X = mat.astype(np.float32).astype(np.int64).reshape(N, 8, 16, P); z = z0.astype(np.float32).astype(np.int64).reshape(N, 8, 16, L)
    th = thr.astype(np.int64).reshape(N, 8, 16, 1); v = np.array(np.broadcast_to(ST * np.arange(L), (N, 8, L)))
    failures = np.zeros(N, np.int64); rv_old = np.zeros((N, 8, 16), np.int64); row = np.arange(16)[:, None]
    for t in range(RO):
        j = (np.sum(z, axis=2) + t) & 15
        n = np.take_along_axis(columns(B, v), j[:, :, None, :], 2)[:, :, 0]
        Kv = columns(K, v); Kn = columns(K, n)
        direct = np.sum((Kv == Kn) & (Kv > 0), axis=2) >= Q
        cand = by_lane(columns(B, n)); Kc = columns(K, cand).reshape(N, 8, 16, L, 16)
        score = np.minimum(np.sum((Kc == Kv[..., None]) & (Kc > 0), axis=2), np.sum((Kc == Kn[..., None]) & (Kc > 0), axis=2))
        k = np.argmax(score, axis=3)
        bridged = ~direct & (np.max(score, axis=3) >= Q); failed = ~direct & ~bridged
        w = np.where(bridged, np.take_along_axis(cand.reshape(N, 8, L, 16), k[..., None], 3)[..., 0], n)
        Kw = columns(K, w)
        place = (((Kw * (2 * v + 1)[:, :, None, :]) >> 2) + 811 * row + t) & (P - 1)
        Xc = columns(X, by_lane(place)).reshape(N, 8, 16, L, 16)
        d = np.sum(np.abs(Xc - z[..., None]), axis=2)
        p = np.argmin(d, axis=3)
        x = np.take_along_axis(Xc, p[:, :, None, :, None], 4)[..., 0]
        caught = (d.transpose(0, 1, 3, 2) < th + (failures & 15)[:, None, None, None]) & (Kw > 0)
        low = np.argmax(caught, axis=3)
        rv = np.where(np.any(caught, axis=3), np.take_along_axis(Kw, low[..., None], 3)[..., 0], 0)
        fi = failed.astype(np.int64); served = failed & (np.add.accumulate(fi, axis=2) - fi < CAP)
        h = np.sum(Kw * z, axis=2) & (H - 1)
        given = columns(np.roll(K, -1, axis=0), h)
        filled = np.where(Kv > 0, Kv, np.where(bridged[:, :, None, :], Kw, given))
        K2 = np.array(K); B2 = np.array(B); active = bridged | served
        for a in range(N):
            for g in range(8):
                i = np.nonzero(active[a, g])[0]
                u, first = np.unique(v[a, g, i], return_index=True); i = i[first]
                K2[a, g][:, u] = filled[a, g][:, i]
                i = i[bridged[a, g, i]]; B2[a, g, j[a, g, i], v[a, g, i]] = w[a, g, i]
        come = np.roll(rv_old, 1, axis=0)
        K = np.where((K2 == rv[..., None]) | (K2 == come[..., None]), 0, K2); B = B2
        z = (z + x) >> 1; v = w; rv_old = rv; failures = np.sum(fi, axis=(1, 2))
    return {"yk": K.reshape(N, 128, V).astype(np.float32).astype(BF), "yz": z.reshape(N, 128, L).astype(np.float32)}

@@ -1,0 +1,628 @@
+from concourse.mybir import AluOpType as ALU, AxisListType, ActivationFunctionType as AF
+
+L, V = 224, 2048
+CH = [(0, 128), (128, 224)]
+BASE = [0, 17 * 128]
+NXT = 17 * 224
+SCRATCH, SMALL, PLAN = {}, {}, []
+SPLIT = ("M2", "MM", "PR", "PI", "PJ", "ZS", "ZI")
+for _n, _w, _d in (
+        ("ringS", V + L, "bfloat16"), ("nbrS", V + L, "int32"), ("matS", 4096, "bfloat16"), ("thrI", 1, "int32"),
+        ("num", V + L, "float32"), ("BIG0", NXT + V, "bfloat16"), ("BIG1", NXT + V, "bfloat16"),
+        ("zb0", L, "bfloat16"), ("zb1", L, "bfloat16"), ("zf", L, "float32"), ("XC0", 2048, "bfloat16"), ("XC1", 1536, "bfloat16"),
+        ("ones", 256, "bfloat16"), ("sel1", 144, "bfloat16"), ("selk", 144, "bfloat16"), ("selm", 144, "bfloat16"),
+        ("blk", 128, "bfloat16"), ("blkz", 128, "bfloat16"), ("blkf", 128, "float32"), ("trid", 128, "bfloat16"),
+        ("idn", 128, "bfloat16"), ("nidn", 128, "bfloat16"), ("l16", 128, "bfloat16"), ("cn", L, "bfloat16"), ("chh", L, "bfloat16"),
+        ("rowA", 128, "bfloat16"), ("rowB", 128, "bfloat16"), ("rneg", L, "float32"), ("rmul", L, "float32"), ("ramp", L, "bfloat16"),
+        ("tri", L, "bfloat16"), ("zer", 16, "float32"), ("pI", 1, "int32"), ("qI", 1, "int32"), ("qc", 1, "float32"),
+        ("pc0", 1, "float32"), ("pc1", 1, "float32"), ("tp0", 1, "float32"), ("tp1", 1, "float32"), ("pk", 1, "float32"),
+        ("thr0", 1, "float32"), ("thr1", 1, "float32"), ("tmpc", 1, "float32"), ("rowc", 16, "float32"),
+        ("iW", 14, "float32"), ("nk", 14, "float32"), ("dW", 14, "float32"), ("cb", 14, "float32"), ("vW0", 14, "float32"),
+        ("vW1", 14, "float32"), ("V20", L, "float32"), ("V21", L, "float32"),
+        ("JI", L, "int32"), ("JM", L, "int32"), ("YY", L, "float32"), ("SW", L, "float32"), ("nW", 14, "float32"),
+        ("noff", 14, "uint16"), ("Bn", L, "uint16"), ("BnF", L, "float32"), ("BvT", L, "int32"), ("KvT", L, "bfloat16"),
+        ("hv", L, "bfloat16"), ("hn", L, "bfloat16"), ("E3", L, "bfloat16"),
+        ("M2", L, "float32"), ("MM", L, "float32"), ("SK", L, "float32"), ("SD", L, "float32"),
+        ("posU", 14, "uint16"), ("KI", 14, "int32"), ("KA", 14, "int32"), ("KK", 14, "int32"), ("xn", 14, "float32"),
+        ("bb", 14, "float32"), ("nb", 14, "float32"), ("nd", 14, "float32"), ("PR", L, "float32"), ("PI", L, "int32"),
+        ("PJ", L, "int32"), ("ths", 14, "float32"), ("thn", 14, "float32"), ("taB", 14, "float32"), ("taD", 14, "float32"), ("YW", L, "float32"), ("PL", L, "uint16"), ("KwT", L, "bfloat16"), ("DI", 14, "int32"), ("DA", 14, "int32"),
+        ("pxU", 14, "uint16"), ("ZS", L, "float32"), ("ZI", L, "int32"),
+        ("NZ", L, "bfloat16"), ("N1", L, "bfloat16"), ("cap", L, "float32"), ("com", L, "float32"), ("rvc", 1, "float32"),
+        ("rvi", 1, "int32"), ("rvj", 1, "int32"), ("rv0", 4, "float32"), ("rv1", 4, "float32"), ("come", 4, "float32"), ("HZ", L, "float32"),
+        ("SH", L, "float32"), ("HI", 14, "int32"), ("HJ", 14, "int32"), ("FF", 14, "bfloat16"), ("Finc", 14, "bfloat16"),
+        ("srv", 14, "float32"), ("th", 14, "float32"), ("sp", 14, "float32"), ("spU", 14, "uint16"),
+        ("SRC", L, "bfloat16"), ("FP", L, "bfloat16"), ("ta", 14, "float32"), ("oKf", 14, "float32"), ("oKU", 28, "uint16"),
+        ("oBU", 14, "uint16"), ("oB2", 14, "float32"), ("cdU", 14, "uint16"), ("cdR", L, "float32"), ("mk", L, "float32"), ("SV", L, "float32"),
+        ("voff", 14, "uint16"), ("wR", L, "float32"), ("Bm", L, "float32"), ("Bs", L, "float32"), ("Bx", L, "int32"),
+        ("fc", 1, "float32"), ("fi", 1, "int32"), ("fj", 1, "int32"),
+        ("rpI", L, "int32"), ("rp", 14, "uint16"), ("vh", L, "float32"), ("va", L, "float32"), ("eq", L, "float32"), ("SE", L, "float32"),
+        ("e0", V, "bfloat16"), ("e1", V, "bfloat16"), ("ykS", V, "bfloat16"), ("vWp", 16, "float32")):
+    if _w in (1, 14) and _d != "uint16" and _n not in ("thrI", "FF", "Finc"):
+        _b = "small" + _d
+        SMALL[_n] = (_b, 16 * len(SMALL), _w)
+        SCRATCH[_b] = ("sbuf", [128, 16 * len(SMALL)], _d)
+    else:
+        SCRATCH[_n] = ("sbuf", [128, _w], _d)
+for _n in ("E1", "E2", "DD"):
+    SCRATCH[_n] = ("sbuf", [128, L, 16], "bfloat16")
+BANKS = ("PZ", "PK", "PC0", "PC1", "PD0", "PD1", "PA", "PM")
+for _n in BANKS:
+    SCRATCH[_n] = ("psum", [128, 512], "float32")
+SEMAPHORES = ["sV", "sS", "sP", "sG", "xr0", "xr1", "xl0", "xl1", "rr", "rl"] + ["d%d" % i for i in range(16)]
+
+
+def rank_program(g, core, T, topo):
+    rank = T.rank_of(core)
+    if rank is None:
+        return
+    N = len(T.cores)
+    queue = {"V": g.vector, "S": g.scalar, "P": g.tensor, "G": g, "Y": g.sync}
+    semof = {"V": "sV", "S": "sS", "P": "sP", "G": "sG"}
+    total = {}
+    known = {e: {} for e in queue}
+    log = {}
+
+    def need(e, refs, write):
+        out = []
+        for name, lo, hi, tag in refs:
+            for (l2, h2, w2, e2, s2, c2, k2, t2) in log.get(name, ()):
+                if name in BANKS:
+                    if e2 == e and (write or not w2):
+                        continue
+                else:
+                    if not (l2 < hi and lo < h2) or not (write or w2):
+                        continue
+                    if tag and t2 and tag[0] == t2[0] and tag[1] != t2[1]:
+                        continue
+                    if e2 == e and s2 == semof.get(e) and not w2:
+                        continue
+                out.append((s2, c2, k2))
+        return out
+
+    def note(e, refs, write, s, c, snap):
+        for name, lo, hi, tag in refs:
+            acc = log.setdefault(name, [])
+            if name in BANKS:
+                acc[:] = [a for a in acc if not (a[3] == e and a[2] == write)]
+            elif write:
+                acc[:] = [a for a in acc if not (lo <= a[0] and a[1] <= hi and tag in (None, a[7]))]
+            else:
+                acc[:] = [a for a in acc if a[2] or not (a[3] == e and a[4] == s and lo <= a[0] and a[1] <= hi and tag in (None, a[7]))]
+            acc.append((lo, hi, write, e, s, c, snap, tag))
+
+    def waits(e, deps):
+        todo = {}
+        for s, c, k in deps:
+            if known[e].get(s, 0) < c and todo.get(s, (0,))[0] < c:
+                todo[s] = (c, k)
+        for s in list(todo):
+            c = todo[s][0]
+            if any(o != s and todo[o][1].get(s, 0) >= c for o in todo):
+                del todo[s]
+        for s, (c, k) in todo.items():
+            queue[e].wait_ge(T.sem[s], c)
+            for a, b in k.items():
+                known[e][a] = max(known[e].get(a, 0), b)
+            known[e][s] = max(known[e].get(s, 0), c)
+
+    ops = []
+
+    def emit(e, fn, reads, writes, sem=None, inc=1, cost=0.06, lat=0.1):
+        ops.append((e, fn, [r[1:] for r in reads], [r[1:] for r in writes], sem or semof[e], inc, cost, lat))
+
+    def issue(e, fn, rd, wr, s, inc, cost, lat):
+        if e != "R":
+            waits(e, need(e, rd, False) + need(e, wr, True))
+            ins = fn()
+            if ins is not None:
+                ins.then_inc(T.sem[s], inc)
+        total[s] = total.get(s, 0) + inc
+        snap = dict(known[e]) if e != "R" else {}
+        snap[s] = total[s]
+        note(e, rd, False, s, total[s], snap)
+        note(e, wr, True, s, total[s], snap)
+
+    def order():
+        succ, npred, acc = [[] for _ in ops], [0] * len(ops), {}
+        for i, (e, fn, rd, wr, s, inc, cost, lat) in enumerate(ops):
+            before = {}
+            for refs, write in ((rd, False), (wr, True)):
+                for name, lo, hi, tag in refs:
+                    for (l2, h2, w2, j, t2) in acc.get(name, ()):
+                        same = ops[j][0] == e
+                        if name in BANKS:
+                            if same and not (write and w2):
+                                continue
+                            d = 0.0 if same else ops[j][7]
+                        else:
+                            if not (l2 < hi and lo < h2) or not (write or w2) or (tag and t2 and tag[0] == t2[0] and tag[1] != t2[1]):
+                                continue
+                            d = 0.0 if same and not w2 else ops[j][7]
+                        before[j] = max(before.get(j, 0.0), d)
+            for refs, write in ((rd, False), (wr, True)):
+                for name, lo, hi, tag in refs:
+                    a = acc.setdefault(name, [])
+                    if write and name in BANKS:
+                        a[:] = [x for x in a if ops[x[3]][0] == e and not x[2]]
+                    elif write:
+                        a[:] = [x for x in a if not (lo <= x[0] and x[1] <= hi and tag in (None, x[4]))]
+                    a.append((lo, hi, write, i, tag))
+            for j, d in before.items():
+                if j != i:
+                    succ[j].append((i, d))
+                    npred[i] += 1
+        rank_ = [0.0] * len(ops)
+        for i in range(len(ops) - 1, -1, -1):
+            rank_[i] = ops[i][6] + max([d + rank_[k] for k, d in succ[i]] + [0.0])
+        ready = {e: [] for e in ("V", "S", "P", "G", "Y", "R")}
+        rt, free, out = [0.0] * len(ops), {e: 0.0 for e in ready}, []
+        for i, n in enumerate(npred):
+            if n == 0:
+                ready[ops[i][0]].append(i)
+        while len(out) < len(ops):
+            start, e = min((max(free[e], min(rt[i] for i in ready[e])), e) for e in ready if ready[e])
+            i = min(ready[e]) if e == "Y" else max((k for k in ready[e] if rt[k] <= start + 0.01), key=lambda k: (rank_[k], -k))
+            ready[e].remove(i)
+            out.append(i)
+            end = max(start, rt[i]) + ops[i][6]
+            free[e] = end
+            for k, d in succ[i]:
+                rt[k] = max(rt[k], end + d)
+                npred[k] -= 1
+                if npred[k] == 0:
+                    ready[ops[k][0]].append(k)
+        return out
+
+    def width(r):
+        return r[3] - r[2] if r[4] is None or r[4][0] in ("k", "q") else (r[3] - r[2] + r[4][0] - 1) // r[4][0]
+
+    def wide(*refs):
+        return all(SCRATCH[r[1]][0] == "sbuf" and SCRATCH[r[1]][2] in ("bfloat16", "uint16") for r in refs)
+
+    def vcost(n, per):
+        return 0.00083 * max(64, n * per)
+
+    def R(name, lo=0, hi=None, step=1, p=None):
+        if name in SPLIT and lo == 0 and hi == 96:
+            lo, hi = 128, 224
+        if name in SMALL:
+            name, off, w = SMALL[name]
+            lo, hi = lo + off, off + (w if hi is None else hi)
+        hi = T[name].shape[1] if hi is None else hi
+        ps = slice(None) if p is None else slice(0, p)
+        ap = T[name][ps, lo:hi] if step == 1 else T[name][ps, lo:hi:step]
+        return (ap, name, lo, hi, None if step == 1 else (step, lo % step))
+
+    def X(name, lo, hi, off):
+        return (T[name][:, lo:hi].indirect(off[0]), name, lo, hi, None)
+
+    def E3d(name, l0, l1, k=None, q=None):
+        ap = T[name][:, l0:l1, k] if k is not None else T[name][:, l0 + q:l1:16, :]
+        return (ap, name, l0, l1, ("q", q) if k is None else ("k", k))
+
+    def cols(*xs):
+        return [x for x in xs if isinstance(x, tuple)]
+
+    def val(x):
+        return x[0] if isinstance(x, tuple) else x
+
+    def ts(out, a, s1, s2, op0, op1=None):
+        rd = [a] + cols(s1, s2)
+        c = vcost(width(out), 0.5 if wide(out, a) else 1)
+        if op1 is None:
+            emit("V", lambda: g.vector.tensor_scalar(out[0], a[0], val(s1), None, op0), rd, [out], cost=c)
+        else:
+            emit("V", lambda: g.vector.tensor_scalar(out[0], a[0], val(s1), val(s2), op0, op1), rd, [out], cost=c)
+
+    def tt(out, a, b, op, off=()):
+        n = width(b)
+        c = vcost(n, 1 if a[1] in BANKS or b[1] in BANKS else 2)
+        if off:
+            c = 0.05 + vcost(n, 1.6 if a[3] - a[2] > n else 3.8)
+        emit("V", lambda: g.vector.tensor_tensor(out[0], a[0], b[0], op), [a, b] + list(off), [out], cost=c)
+
+    def cp(out, a, off=()):
+        n = min(width(out), width(a))
+        c = 0.05 + vcost(n, 1.6 if width(out) <= width(a) else 3.8) if off else vcost(n, 0.5 if wide(out, a) else 1)
+        emit("V", lambda: g.vector.tensor_copy(out[0], a[0]), [a] + list(off), [out], cost=c)
+
+    def scan(out, d0, d1, op0, op1):
+        emit("V", lambda: g.vector.tensor_tensor_scan(out[0], d0[0], d1[0], 0.0, op0, op1), [d0, d1], [out], cost=vcost(width(out), 1))
+
+    def red(out, a, op):
+        emit("V", lambda: g.vector.tensor_reduce(out[0], a[0], AxisListType.X, op), [a], [out], cost=vcost(width(a), 1))
+
+    def ac(out, a, func=AF.Copy, off=(), **kw):
+        n = width(out)
+        emit("S", lambda: g.scalar.activation(out[0], a[0], func, **kw), [a] + list(off), [out], cost=0.065 + vcost(n, 1.6) if off else vcost(n, 1))
+
+    def fill(out, c):
+        emit("V", lambda: g.vector.memset(out[0], c), [], [out], cost=vcost(width(out), 1))
+
+    def mm(out, lhsT, rhs, start, stop):
+        c = 0.00042 * max(64, width(out)) * (1 if wide(rhs) else 4)
+        emit("P", lambda: g.tensor.matmul(out[0], lhsT[0], rhs[0], start, stop), [lhsT, rhs], [out], cost=c)
+
+    def iota(out, pattern, base, cm):
+        c = 0.13 + vcost(width(out), 2)
+        emit("G", lambda: g.iota(out[0], pattern, base, cm, allow_small_or_imprecise_dtypes=True), [], [out], cost=c)
+
+    def asel(out, a, pattern, op, fillv, base, cm):
+        c = 0.17 + vcost(width(out), 2)
+        emit("G", lambda: g.affine_select(out[0], a[0], pattern, op, fillv, base, cm), [a], [out], cost=c)
+
+    ndma = [0]
+
+    def dma(e, out, a, rd=(), wr=()):
+        s = "d%d" % ndma[0]
+        ndma[0] += 1
+        n = sum(width(r) for r in wr)
+        emit(e, lambda: queue[e].dma_start(out, a), list(rd), list(wr), s, 16, lat=2.0 + n * 0.002)
+
+    def remote(out_ap, src, rsem, lsem, dst):
+        rid, pid, _ = topo.addr(dst)
+
+        def call():
+            g.remote_dma(out_ap, src[0], T.sem[rsem], T.sem[lsem], pid, rid, topo.mask(core, dst))
+        emit("G", call, [src], [(None, lsem, 0, 1, None)], lsem, len(topo.engines(core, dst)), 1.0, 9.0)
+
+    def landed(name, lo, hi, rsem, lsem, src):
+        emit("R", None, [(None, lsem, 0, 1, None)], [(None, name, lo, hi, None)], rsem, len(topo.engines(src, core)), 0.0, 0.0)
+
+    prev, nxt = T.cores[(rank - 1) % N], T.cores[(rank + 1) % N]
+    dma("Y", T.zb0[:, :], T.z0[:, :], wr=[R("zb0")])
+    dma("Y", T.nbrS[:, 0:V], T.nbr[:, :], wr=[R("nbrS", 0, V)])
+    dma("Y", T.ringS[:, 0:V], T.ring[:, :], wr=[R("ringS", 0, V)])
+    dma("Y", T.matS[:, :], T.mat[:, :], wr=[R("matS")])
+    dma("Y", T.thrI[:, :], T.thr[:, :], wr=[R("thrI")])
+    fill(R("ones"), 1.0)
+    fill(R("sel1"), 0.0)
+    fill(R("sel1", 15, 143, 16), 1.0)
+    iota(R("pI"), [[1, 1]], 0, 1)
+    o8 = R("ones", 0, 128)
+    asel(R("blk"), o8, [[-16, 8], [0, 16]], ALU.is_ge, 0.0, 0, 1)
+    asel(R("blk"), R("blk"), [[16, 8], [0, 16]], ALU.is_ge, 0.0, 15, -1)
+    asel(R("idn"), o8, [[-1, 128]], ALU.is_equal, 0.0, 0, 1)
+    asel(R("l16", p=16), R("ones", 0, 128, p=16), [[0, 8], [-1, 16]], ALU.is_equal, 0.0, 0, 1)
+    asel(R("cn", p=16), R("ones", 0, L, p=16), [[0, 14], [-1, 16]], ALU.is_equal, 0.0, 0, 1)
+    s8 = R("sel1", 15, 143, 16)
+    asel(s8, s8, [[-16, 8]], ALU.is_ge, 0.0, 0, 1)
+    asel(s8, s8, [[16, 8]], ALU.is_ge, 0.0, 15, -1)
+    iota(R("rowA"), [[-256, 8], [0, 16]], 1792, 0)
+    iota(R("rowB"), [[0, 8], [-1, 16]], 255, -16)
+    iota(R("rowc", 0, 14), [[16, 14]], 0, 0)
+    iota(R("V20"), [[18, L]], 1, 0)
+    iota(R("ramp"), [[-256, L]], 256 * L, 0)
+    asel(R("trid"), R("blk"), [[-1, 128]], ALU.is_gt, 0.0, 0, 1)
+    iota(R("rpI"), [[1, 14], [0, 16]], 0, 0)
+    iota(R("vh"), [[0, 14], [1, 16]], 0, 0)
+    iota(R("num"), [[1, V + L]], 0, 0)
+    ts(R("qI"), R("pI"), 15, None, ALU.bitwise_and)
+    cp(R("qc"), R("qI"))
+    for t in range(2):
+        ts(R("pc%d" % t), R("qc"), 811.0, t - 0.375, ALU.mult, ALU.add)
+        ts(R("tp%d" % t), R("qc"), -2048.0, 2048.0 * (16 + t), ALU.mult, ALU.add)
+    ts(R("pk"), R("qc"), -1.0, 16.0, ALU.mult, ALU.add)
+    fill(R("rneg"), 0.0)
+    fill(R("rneg", 0, L, 16), -float(1 << 24))
+    fill(R("zer"), 0.0)
+    fill(R("rmul"), 1.0)
+    fill(R("rmul", 0, L, 16), 0.0)
+    ts(R("blkz"), R("blk"), 2048.0, None, ALU.mult)
+    cp(R("blkf"), R("blk"))
+    ts(R("chh", p=16), R("cn", p=16), float(1 << 21), -float(1 << 21), ALU.mult, ALU.add)
+    ts(R("cn", p=16), R("cn", p=16), float((1 << 20) - 2048 * 120), -float(1 << 20), ALU.mult, ALU.add)
+    ts(R("selk", 0, 143), R("sel1", 0, 143), 4096.0, None, ALU.mult)
+    ts(R("selm", 0, 143), R("sel1", 0, 143), -2048.0, None, ALU.mult)
+    ts(R("nidn"), R("idn"), -1.0, None, ALU.mult)
+    ts(R("iW"), R("rowc", 0, 14), R("qc"), None, ALU.add)
+    for h, (l0, l1) in enumerate(CH):
+        a, b = l0 // 16, l1 // 16
+        nl = l1 - l0
+        ts(R("nk", a, b), R("iW", a, b), -1.0, float(4096 + 2047 + nl + l0), ALU.mult, ALU.add)
+        fill(R("cb", a, b), float(BASE[h] + 2047 + nl))
+    ts(R("dW"), R("iW"), float(V), None, ALU.add)
+    ts(R("vW0"), R("iW"), 9.0, None, ALU.mult)
+
+    def late_constants():
+        ts(R("trid"), R("trid"), -1.0, None, ALU.mult)
+        ts(R("tri"), R("vh"), R("qc"), None, ALU.is_lt)
+        cp(R("rp"), R("rpI", 0, L, 16))
+        cp(R("thr0"), R("thrI"))
+
+    def sel(name, q):
+        return R(name, 15 - q, 143 - q)
+
+    def low(P, nl, last=False):
+        mm(P, R("ones", 0, 128, p=1), R("rowA", 0, nl, p=1), True, False)
+        mm(P, R("l16", p=16), R("rowB", 0, nl, p=16), False, False)
+
+    def revoke(t, rv, out, banks):
+        for m in range(4):
+            a, b = 512 * m, 512 * m + 512
+            P = R(banks[m])
+            mm(P, R("idn"), R("ringS", a, b), True, False)
+            if t == 1:
+                mm(P, R("nidn"), R("e1", a, b), False, False)
+        for m in range(4):
+            a, b = 512 * m, 512 * m + 512
+            ts(R("e0", a, b), R("ringS", a, b), rv, rv, ALU.is_equal, ALU.mult)
+            mm(R(banks[m]), R("nidn"), R("e0", a, b), False, True)
+        for m in range(4):
+            a, b = 512 * m, 512 * m + 512
+            if t == 0 or m % 2 == 0:
+                ac(R(out, a, b), R(banks[m]))
+            else:
+                cp(R(out, a, b), R(banks[m]))
+            if t == 1:
+                dma("Y" if m % 2 else "S", T.yk[:, a:b], T[out][:, a:b], rd=[R(out, a, b)])
+
+    def step1(t):
+        zb = R("zb%d" % t)
+        mm(R("PZ", 0, L), R("blkz"), zb, True, True)
+        mm(R("PM", 0, L), R("idn"), zb, True, True)
+        ts(R("JI"), R("PZ", 0, L), R("tp%d" % t), None, ALU.add)
+        ts(R("JM"), R("JI"), 15 * 2048, None, ALU.bitwise_and)
+        tt(R("YY"), R("JM"), R("nbrS", 0, 2008, 9) if t == 0 else R("BvT"), ALU.max)
+        mm(R("PZ", 0, L), R("l16", p=16), R("cn", p=16), True, False)
+        mm(R("PZ", 0, L), R("blkf"), R("YY"), False, True)
+        scan(R("SW"), R("rneg"), R("PZ", 0, L), ALU.add, ALU.max)
+        cp(R("noff"), R("SW", 15, L, 16))
+
+    for t in range(2):
+        zb, V2, vW, BIG = "zb%d" % t, "V2%d" % t, "vW%d" % t, "BIG%d" % t
+        if t == 0:
+            remote(T.BIG0[:, NXT:NXT + V], R("ringS", 0, V), "xr0", "xl0", prev)
+            ac(R("KvT"), R("ringS", 0, 2008, 9))
+            step1(0)
+        ts(R("hv"), R("KvT"), 0.0, None, ALU.is_equal)
+        mm(R("PK", 0, L), R("idn"), R("KvT"), True, False)
+        mm(R("PK", 0, L), R("nidn"), R("hv"), False, True)
+        for h, (l0, l1) in enumerate(CH):
+            a, b, nl = l0 // 16, l1 // 16, l1 - l0
+            no = R("noff", a, b)
+            cp(R("Bn", l0, l1), X("nbrS", 0, V, no), off=[no])
+            ac(R(BIG, BASE[h], BASE[h] + nl), X("ringS", 0, V, no), off=[no])
+
+        def gk(h, a, b):
+            l0, l1 = CH[h]
+            lo = BASE[h] + (l1 - l0) + 16 * (a - l0)
+            o = R("Bn", a, b)
+            ac(R(BIG, lo, lo + 16 * (b - a)), X("ringS", 0, V, o), off=[o])
+
+        gk(0, 0, 64)
+        gk(0, 64, 128)
+        gk(1, 128, 224)
+        for h, (l0, l1) in enumerate(CH):
+            nl = l1 - l0
+            ts(R("hn", l0, l1), R(BIG, BASE[h], BASE[h] + nl), 0.0, None, ALU.is_equal)
+            P = R("PK", L + l0, L + l1)
+            mm(P, R("idn"), R(BIG, BASE[h], BASE[h] + nl), True, False)
+            mm(P, R("nidn"), R("hn", l0, l1), False, True)
+        for h, (l0, l1) in enumerate(CH):
+            tt(R("E3", l0, l1), R("PK", l0, l1), R(BIG, BASE[h], BASE[h] + l1 - l0), ALU.is_equal)
+        if t == 0:
+            late_constants()
+
+        def compare(h, which, parts):
+            l0, l1 = CH[h]
+            nl, nc = l1 - l0, (l1 - l0) // 16
+            En, ko = ("E1", 0) if which == 0 else ("E2", L)
+            for a, b in parts:
+                lo = BASE[h] + nl + 16 * (a - l0)
+                for k in range(16):
+                    tt(E3d(En, a, b, k=k), R("PK", ko + a, ko + b), R(BIG, lo + k, lo + 16 * (b - a), 16), ALU.is_equal)
+            if which == 0:
+                P = R("PC%d" % h, 2 * nl, 2 * nl + nc)
+                for q in range(16):
+                    mm(P, sel("sel1", q), R("E3", l0 + q, l1, 16), q == 0, q == 15)
+            P = R("PC%d" % h, which * nl, (which + 1) * nl)
+            low(P, nl)
+            for q in range(16):
+                mm(P, sel("selk", q), E3d(En, l0, l1, q=q), False, q == 15)
+
+        def tail(h):
+            l0, l1 = CH[h]
+            a, b, nl, nc = l0 // 16, l1 // 16, l1 - l0, (l1 - l0) // 16
+            PC = "PC%d" % h
+            cp(R("M2", 0, nl), R(PC, nl, 2 * nl))
+            ts(R("xn", a, b), R(PC, 2 * nl, 2 * nl + nc), 2.0, float(1 << 18), ALU.is_ge, ALU.mult)
+            tt(R("MM", 0, nl), R(PC, 0, nl), R("M2", 0, nl), ALU.min)
+            tt(R("xn", a, b), R("xn", a, b), R("nk", a, b), ALU.add)
+            scan(R("SK", l0, l1), R("rneg", 0, nl), R("MM", 0, nl), ALU.add, ALU.max)
+            tt(R("KI", a, b), R("SK", l0 + 15, l1, 16), R("xn", a, b), ALU.max)
+            ts(R("KA", a, b), R("KI", a, b), 4095, None, ALU.bitwise_and)
+            po = R("posU", a, b)
+            ts(po, R("KA", a, b), -1.0, float(2047 + nl), ALU.mult, ALU.add)
+            w = X(BIG, BASE[h], BASE[h] + 17 * nl, po)
+            tt(R("PR", 0, nl), w, R(V2, l0, l1), ALU.mult, off=[po])
+            ac(R("KwT", l0, l1), w, off=[po])
+            ts(R("PI", 0, nl), R("PR", 0, nl), 0.25, R("pc%d" % t), ALU.mult, ALU.add)
+            ts(R("PJ", 0, nl), R("PI", 0, nl), 4095, None, ALU.bitwise_and)
+            cp(R("PL", l0, l1), R("PJ", 0, nl))
+
+        def gx(h):
+            l0, l1 = CH[h]
+            o = R("PL", l0, l1)
+            ac(R("XC%d" % h), X("matS", 0, 4096, o), off=[o])
+
+        def dsub(h, m):
+            l0, l1 = CH[h]
+            nl = l1 - l0
+            bank = ("PC0", "PK", "PC1")[(4 * h + m) % 3]
+            for p in range(4 * m, 4 * m + 4):
+                P = R(bank, (p & 3) * 128, (p & 3) * 128 + nl)
+                mm(P, R("nidn"), R(zb, l0, l1), True, False)
+                mm(P, R("idn"), R("XC%d" % h, p, 16 * nl, 16), False, True)
+            for p in range(4 * m, 4 * m + 4):
+                ac(E3d("DD", l0, l1, k=p), R(bank, (p & 3) * 128, (p & 3) * 128 + nl), AF.Abs)
+
+        def dW(h, m):
+            l0, l1 = CH[h]
+            P = R("PD%d" % h, 0, l1 - l0)
+            if m == 0:
+                low(P, l1 - l0)
+            for q in range(4 * m, 4 * m + 4):
+                mm(P, sel("selm", q), E3d("DD", l0, l1, q=q), False, q == 15)
+
+        def dA(h, m):
+            l0, l1 = CH[h]
+            for p in range(4 * m, 4 * m + 4):
+                mm(R("PA", l0, l1), sel("sel1", p), E3d("DD", l0, l1, k=p), p == 0, p == 15)
+
+        def best(h):
+            l0, l1 = CH[h]
+            a, b, nl = l0 // 16, l1 // 16, l1 - l0
+            scan(R("SD", l0, l1), R("rneg", 0, nl), R("PD%d" % h, 0, nl), ALU.add, ALU.max)
+            cp(R("DI", a, b), R("SD", l0 + 15, l1, 16))
+            ts(R("DA", a, b), R("DI", a, b), 2047, None, ALU.bitwise_and)
+            po = R("pxU", a, b)
+            ts(po, R("DA", a, b), -1.0, 2047.0, ALU.mult, ALU.add)
+            tt(R("ZS", 0, nl), X("XC%d" % h, 0, 16 * nl, po), R(zb, l0, l1), ALU.add, off=[po])
+            ts(R("ZI", 0, nl), R("ZS", 0, nl), 0.5, -0.25, ALU.mult, ALU.add)
+            cp(R("zb1" if t == 0 else "zf", l0, l1), R("ZI", 0, nl))
+
+        compare(0, 0, [(0, 64), (64, 128)])
+        compare(0, 1, [(0, 128)])
+        compare(1, 0, [(128, 224)])
+        tail(0)
+        gx(0)
+        compare(1, 1, [(128, 224)])
+        tail(1)
+        gx(1)
+        ts(R("FF"), R("KI"), 8192.0, None, ALU.is_lt)
+        emit("V", lambda: g.vector.tensor_tensor_scan(T.Finc[:, :], T.FF[:, :], T.zer[:, 0:14], 0.0, ALU.add, ALU.add), [R("FF"), R("zer", 0, 14)], [R("Finc")])
+        mm(R("PZ", 224, 238), R("blk"), R("Finc"), True, False)
+        mm(R("PZ", 224, 238), R("trid"), R("FF"), False, True)
+        if t == 0:
+            mm(R("PZ", 240, 254), R("ones", 0, 128), R("FF"), True, True)
+        tt(R("HZ"), R("PM", 0, L), R("KwT"), ALU.mult)
+        mm(R("PZ", 0, L), R("l16", p=16), R("chh", p=16), True, False)
+        mm(R("PZ", 0, L), R("blkf"), R("HZ"), False, True)
+        ts(R("nd"), R("KI"), float(1 << 18), None, ALU.is_lt)
+        tt(R("bb"), R("nd"), R("FF"), ALU.subtract)
+        if t == 0:
+            cp(R("nW"), R("SW", 15, L, 16))
+            ts(R("KK"), R("KA"), 15, None, ALU.bitwise_and)
+            cp(R("BnF"), R("Bn"))
+            ts(R("th"), R("KK"), 1.0, None, ALU.add)
+            tt(R("th"), R("th"), R("bb"), ALU.mult)
+            cp(R("cdU"), R("th"))
+            cp(R("cdR"), X("num", 0, 32, R("cdU")), off=[R("cdU")])
+            ts(R("mk"), R("cdR"), R("pk"), None, ALU.is_equal)
+            tt(R("YW"), R("mk"), R("BnF"), ALU.mult)
+            mm(R("PM", L, 2 * L), R("l16", p=16), R("chh", p=16), True, False)
+            mm(R("PM", L, 2 * L), R("blkf"), R("YW"), False, True)
+        scan(R("SH"), R("rneg"), R("PZ", 0, L), ALU.add, ALU.max)
+        ts(R("srv"), R("PZ", 224, 238), 48.0, None, ALU.is_le)
+        if t == 0:
+            red(R("fc"), R("PZ", 240, 254), ALU.add)
+        cp(R("HI"), R("SH", 15, L, 16))
+        ts(R("HJ"), R("HI"), V - 1, None, ALU.bitwise_and)
+        ts(R("ths"), R("bb"), -8192.0, float(NXT), ALU.mult, ALU.add)
+        tt(R("sp"), R("cb"), R("KA"), ALU.subtract)
+        tt(R("ths"), R("ths"), R("HJ"), ALU.add)
+        tt(R("sp"), R("sp"), R("ths"), ALU.max)
+        cp(R("spU"), R("sp"))
+        landed(BIG, NXT, NXT + V, "xr%d" % t, "xl%d" % t, nxt)
+        if t == 0:
+            ts(R("nb"), R("bb"), -1.0, 1.0, ALU.mult, ALU.add)
+            scan(R("SV"), R("rneg"), R("PM", L, 2 * L), ALU.add, ALU.max)
+            tt(R("taB"), R("nb"), R("dW"), ALU.mult)
+            tt(R("thn"), R("nb"), R("nW"), ALU.mult)
+            tt(R("oB2"), R("taB"), R("vW0"), ALU.max)
+            tt(R("vW1"), R("SV", 15, L, 16), R("thn"), ALU.add)
+            cp(R("oBU"), R("oB2"))
+            cp(R("voff"), R("vW1"))
+        ac(R("NZ"), R("KwT"), AF.Sign)
+        dsub(0, 0)
+        dsub(0, 1)
+        ac(R("SRC"), X(BIG, 0, NXT + V, R("spU")), off=[R("spU")])
+        if t == 0:
+            ac(R("wR"), X("num", 0, V, R("voff")), off=[R("voff")])
+        tt(R("N1"), R("NZ"), R("ramp"), ALU.mult)
+        dsub(0, 2)
+        dA(0, 0)
+        dsub(0, 3)
+        dA(0, 1)
+        mm(R("PZ", 256, 256 + L), R("idn"), R("N1"), True, False)
+        mm(R("PZ", 256, 256 + L), R("idn"), R("KwT"), False, True)
+        tt(R("srv"), R("srv"), R("FF"), ALU.mult)
+        tt(R("srv"), R("srv"), R("bb"), ALU.add)
+        ts(R("ta"), R("srv"), -1.0, 1.0, ALU.mult, ALU.add)
+        tt(R("ta"), R("ta"), R("dW"), ALU.mult)
+        tt(R("oKf"), R("ta"), R(vW), ALU.max)
+        if t == 0:
+            tt(R("Bm"), R("nbrS", 0, 2008, 9), R("JM"), ALU.min)
+            cp(R("oKU", 0, 14), R("oKf"))
+            tt(R("FP"), R("hv"), R("SRC"), ALU.mult)
+            tt(R("Bs"), R("wR"), R("JM"), ALU.subtract)
+            tt(R("Bx"), R("Bm"), R("Bs"), ALU.max)
+            cp(X("nbrS", 0, V + L, R("oBU")), R("Bx"), off=[R("oBU")])
+            tt(X("ringS", 0, V + L, R("oKU", 0, 14)), R("KvT"), R("FP"), ALU.add, off=[R("oKU", 0, 14)])
+            cp(R("BvT"), X("nbrS", 0, V, R("voff")), off=[R("voff")])
+            cp(R("fi"), R("fc"))
+            ts(R("fj"), R("fi"), 15, None, ALU.bitwise_and)
+            tt(R("thr1"), R("fj"), R("thr0"), ALU.add)
+        else:
+            cp(R("oBU"), R("oKf"))
+            cp(R("va"), X("num", 0, V + L, R("oBU")), off=[R("oBU")])
+            cp(R("vWp", 0, 14), R(vW))
+            cp(R("vh"), X("vWp", 0, 14, R("rp")), off=[R("rp")])
+            tt(R("eq"), R("va"), R("vh"), ALU.is_equal)
+            tt(R("eq"), R("eq"), R("tri"), ALU.mult)
+            scan(R("SE"), R("rmul"), R("eq"), ALU.mult, ALU.add)
+            ts(R("ta"), R("SE", 15, L, 16), 0.5, None, ALU.is_ge)
+            tt(R("FP"), R("hv"), R("SRC"), ALU.mult)
+            tt(R("ta"), R("ta"), R("dW"), ALU.mult)
+            tt(R("oKf"), R("oKf"), R("ta"), ALU.max)
+            cp(R("oKU", 0, 28, 2), R("oKf"))
+            for c in range(13, -1, -1):
+                o = R("oKU", 2 * c, 2 * c + 1)
+                tt(X("ringS", 0, V + L, o), R("KvT", 16 * c, 16 * c + 16), R("FP", 16 * c, 16 * c + 16), ALU.add, off=[o])
+            landed("come", 0, 1, "rr", "rl", prev)
+            cm = R("come", 0, 1)
+            for m in range(4):
+                a, b = 512 * m, 512 * m + 512
+                ts(R("e1", a, b), R("ringS", a, b), cm, cm, ALU.is_equal, ALU.mult)
+        dA(0, 2)
+        for m in range(4):
+            dsub(1, m)
+            if m == 0:
+                dA(0, 3)
+            dW(0, m)
+            if t == 0 and m == 2:
+                ac(R("V21"), R("wR"), AF.Identity, bias=1.0, scale=2.0)
+        for m in range(4):
+            dA(1, m)
+        for m in range(4):
+            dW(1, m)
+        best(0)
+        ts(R("cap"), R("PA", 0, L), R("thr%d" % t), None, ALU.is_lt)
+        tt(R("com"), R("PZ", 256, 256 + L), R("cap"), ALU.mult)
+        if t == 0:
+            best(1)
+        red(R("rvc"), R("com"), ALU.max)
+        cp(R("rvi"), R("rvc"))
+        ts(R("rvj"), R("rvi"), 255, None, ALU.bitwise_and)
+        if t == 0:
+            cp(R("rv0", 0, 1), R("rvj"))
+            step1(1)
+            remote(T.come[:, 0:1], R("rv0", 0, 1), "rr", "rl", nxt)
+            revoke(0, R("rv0", 0, 1), "ringS", ("PC0", "PC1", "PK", "PD0"))
+            remote(T.BIG1[:, NXT:NXT + V], R("ringS", 0, V), "xr1", "xl1", prev)
+            ac(R("KvT"), X("ringS", 0, V, R("voff")), off=[R("voff")])
+        else:
+            cp(R("rv1", 0, 1), R("rvj"))
+            tt(R("tmpc"), R("rv1", 0, 1), cm, ALU.not_equal)
+            tt(R("rv1", 1, 2), R("rv1", 0, 1), R("tmpc"), ALU.mult)
+            revoke(1, R("rv1", 1, 2), "ykS", ("PC0", "PC1", "PK", "PA"))
+            best(1)
+            dma("Y", T.yz[:, :], T.zf[:, :], rd=[R("zf")])
+    if not PLAN:
+        PLAN.extend(order())
+    for i in PLAN:
+        issue(*ops[i])
+    for s, c in total.items():
+        if known["Y"].get(s, 0) < c:
+            g.sync.wait_ge(T.sem[s], c)

@@ -2,53 +2,52 @@ from concourse.mybir import AluOpType as ALU, AxisListType, ActivationFunctionTy
 
 L, V = 224, 2048
 CH = [(0, 128), (128, 224)]
-BASE = [0, 17 * 128]
-NXT = 17 * 224
-SCRATCH, SMALL, PLAN = {}, {}, []
-SPLIT = ("M2", "MM", "PR", "PI", "PJ", "ZS", "ZI")
-for _n, _w, _d in (
-        ("ringS", V + L, "bfloat16"), ("nbrS", V + L, "int32"), ("matS", 4096, "bfloat16"), ("thrI", 1, "int32"),
-        ("num", V + L, "float32"), ("BIG0", NXT + V, "bfloat16"), ("BIG1", NXT + V, "bfloat16"),
-        ("zb0", L, "bfloat16"), ("zb1", L, "bfloat16"), ("zf", L, "float32"), ("XC0", 2048, "bfloat16"), ("XC1", 1536, "bfloat16"),
-        ("ones", 256, "bfloat16"), ("sel1", 144, "bfloat16"), ("selk", 144, "bfloat16"), ("selm", 144, "bfloat16"),
-        ("blk", 128, "bfloat16"), ("blkz", 128, "bfloat16"), ("blkf", 128, "float32"), ("trid", 128, "bfloat16"),
-        ("idn", 128, "bfloat16"), ("nidn", 128, "bfloat16"), ("l16", 128, "bfloat16"), ("cn", L, "bfloat16"), ("chh", L, "bfloat16"),
-        ("rowA", 128, "bfloat16"), ("rowB", 128, "bfloat16"), ("rneg", L, "float32"), ("rmul", L, "float32"), ("ramp", L, "bfloat16"),
-        ("tri", L, "bfloat16"), ("zer", 16, "float32"), ("pI", 1, "int32"), ("qI", 1, "int32"), ("qc", 1, "float32"),
-        ("pc0", 1, "float32"), ("pc1", 1, "float32"), ("tp0", 1, "float32"), ("tp1", 1, "float32"), ("pk", 1, "float32"),
-        ("thr0", 1, "float32"), ("thr1", 1, "float32"), ("tmpc", 1, "float32"), ("rowc", 16, "float32"),
-        ("iW", 14, "float32"), ("nk", 14, "float32"), ("dW", 14, "float32"), ("cb", 14, "float32"), ("vW0", 14, "float32"),
-        ("vW1", 14, "float32"), ("V20", L, "float32"), ("V21", L, "float32"),
-        ("JI", L, "int32"), ("JM", L, "int32"), ("YY", L, "float32"), ("SW", L, "float32"), ("nW", 14, "float32"),
-        ("noff", 14, "uint16"), ("Bn", L, "uint16"), ("BnF", L, "float32"), ("BvT", L, "int32"), ("KvT", L, "bfloat16"),
-        ("hv", L, "bfloat16"), ("hn", L, "bfloat16"), ("E3", L, "bfloat16"),
-        ("M2", L, "float32"), ("MM", L, "float32"), ("SK", L, "float32"), ("SD", L, "float32"),
-        ("posU", 14, "uint16"), ("KI", 14, "int32"), ("KA", 14, "int32"), ("KK", 14, "int32"), ("xn", 14, "float32"),
-        ("bb", 14, "float32"), ("nb", 14, "float32"), ("nd", 14, "float32"), ("PR", L, "float32"), ("PI", L, "int32"),
-        ("PJ", L, "int32"), ("ths", 14, "float32"), ("thn", 14, "float32"), ("taB", 14, "float32"), ("taD", 14, "float32"), ("YW", L, "float32"), ("PL", L, "uint16"), ("KwT", L, "bfloat16"), ("DI", 14, "int32"), ("DA", 14, "int32"),
-        ("pxU", 14, "uint16"), ("ZS", L, "float32"), ("ZI", L, "int32"),
-        ("NZ", L, "bfloat16"), ("N1", L, "bfloat16"), ("cap", L, "float32"), ("com", L, "float32"), ("rvc", 1, "float32"),
-        ("rvi", 1, "int32"), ("rvj", 1, "int32"), ("rv0", 4, "float32"), ("rv1", 4, "float32"), ("come", 4, "float32"), ("HZ", L, "float32"),
-        ("SH", L, "float32"), ("HI", 14, "int32"), ("HJ", 14, "int32"), ("FF", 14, "bfloat16"), ("Finc", 14, "bfloat16"),
-        ("srv", 14, "float32"), ("th", 14, "float32"), ("sp", 14, "float32"), ("spU", 14, "uint16"),
-        ("SRC", L, "bfloat16"), ("FP", L, "bfloat16"), ("ta", 14, "float32"), ("oKf", 14, "float32"), ("oKU", 28, "uint16"),
-        ("oBU", 14, "uint16"), ("oB2", 14, "float32"), ("cdU", 14, "uint16"), ("cdR", L, "float32"), ("mk", L, "float32"), ("SV", L, "float32"),
-        ("voff", 14, "uint16"), ("wR", L, "float32"), ("Bm", L, "float32"), ("Bs", L, "float32"), ("Bx", L, "int32"),
-        ("fc", 1, "float32"), ("fi", 1, "int32"), ("fj", 1, "int32"),
-        ("rpI", L, "int32"), ("rp", 14, "uint16"), ("vh", L, "float32"), ("va", L, "float32"), ("eq", L, "float32"), ("SE", L, "float32"),
-        ("e0", V, "bfloat16"), ("e1", V, "bfloat16"), ("ykS", V, "bfloat16"), ("vWp", 16, "float32")):
-    if _w in (1, 14) and _d != "uint16" and _n not in ("thrI", "FF", "Finc"):
-        _b = "small" + _d
-        SMALL[_n] = (_b, 16 * len(SMALL), _w)
-        SCRATCH[_b] = ("sbuf", [128, 16 * len(SMALL)], _d)
-    else:
-        SCRATCH[_n] = ("sbuf", [128, _w], _d)
-for _n in ("E1", "E2", "DD"):
-    SCRATCH[_n] = ("sbuf", [128, L, 16], "bfloat16")
-BANKS = ("PZ", "PK", "PC0", "PC1", "PD0", "PD1", "PA", "PM")
+GIV = 240
+ZOFF = 1025.0
+BIGN = float(1 << 24)
+NENG = 8
+PASSES = 2500
+FIRST = 4.0
+WAKE, PE, HOP = 0.15, 0.00045, 4.5
+SCRATCH, SMALL, PLAN, SPAN, GRAPH = {}, {}, [], [], []
+B16, F16, F32, I32, U16 = "bfloat16", "float16", "float32", "int32", "uint16"
+for _d, _list in (
+        (B16, (("ringS", V), ("matS", 4096), ("BIG0", 17 * 128), ("BIG1", 17 * 128), ("XC0", 2048), ("XC1", 2048),
+               ("SRW0", 480), ("SRW1", 480), ("rsp0", 240), ("rsp1", 240), ("zb0", L), ("zb1", L),
+               ("ones", 128), ("sel1", 144), ("selk", 144), ("selm", 144), ("blk", 128), ("blk16", 128), ("trid", 128),
+               ("idn", 128), ("nidn", 128), ("n256", 128), ("n128", 128), ("l16", 128), ("pen", L), ("tripen", L), ("OH", 32),
+               ("LA", 128), ("r9", 72), ("r8", 64), ("b9", 72), ("b9n", 72), ("b8a", 64), ("b8b", 64), ("tpr0", 128), ("tpr1", 128),
+               ("c16", 128), ("ramp", L), ("col", 128), ("colg", 128), ("c15", L),
+               ("KvT0", L), ("KvT1", L), ("hv", L), ("ev", L), ("hn", L), ("hw", L), ("nm", L), ("mq", L), ("cap", L),
+               ("GG", L), ("GA", L), ("eG", L), ("eH", L), ("KvP", L), ("fil", L), ("ne", L), ("eq", L),
+               ("TT", V + L), ("e1", V), ("ykS", V), ("FF", 14), ("Finc", 14), ("na", 14))),
+        (F16, (("YY0", L), ("YY1", L), ("en", L), ("BnD", L), ("YW", L), ("z16", L))),
+        (F32, (("zf", L), ("blkf", 128), ("rneg", L), ("rneg8", 64), ("V20", L), ("V21", L), ("M1", 272), ("MM", 272), ("S0", 144),
+               ("D0s", 128), ("PR", L), ("SD", 256), ("ZS", L), ("HZ", L), ("BnF", L), ("dS", L), ("SV", L), ("com", L), ("oh", L),
+               ("come", 4), ("okf", 16), ("zer", 16),
+               ("pf", 1), ("gf", 1), ("qc", 1), ("q15", 1), ("pc0", 1), ("pc1", 1), ("thr0", 1), ("thr1", 1), ("rowc", 14), ("iW", 14),
+               ("nk", 14), ("dW", 14), ("cA", 14), ("cB", 14), ("i1", 14), ("vW1", 14), ("vWi", 14), ("x1", 14), ("nd", 14), ("bb", 14),
+               ("srv", 14), ("s1", 14), ("s2", 14), ("t1", 14), ("xr", 1), ("rv0", 1), ("rv1", 1), ("nrv", 1), ("m2rv", 1),
+               ("krv", 1), ("cm1", 1), ("cm2", 1), ("ncm", 1), ("ncm2", 1))),
+        (I32, (("nbrS", V), ("thrI", 1), ("RI", L), ("SW", L), ("SH", L), ("SK", 128), ("BvT", L), ("PI", L), ("PJ", L),
+               ("pI", 1), ("qI", 1), ("gI", 1), ("KA", 14), ("KS", 14), ("KK", 14), ("DI", 14), ("DA", 14), ("HJ", 14),
+               ("hi", 1), ("fi", 1), ("fj", 1))),
+        (U16, (("Bn", L), ("PL", L), ("hU0", 16), ("hU1", 16), ("req0", 16), ("req1", 16), ("oKU", 28),
+               ("noff", 14), ("posU", 14), ("kU", 14), ("pxU", 14), ("voff", 14), ("spU", 14), ("rp", 14)))):
+    for _n, _w in _list:
+        if _w in (1, 14) and _n != "thrI":
+            _k = sum(1 for _v in SMALL.values() if _v[0] == "small" + _d)
+            SMALL[_n] = ("small" + _d, 16 * _k, _w)
+            SCRATCH["small" + _d] = ("sbuf", [128, 16 * _k + 16], _d)
+        else:
+            SCRATCH[_n] = ("sbuf", [128, _w], _d)
+SCRATCH["E1"] = SCRATCH["E2"] = ("sbuf", [128, L, 17], B16)
+SCRATCH["DD"] = ("sbuf", [128, L, 16], B16)
+BANKS = ("PK0", "PK1", "PC0", "PC1", "PD0", "PD1", "PA", "PM")
 for _n in BANKS:
-    SCRATCH[_n] = ("psum", [128, 512], "float32")
-SEMAPHORES = ["sV", "sS", "sP", "sG", "xr0", "xr1", "xl0", "xl1", "rr", "rl"] + ["d%d" % i for i in range(16)]
+    SCRATCH[_n] = ("psum", [128, 512], F32)
+SEMAPHORES = (["sV", "sS", "sP", "sG"] + ["d%d" % i for i in range(20)]
+              + [a + b for a in ("q0", "q1", "a0", "a1", "rv") for b in "rl"])
 
 
 def rank_program(g, core, T, topo):
@@ -62,20 +61,24 @@ def rank_program(g, core, T, topo):
     known = {e: {} for e in queue}
     log = {}
 
+    def meet(lo, hi, tag, l2, h2, t2):
+        if not (l2 < hi and lo < h2):
+            return False
+        if tag and t2 and tag[0] == t2[0]:
+            if tag[0] == "k":
+                return t2[1] < tag[2] and tag[1] < t2[2]
+            return tag[1] == t2[1]
+        return True
+
     def need(e, refs, write):
         out = []
         for name, lo, hi, tag in refs:
             for (l2, h2, w2, e2, s2, c2, k2, t2) in log.get(name, ()):
                 if name in BANKS:
-                    if e2 == e and (write or not w2):
+                    if e2 == e and (e == "P" or not (write or w2)):
                         continue
-                else:
-                    if not (l2 < hi and lo < h2) or not (write or w2):
-                        continue
-                    if tag and t2 and tag[0] == t2[0] and tag[1] != t2[1]:
-                        continue
-                    if e2 == e and s2 == semof.get(e) and not w2:
-                        continue
+                elif not (write or w2) or not meet(lo, hi, tag, l2, h2, t2):
+                    continue
                 out.append((s2, c2, k2))
         return out
 
@@ -107,8 +110,8 @@ def rank_program(g, core, T, topo):
 
     ops = []
 
-    def emit(e, fn, reads, writes, sem=None, inc=1, cost=0.06, lat=0.1):
-        ops.append((e, fn, [r[1:] for r in reads], [r[1:] for r in writes], sem or semof[e], inc, cost, lat))
+    def emit(e, fn, reads, writes, sem=None, inc=1, cost=0.06, lat=WAKE):
+        ops.append((e, fn, [r[1:5] for r in reads], [r[1:5] for r in writes], sem or semof[e], inc, cost, lat))
 
     def issue(e, fn, rd, wr, s, inc, cost, lat):
         if e != "R":
@@ -123,82 +126,124 @@ def rank_program(g, core, T, topo):
         note(e, wr, True, s, total[s], snap)
 
     def order():
-        succ, npred, acc = [[] for _ in ops], [0] * len(ops), {}
+        succ, chain, acc = [[] for _ in ops], [], {}
         for i, (e, fn, rd, wr, s, inc, cost, lat) in enumerate(ops):
             before = {}
+            if e == "Y":
+                if chain:
+                    before[chain[-1]] = 0.0
+                chain.append(i)
             for refs, write in ((rd, False), (wr, True)):
                 for name, lo, hi, tag in refs:
                     for (l2, h2, w2, j, t2) in acc.get(name, ()):
                         same = ops[j][0] == e
                         if name in BANKS:
-                            if same and not (write and w2):
+                            if same and not (write or w2):
                                 continue
-                            d = 0.0 if same else ops[j][7]
+                            d = 0.0 if same and e == "P" else ops[j][7]
                         else:
-                            if not (l2 < hi and lo < h2) or not (write or w2) or (tag and t2 and tag[0] == t2[0] and tag[1] != t2[1]):
+                            if not (write or w2) or not meet(lo, hi, tag, l2, h2, t2):
                                 continue
-                            d = 0.0 if same and not w2 else ops[j][7]
+                            d = ops[j][7]
                         before[j] = max(before.get(j, 0.0), d)
             for refs, write in ((rd, False), (wr, True)):
                 for name, lo, hi, tag in refs:
                     a = acc.setdefault(name, [])
                     if write and name in BANKS:
-                        a[:] = [x for x in a if ops[x[3]][0] == e and not x[2]]
+                        a[:] = []
+                    elif name in BANKS:
+                        a[:] = [x for x in a if x[2] or ops[x[3]][0] == e]
                     elif write:
                         a[:] = [x for x in a if not (lo <= x[0] and x[1] <= hi and tag in (None, x[4]))]
                     a.append((lo, hi, write, i, tag))
             for j, d in before.items():
                 if j != i:
                     succ[j].append((i, d))
-                    npred[i] += 1
-        rank_ = [0.0] * len(ops)
-        for i in range(len(ops) - 1, -1, -1):
-            rank_[i] = ops[i][6] + max([d + rank_[k] for k, d in succ[i]] + [0.0])
-        ready = {e: [] for e in ("V", "S", "P", "G", "Y", "R")}
-        rt, free, out = [0.0] * len(ops), {e: 0.0 for e in ready}, []
-        for i, n in enumerate(npred):
-            if n == 0:
-                ready[ops[i][0]].append(i)
-        while len(out) < len(ops):
-            start, e = min((max(free[e], min(rt[i] for i in ready[e])), e) for e in ready if ready[e])
-            i = min(ready[e]) if e == "Y" else max((k for k in ready[e] if rt[k] <= start + 0.01), key=lambda k: (rank_[k], -k))
-            ready[e].remove(i)
-            out.append(i)
-            end = max(start, rt[i]) + ops[i][6]
-            free[e] = end
-            for k, d in succ[i]:
-                rt[k] = max(rt[k], end + d)
-                npred[k] -= 1
-                if npred[k] == 0:
-                    ready[ops[k][0]].append(k)
-        return out
+        n = len(ops)
+        pred = [[] for _ in ops]
+        for j in range(n):
+            for i, d in succ[j]:
+                pred[i].append((j, d))
+        eng, cost, tail = [o[0] for o in ops], [o[6] for o in ops], [o[7] for o in ops]
+        kind = [o[3][0][0] if o[3] else "" for o in ops]
+        GRAPH.append((succ, list(zip(eng, cost, tail, kind))))
 
-    def width(r):
-        return r[3] - r[2] if r[4] is None or r[4][0] in ("k", "q") else (r[3] - r[2] + r[4][0] - 1) // r[4][0]
+        def place(seq, links, lead):
+            end, busy = [0.0] * n, {e: [] for e in eng}
+            for i in seq:
+                t, c, line = lead[i], cost[i], busy[eng[i]]
+                for j, d in links[i]:
+                    if end[j] + d > t:
+                        t = end[j] + d
+                k = len(line)
+                while k and line[k - 1][1] > t:
+                    k -= 1
+                while k < len(line) and line[k][0] < t + c:
+                    t = max(t, line[k][1])
+                    k += 1
+                line.insert(k, (t, t + c))
+                end[i] = t + c
+            return end
+
+        def forwards(key):
+            for i in range(n):
+                for j, d in pred[i]:
+                    if key[j] > key[i]:
+                        key[i] = key[j]
+            end = place(sorted(range(n), key=lambda i: (key[i], i)), pred, [0.0] * n)
+            return max(e + x for e, x in zip(end, tail)), end
+
+        def again(end):
+            back = place(sorted(range(n), key=lambda i: (-end[i], -i)), succ, tail)
+            return forwards([-b for b in back])
+
+        seed = [1]
+
+        def draw():
+            seed[0] = (seed[0] * 1103515245 + 12345) % (1 << 31)
+            return seed[0] / (1 << 31)
+
+        best_ = cur = forwards([float(i) for i in range(n)])
+        for _ in range(PASSES):
+            size, shift, key = (0.2, 0.5, 1.5, 3.0)[int(4 * draw())], {}, []
+            for i in range(n):
+                k = (kind[i], int(cur[1][i] / 4))
+                if k not in shift:
+                    shift[k] = size * (2 * draw() - 1) if draw() < 0.3 else 0.0
+                key.append(cur[1][i] - cost[i] + shift[k])
+            a = forwards(key)
+            b = again(a[1])
+            a = a if a[0] < b[0] else b
+            if a[0] <= cur[0] + 0.05:
+                cur = a
+            if a[0] < best_[0]:
+                best_ = a
+        SPAN.append(best_[0])
+        return sorted(range(n), key=lambda i: (round(best_[1][i] - cost[i], 6), i))
 
     def wide(*refs):
-        return all(SCRATCH[r[1]][0] == "sbuf" and SCRATCH[r[1]][2] in ("bfloat16", "uint16") for r in refs)
+        return all(SCRATCH[r[1]][0] == "sbuf" and SCRATCH[r[1]][2] in (B16, F16, U16) for r in refs)
 
     def vcost(n, per):
         return 0.00083 * max(64, n * per)
 
     def R(name, lo=0, hi=None, step=1, p=None):
-        if name in SPLIT and lo == 0 and hi == 96:
-            lo, hi = 128, 224
         if name in SMALL:
             name, off, w = SMALL[name]
             lo, hi = lo + off, off + (w if hi is None else hi)
         hi = T[name].shape[1] if hi is None else hi
         ps = slice(None) if p is None else slice(0, p)
         ap = T[name][ps, lo:hi] if step == 1 else T[name][ps, lo:hi:step]
-        return (ap, name, lo, hi, None if step == 1 else (step, lo % step))
+        return (ap, name, lo, hi, None if step == 1 else (step, lo % step), (hi - lo + step - 1) // step)
 
     def X(name, lo, hi, off):
-        return (T[name][:, lo:hi].indirect(off[0]), name, lo, hi, None)
+        return (T[name][:, lo:hi].indirect(off[0]), name, lo, hi, None, 16 * off[5])
 
-    def E3d(name, l0, l1, k=None, q=None):
-        ap = T[name][:, l0:l1, k] if k is not None else T[name][:, l0 + q:l1:16, :]
-        return (ap, name, l0, l1, ("q", q) if k is None else ("k", k))
+    def col3(name, l0, l1, k):
+        return (T[name][:, l0:l1, k], name, l0, l1, ("k", k, k + 1), l1 - l0)
+
+    def lane3(name, l0, l1, q, k0, k1):
+        return (T[name][:, l0 + q:l1:16, k0:k1], name, l0, l1, ("k", k0, k1), (l1 - l0) // 16 * (k1 - k0))
 
     def cols(*xs):
         return [x for x in xs if isinstance(x, tuple)]
@@ -206,419 +251,428 @@ def rank_program(g, core, T, topo):
     def val(x):
         return x[0] if isinstance(x, tuple) else x
 
-    def ts(out, a, s1, s2, op0, op1=None):
-        rd = [a] + cols(s1, s2)
-        c = vcost(width(out), 0.5 if wide(out, a) else 1)
+    def ts(out, a, s1, s2, op0, op1=None, off=()):
+        rd = [a] + cols(s1, s2) + list(off)
+        c = 0.05 + 0.00083 * 1.56 * out[5] if off else vcost(out[5], 0.5 if wide(out, a) else 1)
         if op1 is None:
             emit("V", lambda: g.vector.tensor_scalar(out[0], a[0], val(s1), None, op0), rd, [out], cost=c)
         else:
             emit("V", lambda: g.vector.tensor_scalar(out[0], a[0], val(s1), val(s2), op0, op1), rd, [out], cost=c)
 
-    def tt(out, a, b, op, off=()):
-        n = width(b)
-        c = vcost(n, 1 if a[1] in BANKS or b[1] in BANKS else 2)
+    def tt(out, a, b, op, off=(), scatter=False):
+        c = vcost(b[5], 1 if a[1] in BANKS or b[1] in BANKS else 2)
         if off:
-            c = 0.05 + vcost(n, 1.6 if a[3] - a[2] > n else 3.8)
+            c = 0.05 + 0.00083 * b[5] * (3.8 if scatter else 1.56)
         emit("V", lambda: g.vector.tensor_tensor(out[0], a[0], b[0], op), [a, b] + list(off), [out], cost=c)
 
     def cp(out, a, off=()):
-        n = min(width(out), width(a))
-        c = 0.05 + vcost(n, 1.6 if width(out) <= width(a) else 3.8) if off else vcost(n, 0.5 if wide(out, a) else 1)
+        c = 0.05 + 0.00083 * 1.56 * out[5] if off else vcost(out[5], 0.5 if wide(out, a) else 1)
         emit("V", lambda: g.vector.tensor_copy(out[0], a[0]), [a] + list(off), [out], cost=c)
 
-    def scan(out, d0, d1, op0, op1):
-        emit("V", lambda: g.vector.tensor_tensor_scan(out[0], d0[0], d1[0], 0.0, op0, op1), [d0, d1], [out], cost=vcost(width(out), 1))
+    def scan(out, d0, d1, op0, op1, first=0.0):
+        emit("V", lambda: g.vector.tensor_tensor_scan(out[0], d0[0], d1[0], first, op0, op1), [d0, d1], [out], cost=vcost(out[5], 1))
 
     def red(out, a, op):
-        emit("V", lambda: g.vector.tensor_reduce(out[0], a[0], AxisListType.X, op), [a], [out], cost=vcost(width(a), 1))
+        emit("V", lambda: g.vector.tensor_reduce(out[0], a[0], AxisListType.X, op), [a], [out], cost=vcost(a[5], 1))
 
     def ac(out, a, func=AF.Copy, off=(), **kw):
-        n = width(out)
-        emit("S", lambda: g.scalar.activation(out[0], a[0], func, **kw), [a] + list(off), [out], cost=0.065 + vcost(n, 1.6) if off else vcost(n, 1))
+        c = 0.065 + 0.00083 * 1.56 * out[5] if off else vcost(out[5], 1)
+        emit("S", lambda: g.scalar.activation(out[0], a[0], func, **kw), [a] + list(off), [out], cost=c)
 
     def fill(out, c):
-        emit("V", lambda: g.vector.memset(out[0], c), [], [out], cost=vcost(width(out), 1))
+        emit("V", lambda: g.vector.memset(out[0], c), [], [out], cost=vcost(out[5], 0.5 if wide(out) else 1))
 
     def mm(out, lhsT, rhs, start, stop):
-        c = 0.00042 * max(64, width(out)) * (1 if wide(rhs) else 4)
+        c = PE * max(64, out[5]) * (1 if wide(rhs) else 4)
         emit("P", lambda: g.tensor.matmul(out[0], lhsT[0], rhs[0], start, stop), [lhsT, rhs], [out], cost=c)
 
-    def iota(out, pattern, base, cm):
-        c = 0.13 + vcost(width(out), 2)
-        emit("G", lambda: g.iota(out[0], pattern, base, cm, allow_small_or_imprecise_dtypes=True), [], [out], cost=c)
+    def group(out, *terms):
+        for i, (lhsT, rhs) in enumerate(terms):
+            mm(out, lhsT, rhs, i == 0, i == len(terms) - 1)
 
-    def asel(out, a, pattern, op, fillv, base, cm):
-        c = 0.17 + vcost(width(out), 2)
-        emit("G", lambda: g.affine_select(out[0], a[0], pattern, op, fillv, base, cm), [a], [out], cost=c)
+    def iota(out, pattern, base, cm):
+        emit("G", lambda: g.iota(out[0], pattern, base, cm, allow_small_or_imprecise_dtypes=True), [], [out], cost=0.13 + 0.00166 * out[5])
 
     ndma = [0]
 
-    def dma(e, out, a, rd=(), wr=()):
+    def dma(e, out, a, rd=(), wr=(), lat=2.0, cost=0.06, **kw):
         s = "d%d" % ndma[0]
         ndma[0] += 1
-        n = sum(width(r) for r in wr)
-        emit(e, lambda: queue[e].dma_start(out, a), list(rd), list(wr), s, 16, lat=2.0 + n * 0.002)
+        emit(e, lambda: queue[e].dma_start(out, a, **kw), list(rd), list(wr), s, 16, cost=cost, lat=lat)
 
-    def remote(out_ap, src, rsem, lsem, dst):
+    def send(out, src, sem, dst, frm):
         rid, pid, _ = topo.addr(dst)
+        mask = sum(1 << e for e in topo.engines(core, dst)[:NENG])
 
         def call():
-            g.remote_dma(out_ap, src[0], T.sem[rsem], T.sem[lsem], pid, rid, topo.mask(core, dst))
-        emit("G", call, [src], [(None, lsem, 0, 1, None)], lsem, len(topo.engines(core, dst)), 1.0, 9.0)
-
-    def landed(name, lo, hi, rsem, lsem, src):
-        emit("R", None, [(None, lsem, 0, 1, None)], [(None, name, lo, hi, None)], rsem, len(topo.engines(src, core)), 0.0, 0.0)
+            g.remote_dma(out[0], src[0], T.sem[sem + "r"], T.sem[sem + "l"], pid, rid, mask)
+        flag = (None, sem + "l", 0, 1, None)
+        emit("G", call, [src], [flag], sem + "l", NENG, 1.2 + FIRST * (sem == "q0"), HOP)
+        emit("R", None, [flag], [out], sem + "r", len(topo.engines(frm, core)[:NENG]), 0.0, 0.1)
 
     prev, nxt = T.cores[(rank - 1) % N], T.cores[(rank + 1) % N]
-    dma("Y", T.zb0[:, :], T.z0[:, :], wr=[R("zb0")])
-    dma("Y", T.nbrS[:, 0:V], T.nbr[:, :], wr=[R("nbrS", 0, V)])
-    dma("Y", T.ringS[:, 0:V], T.ring[:, :], wr=[R("ringS", 0, V)])
-    dma("Y", T.matS[:, :], T.mat[:, :], wr=[R("matS")])
-    dma("Y", T.thrI[:, :], T.thr[:, :], wr=[R("thrI")])
-    fill(R("ones"), 1.0)
-    fill(R("sel1"), 0.0)
-    fill(R("sel1", 15, 143, 16), 1.0)
+    dma("Y", T.zb0[:, :], T.z0[:, :], wr=[R("zb0")], lat=1.5)
+    dma("Y", T.thrI[:, :], T.thr[:, :], wr=[R("thrI")], lat=1.5)
+    dma("Y", T.nbrS[:, :], T.nbr[:, :], wr=[R("nbrS")], lat=4.5)
+    dma("Y", T.ringS[:, :], T.ring[:, :], wr=[R("ringS")], lat=6.0)
+    dma("Y", T.matS[:, :], T.mat[:, :], wr=[R("matS")], lat=9.0)
     iota(R("pI"), [[1, 1]], 0, 1)
-    o8 = R("ones", 0, 128)
-    asel(R("blk"), o8, [[-16, 8], [0, 16]], ALU.is_ge, 0.0, 0, 1)
-    asel(R("blk"), R("blk"), [[16, 8], [0, 16]], ALU.is_ge, 0.0, 15, -1)
-    asel(R("idn"), o8, [[-1, 128]], ALU.is_equal, 0.0, 0, 1)
-    asel(R("l16", p=16), R("ones", 0, 128, p=16), [[0, 8], [-1, 16]], ALU.is_equal, 0.0, 0, 1)
-    asel(R("cn", p=16), R("ones", 0, L, p=16), [[0, 14], [-1, 16]], ALU.is_equal, 0.0, 0, 1)
-    s8 = R("sel1", 15, 143, 16)
-    asel(s8, s8, [[-16, 8]], ALU.is_ge, 0.0, 0, 1)
-    asel(s8, s8, [[16, 8]], ALU.is_ge, 0.0, 15, -1)
-    iota(R("rowA"), [[-256, 8], [0, 16]], 1792, 0)
-    iota(R("rowB"), [[0, 8], [-1, 16]], 255, -16)
-    iota(R("rowc", 0, 14), [[16, 14]], 0, 0)
+    iota(R("colg"), [[1, 8], [0, 16]], 0, 0)
+    iota(R("tpr0", p=1), [[0, 8], [-1, 16]], 0, 0)
+    iota(R("c15"), [[0, 14], [1, 16]], 0, 0)
+    iota(R("col"), [[1, 128]], 0, 0)
+    iota(R("rowc"), [[16, 14]], 0, 0)
+    iota(R("LA", p=2), [[0, 128]], 256, -(1 << 19) - 256)
+    iota(R("r9", p=2), [[-1, 8], [0, 9]], 7, 0)
+    iota(R("r8", p=2), [[-1, 8], [0, 8]], 7, 0)
+    iota(R("b9", p=16), [[0, 8], [-1, 9]], 256, -16)
+    iota(R("b8a", p=16), [[0, 8], [-1, 8]], 255, -16)
     iota(R("V20"), [[18, L]], 1, 0)
-    iota(R("ramp"), [[-256, L]], 256 * L, 0)
-    asel(R("trid"), R("blk"), [[-1, 128]], ALU.is_gt, 0.0, 0, 1)
-    iota(R("rpI"), [[1, 14], [0, 16]], 0, 0)
-    iota(R("vh"), [[0, 14], [1, 16]], 0, 0)
-    iota(R("num"), [[1, V + L]], 0, 0)
+    iota(R("ramp", p=1), [[-256, L]], 256 * L, 0)
+    fill(R("ones"), 1.0)
+    fill(R("c16", p=1), 1.0 / 16)
     ts(R("qI"), R("pI"), 15, None, ALU.bitwise_and)
+    ts(R("gI"), R("pI"), 4, None, ALU.arith_shift_right)
     cp(R("qc"), R("qI"))
+    cp(R("gf"), R("gI"))
+    cp(R("pf"), R("pI"))
+    ts(R("blk"), R("colg"), R("gf"), None, ALU.is_equal)
+    ts(R("blk16"), R("blk"), 1.0 / 16, None, ALU.mult)
+    ts(R("tpr1", p=1), R("tpr0", p=1), 1.0, None, ALU.add)
+    ts(R("l16"), R("c15", 0, 128), R("qc"), None, ALU.is_equal)
+    ts(R("pen"), R("c15"), R("qc"), -BIGN, ALU.not_equal, ALU.mult)
+    ts(R("tripen"), R("c15"), R("qc"), -4096.0, ALU.is_le, ALU.mult)
+    ts(R("idn"), R("col"), R("pf"), None, ALU.is_equal)
+    for name, c in (("nidn", -1.0), ("n256", -256.0), ("n128", -128.0)):
+        ts(R(name), R("idn"), c, None, ALU.mult)
+    ts(R("trid"), R("col"), R("pf"), -1.0, ALU.is_lt, ALU.mult)
+    tt(R("trid"), R("trid"), R("blk"), ALU.mult)
+    cp(R("blkf"), R("blk"))
+    fill(R("sel1"), 0.0)
+    cp(R("sel1", 15, 143, 16), R("blk", 0, 128, 16))
+    ts(R("selk"), R("sel1"), 4096.0, None, ALU.mult)
+    ts(R("selm"), R("sel1"), -2048.0, None, ALU.mult)
+    ts(R("q15"), R("qc"), -1.0, 15.0, ALU.mult, ALU.add)
+    fill(R("OH", 16, 32), 0.0)
+    ts(R("OH", 0, 16), R("c15", 0, 16), R("q15"), None, ALU.is_equal)
+    fill(R("r9", 0, 72, 9, p=2), 0.0)
+    cp(R("b9n", p=16), R("b9", p=16))
+    fill(R("b9", 0, 72, 9, p=16), 0.0)
+    fill(R("b9n", 0, 72, 9, p=16), float(1 << 23))
+    ts(R("b8b", p=16), R("b8a", p=16), -8.0, None, ALU.add)
     for t in range(2):
         ts(R("pc%d" % t), R("qc"), 811.0, t - 0.375, ALU.mult, ALU.add)
-        ts(R("tp%d" % t), R("qc"), -2048.0, 2048.0 * (16 + t), ALU.mult, ALU.add)
-    ts(R("pk"), R("qc"), -1.0, 16.0, ALU.mult, ALU.add)
+        fill(R("SRW%d" % t, L, GIV), 0.0)
     fill(R("rneg"), 0.0)
-    fill(R("rneg", 0, L, 16), -float(1 << 24))
+    fill(R("rneg", 0, L, 16), -BIGN)
+    fill(R("rneg8"), 0.0)
+    fill(R("rneg8", 0, 64, 8), -BIGN)
+    fill(R("D0s"), -BIGN / 2)
     fill(R("zer"), 0.0)
-    fill(R("rmul"), 1.0)
-    fill(R("rmul", 0, L, 16), 0.0)
-    ts(R("blkz"), R("blk"), 2048.0, None, ALU.mult)
-    cp(R("blkf"), R("blk"))
-    ts(R("chh", p=16), R("cn", p=16), float(1 << 21), -float(1 << 21), ALU.mult, ALU.add)
-    ts(R("cn", p=16), R("cn", p=16), float((1 << 20) - 2048 * 120), -float(1 << 20), ALU.mult, ALU.add)
-    ts(R("selk", 0, 143), R("sel1", 0, 143), 4096.0, None, ALU.mult)
-    ts(R("selm", 0, 143), R("sel1", 0, 143), -2048.0, None, ALU.mult)
-    ts(R("nidn"), R("idn"), -1.0, None, ALU.mult)
-    ts(R("iW"), R("rowc", 0, 14), R("qc"), None, ALU.add)
+    fill(R("okf"), 0.0)
+    fill(col3("E2", 0, L, 0), 0.0)
+    ts(R("iW"), R("rowc"), R("qc"), None, ALU.add)
     for h, (l0, l1) in enumerate(CH):
         a, b = l0 // 16, l1 // 16
-        nl = l1 - l0
-        ts(R("nk", a, b), R("iW", a, b), -1.0, float(4096 + 2047 + nl + l0), ALU.mult, ALU.add)
-        fill(R("cb", a, b), float(BASE[h] + 2047 + nl))
+        ts(R("x1", a, b), R("rowc", a, b), float(1 << 15), -float((1 << 19) * (7 + a)), ALU.mult, ALU.add)
+        ts(R("nk", a, b), R("iW", a, b), -1.0, float(4096 + 2047 + l1), ALU.mult, ALU.add)
+    tt(R("nk"), R("nk"), R("x1"), ALU.add)
     ts(R("dW"), R("iW"), float(V), None, ALU.add)
-    ts(R("vW0"), R("iW"), 9.0, None, ALU.mult)
+    ts(R("cA"), R("iW"), -float(L), None, ALU.add)
+    ts(R("cB"), R("iW"), float(GIV - L), None, ALU.add)
+    ts(R("i1"), R("iW"), 1.0, None, ALU.add)
+    ts(R("rp"), R("rowc"), 1.0 / 16, None, ALU.mult)
+    cp(R("thr0"), R("thrI"))
 
-    def late_constants():
-        ts(R("trid"), R("trid"), -1.0, None, ALU.mult)
-        ts(R("tri"), R("vh"), R("qc"), None, ALU.is_lt)
-        cp(R("rp"), R("rpI", 0, L, 16))
-        cp(R("thr0"), R("thrI"))
+    idn, nidn, blk, l16 = R("idn"), R("nidn"), R("blk"), R("l16", p=16)
+    v0 = (0, 9 * (L - 1) + 1, 9)
 
     def sel(name, q):
         return R(name, 15 - q, 143 - q)
 
-    def low(P, nl, last=False):
-        mm(P, R("ones", 0, 128, p=1), R("rowA", 0, nl, p=1), True, False)
-        mm(P, R("l16", p=16), R("rowB", 0, nl, p=16), False, False)
+    def first(name, l0, l1):
+        return R(name, 9 * l0, 9 * (l1 - 1) + 1, 9)
 
-    def revoke(t, rv, out, banks):
-        for m in range(4):
-            a, b = 512 * m, 512 * m + 512
-            P = R(banks[m])
-            mm(P, R("idn"), R("ringS", a, b), True, False)
-            if t == 1:
-                mm(P, R("nidn"), R("e1", a, b), False, False)
-        for m in range(4):
-            a, b = 512 * m, 512 * m + 512
-            ts(R("e0", a, b), R("ringS", a, b), rv, rv, ALU.is_equal, ALU.mult)
-            mm(R(banks[m]), R("nidn"), R("e0", a, b), False, True)
-        for m in range(4):
-            a, b = 512 * m, 512 * m + 512
-            if t == 0 or m % 2 == 0:
-                ac(R(out, a, b), R(banks[m]))
-            else:
-                cp(R(out, a, b), R(banks[m]))
-            if t == 1:
-                dma("Y" if m % 2 else "S", T.yk[:, a:b], T[out][:, a:b], rd=[R(out, a, b)])
+    def step1(t, h):
+        l0, l1 = CH[h]
+        a, b, nl, PK = l0 // 16, l1 // 16, l1 - l0, "PK%d" % h
+        u, EJ, YY = R(PK, 384, 384 + nl), R(PK, 256, 256 + nl), R("YY%d" % t, l0, l1)
+        group(u, (R("tpr%d" % t, p=1), R("c16", 0, nl, p=1)), (R("blk16"), R("zb0" if t == 0 else "z16", l0, l1)))
+        cp(R("RI", l0, l1), u)
+        tt(EJ, u, R("RI", l0, l1), ALU.is_equal)
+        tt(YY, EJ, first("nbrS", l0, l1) if t == 0 else R("BvT", l0, l1), ALU.mult)
+        group(u, (l16, R("pen", 0, nl, p=16)), (blk, YY))
+        scan(R("SW", l0, l1), R("rneg", 0, nl), u, ALU.add, ALU.max)
+        cp(R("noff", a, b), R("SW", l0 + 15, l1, 16))
 
-    def step1(t):
-        zb = R("zb%d" % t)
-        mm(R("PZ", 0, L), R("blkz"), zb, True, True)
-        mm(R("PM", 0, L), R("idn"), zb, True, True)
-        ts(R("JI"), R("PZ", 0, L), R("tp%d" % t), None, ALU.add)
-        ts(R("JM"), R("JI"), 15 * 2048, None, ALU.bitwise_and)
-        tt(R("YY"), R("JM"), R("nbrS", 0, 2008, 9) if t == 0 else R("BvT"), ALU.max)
-        mm(R("PZ", 0, L), R("l16", p=16), R("cn", p=16), True, False)
-        mm(R("PZ", 0, L), R("blkf"), R("YY"), False, True)
-        scan(R("SW"), R("rneg"), R("PZ", 0, L), ALU.add, ALU.max)
-        cp(R("noff"), R("SW", 15, L, 16))
-
-    for t in range(2):
-        zb, V2, vW, BIG = "zb%d" % t, "V2%d" % t, "vW%d" % t, "BIG%d" % t
+    def around(t, h):
+        l0, l1 = CH[h]
+        a, b, nl, PK, BIG = l0 // 16, l1 // 16, l1 - l0, "PK%d" % h, "BIG%d" % h
+        no, Kv, Kn = R("noff", a, b), R("KvT%d" % t, l0, l1), R(BIG, 0, nl)
+        cp(R("Bn", l0, l1), X("nbrS", 0, V, no), off=[no])
+        ac(Kn, X("ringS", 0, V, no), off=[no])
+        for x, y in parts(h):
+            o = R("Bn", x, y)
+            ac(R(BIG, nl + 16 * (x - l0), nl + 16 * (y - l0)), X("ringS", 0, V, o), off=[o])
+        ts(R("hv", l0, l1), Kv, 0.0, -1.0, ALU.is_equal, ALU.mult)
+        ts(R("hn", l0, l1), Kn, 0.0, 2048.0, ALU.is_equal, ALU.mult)
+        tv, tn = [(idn, Kv), (idn, R("hv", l0, l1))], [(idn, Kn), (idn, R("hn", l0, l1))]
+        if t == 1:
+            ts(R("ev", l0, l1), Kv, R("rv0"), R("m2rv"), ALU.is_equal, ALU.mult)
+            ts(R("en", l0, l1), Kn, R("rv0"), R("krv"), ALU.is_equal, ALU.mult)
+            tv.append((idn, R("ev", l0, l1)))
+            tn.append((idn, R("en", l0, l1)))
+        group(R(PK, 0, nl), *tv)
+        group(R(PK, 128, 128 + nl), *tn)
+        tt(R("HZ", l0, l1), R(PK, 128, 128 + nl), R("zb%d" % t, l0, l1), ALU.mult)
+        tt(col3("E1", l0, l1, 0), R(PK, 0, nl), Kn, ALU.is_equal)
         if t == 0:
-            remote(T.BIG0[:, NXT:NXT + V], R("ringS", 0, V), "xr0", "xl0", prev)
-            ac(R("KvT"), R("ringS", 0, 2008, 9))
-            step1(0)
-        ts(R("hv"), R("KvT"), 0.0, None, ALU.is_equal)
-        mm(R("PK", 0, L), R("idn"), R("KvT"), True, False)
-        mm(R("PK", 0, L), R("nidn"), R("hv"), False, True)
-        for h, (l0, l1) in enumerate(CH):
-            a, b, nl = l0 // 16, l1 // 16, l1 - l0
-            no = R("noff", a, b)
-            cp(R("Bn", l0, l1), X("nbrS", 0, V, no), off=[no])
-            ac(R(BIG, BASE[h], BASE[h] + nl), X("ringS", 0, V, no), off=[no])
+            P = R("PD%d" % h, 0, nl)
+            group(P, (blk, R("YY0", l0, l1)))
+            cp(R("BnF", l0, l1), R("Bn", l0, l1))
+            tt(R("BnD", l0, l1), R("BnF", l0, l1), P, ALU.subtract)
 
-        def gk(h, a, b):
-            l0, l1 = CH[h]
-            lo = BASE[h] + (l1 - l0) + 16 * (a - l0)
-            o = R("Bn", a, b)
-            ac(R(BIG, lo, lo + 16 * (b - a)), X("ringS", 0, V, o), off=[o])
+    def parts(h):
+        l0, l1 = CH[h]
+        return [(l0, l0 + 64), (l0 + 64, l1)] if l1 - l0 == 128 else [(l0, l1)]
 
-        gk(0, 0, 64)
-        gk(0, 64, 128)
-        gk(1, 128, 224)
-        for h, (l0, l1) in enumerate(CH):
-            nl = l1 - l0
-            ts(R("hn", l0, l1), R(BIG, BASE[h], BASE[h] + nl), 0.0, None, ALU.is_equal)
-            P = R("PK", L + l0, L + l1)
-            mm(P, R("idn"), R(BIG, BASE[h], BASE[h] + nl), True, False)
-            mm(P, R("nidn"), R("hn", l0, l1), False, True)
-        for h, (l0, l1) in enumerate(CH):
-            tt(R("E3", l0, l1), R("PK", l0, l1), R(BIG, BASE[h], BASE[h] + l1 - l0), ALU.is_equal)
-        if t == 0:
-            late_constants()
+    def request(t):
+        P = R("PD0", 256, 256 + L)
+        group(P, (l16, R("pen", p=16)), (R("blkf"), R("HZ")))
+        scan(R("SH"), R("rneg"), P, ALU.add, ALU.max)
+        ts(R("HJ"), R("SH", 15, L, 16), V - 1, None, ALU.bitwise_and)
+        cp(R("hU%d" % t, 0, 14), R("HJ"))
+        rq = R("req%d" % t, 0, 14)
+        send(rq, R("hU%d" % t, 0, 14), "q%d" % t, nxt, prev)
+        ac(R("rsp%d" % t, 0, L), X("ringS", 0, V, rq), off=[rq])
+        if t == 1:
+            cp(R("rsp1", L, L + 1), R("rv0"))
+        send(R("SRW%d" % t, GIV, GIV + L + t), R("rsp%d" % t, 0, L + t), "a%d" % t, prev, nxt)
 
-        def compare(h, which, parts):
-            l0, l1 = CH[h]
-            nl, nc = l1 - l0, (l1 - l0) // 16
-            En, ko = ("E1", 0) if which == 0 else ("E2", L)
-            for a, b in parts:
-                lo = BASE[h] + nl + 16 * (a - l0)
-                for k in range(16):
-                    tt(E3d(En, a, b, k=k), R("PK", ko + a, ko + b), R(BIG, lo + k, lo + 16 * (b - a), 16), ALU.is_equal)
-            if which == 0:
-                P = R("PC%d" % h, 2 * nl, 2 * nl + nc)
-                for q in range(16):
-                    mm(P, sel("sel1", q), R("E3", l0 + q, l1, 16), q == 0, q == 15)
-            P = R("PC%d" % h, which * nl, (which + 1) * nl)
-            low(P, nl)
-            for q in range(16):
-                mm(P, sel("selk", q), E3d(En, l0, l1, q=q), False, q == 15)
+    def compare(h, which, k0, k1, runs):
+        l0, l1 = CH[h]
+        nl, En = l1 - l0, "E%d" % (which + 1)
+        for x, y in runs:
+            lo = nl + 16 * (x - l0)
+            for k in range(k0, k1):
+                tt(col3(En, x, y, k + 1), R("PK%d" % h, 128 * which + x - l0, 128 * which + y - l0),
+                   R("BIG%d" % h, lo + k, lo + 16 * (y - x), 16), ALU.is_equal)
 
-        def tail(h):
-            l0, l1 = CH[h]
-            a, b, nl, nc = l0 // 16, l1 // 16, l1 - l0, (l1 - l0) // 16
-            PC = "PC%d" % h
-            cp(R("M2", 0, nl), R(PC, nl, 2 * nl))
-            ts(R("xn", a, b), R(PC, 2 * nl, 2 * nl + nc), 2.0, float(1 << 18), ALU.is_ge, ALU.mult)
-            tt(R("MM", 0, nl), R(PC, 0, nl), R("M2", 0, nl), ALU.min)
-            tt(R("xn", a, b), R("xn", a, b), R("nk", a, b), ALU.add)
-            scan(R("SK", l0, l1), R("rneg", 0, nl), R("MM", 0, nl), ALU.add, ALU.max)
-            tt(R("KI", a, b), R("SK", l0 + 15, l1, 16), R("xn", a, b), ALU.max)
-            ts(R("KA", a, b), R("KI", a, b), 4095, None, ALU.bitwise_and)
-            po = R("posU", a, b)
-            ts(po, R("KA", a, b), -1.0, float(2047 + nl), ALU.mult, ALU.add)
-            w = X(BIG, BASE[h], BASE[h] + 17 * nl, po)
-            tt(R("PR", 0, nl), w, R(V2, l0, l1), ALU.mult, off=[po])
-            ac(R("KwT", l0, l1), w, off=[po])
-            ts(R("PI", 0, nl), R("PR", 0, nl), 0.25, R("pc%d" % t), ALU.mult, ALU.add)
-            ts(R("PJ", 0, nl), R("PI", 0, nl), 4095, None, ALU.bitwise_and)
-            cp(R("PL", l0, l1), R("PJ", 0, nl))
+    def count(h, which, half):
+        l0, l1 = CH[h]
+        nc = (l1 - l0) // 16
+        w, lo = (9, 136 * which) if half == 0 else (8, 136 * which + 72)
+        P = R("PC%d" % h, lo, lo + w * nc)
+        low = ("b9", "b9n")[which] if half == 0 else "b8b"
+        group(P, (R("LA", p=2), R("r%d" % w, 0, w * nc, p=2)), (l16, R(low, 0, w * nc, p=16)),
+              *[(sel("selk", q), lane3("E%d" % (which + 1), l0, l1, q, 9 * half, 9 + 8 * half)) for q in range(16)])
+        return P
 
-        def gx(h):
-            l0, l1 = CH[h]
-            o = R("PL", l0, l1)
-            ac(R("XC%d" % h), X("matS", 0, 4096, o), off=[o])
+    def choose(t, h):
+        l0, l1 = CH[h]
+        a, b, nl, nc = l0 // 16, l1 // 16, l1 - l0, (l1 - l0) // 16
+        BIG, m0 = "BIG%d" % h, 136 * h
+        compare(h, 0, 0, 16, parts(h) if t == 0 else [(l0, l1)])
+        ac(R("M1", m0, m0 + 9 * nc), count(h, 0, 0))
+        ac(R("M1", m0 + 72, m0 + 72 + 8 * nc), count(h, 0, 1))
+        mn = R("M1", m0, m0 + 9 * nc, 9)
+        ts(R("x1", a, b), mn, 8192.0, float(1 << 18), ALU.is_ge, ALU.mult)
+        tt(mn, R("x1", a, b), R("nk", a, b), ALU.add)
+        compare(h, 1, 0, 8, [(l0, l1)])
+        MM = R("MM", m0, m0 + 9 * nc)
+        tt(MM, count(h, 1, 0), R("M1", m0, m0 + 9 * nc), ALU.min)
+        scan(R("S0", 72 * h, 72 * h + 9 * nc), MM, MM, ALU.max, ALU.max, -BIGN / 2)
+        cp(R("D0s", 64 * h, 64 * h + 8 * nc, 8), R("S0", 72 * h + 8, 72 * h + 9 * nc, 9))
+        compare(h, 1, 8, 16, [(l0, l1)])
+        MM = R("MM", m0 + 72, m0 + 72 + 8 * nc)
+        tt(MM, count(h, 1, 1), R("M1", m0 + 72, m0 + 72 + 8 * nc), ALU.min)
+        scan(R("SK", 64 * h, 64 * h + 8 * nc), R("D0s", 64 * h, 64 * h + 8 * nc), MM, ALU.max, ALU.max, -BIGN / 2)
+        top = R("SK", 64 * h + 7, 64 * h + 8 * nc, 8)
+        ts(R("KA", a, b), top, 4095, None, ALU.bitwise_and)
+        po = R("posU", a, b)
+        ts(po, R("KA", a, b), -1.0, float(2047 + nl), ALU.mult, ALU.add)
+        w, PR = X(BIG, 0, 17 * nl, po), R("PR", l0, l1)
+        tt(PR, w, R("V2%d" % t, l0, l1), ALU.mult, off=[po])
+        if t == 1:
+            ts(R("mq", l0, l1), w, R("rv0"), None, ALU.not_equal, off=[po])
+            tt(PR, PR, R("mq", l0, l1), ALU.mult)
+        Kw = R("SRW%d" % t, l0, l1)
+        ac(Kw, w, off=[po], scale=-1.0)
+        ts(R("PI", l0, l1), PR, 0.25, R("pc%d" % t), ALU.mult, ALU.add)
+        ts(R("PJ", l0, l1), R("PI", l0, l1), 4095, None, ALU.bitwise_and)
+        cp(R("PL", l0, l1), R("PJ", l0, l1))
+        o = R("PL", l0, l1)
+        ac(R("XC%d" % h, 0, 16 * nl), X("matS", 0, 4096, o), off=[o])
+        ts(R("KS", a, b), top, (1 << 19) - 1, None, ALU.bitwise_and)
+        ts(R("hw", l0, l1), Kw, 0.0, 8192.0, ALU.is_equal, ALU.mult)
+        if t == 1:
+            ts(R("nm", l0, l1), Kw, R("nrv"), 8192.0, ALU.is_equal, ALU.mult)
 
-        def dsub(h, m):
-            l0, l1 = CH[h]
-            nl = l1 - l0
-            bank = ("PC0", "PK", "PC1")[(4 * h + m) % 3]
-            for p in range(4 * m, 4 * m + 4):
-                P = R(bank, (p & 3) * 128, (p & 3) * 128 + nl)
-                mm(P, R("nidn"), R(zb, l0, l1), True, False)
-                mm(P, R("idn"), R("XC%d" % h, p, 16 * nl, 16), False, True)
-            for p in range(4 * m, 4 * m + 4):
-                ac(E3d("DD", l0, l1, k=p), R(bank, (p & 3) * 128, (p & 3) * 128 + nl), AF.Abs)
+    def move(h):
+        l0, l1 = CH[h]
+        a, b, nl = l0 // 16, l1 // 16, l1 - l0
+        ts(R("KK", a, b), R("KA", a, b), 2048 + 15, None, ALU.bitwise_and)
+        ko, YW, YY = R("kU", a, b), R("YW", l0, l1), R("YY0", l0, l1)
+        ts(ko, R("KK", a, b), 16.0, None, ALU.min)
+        tt(YW, X("OH", 0, 32, ko), R("BnD", l0, l1), ALU.mult, off=[ko])
+        group(R("PM", 0, nl), (blk, YW))
+        group(R("PM", 128, 128 + nl), (blk, YW), (blk, YY))
+        group(R("PM", 256, 256 + nl), (l16, R("pen", 0, nl, p=16)), (blk, YY), (blk, YW))
+        scan(R("SV", l0, l1), R("rneg", 0, nl), R("PM", 256, 256 + nl), ALU.add, ALU.max)
+        ac(R("dS", l0, l1), R("PM", 0, nl))
+        ac(R("V21", l0, l1), R("PM", 128, 128 + nl), AF.Identity, bias=1.0, scale=2.0)
+        cp(R("voff", a, b), R("SV", l0 + 15, l1, 16))
+        EJ = R("PK%d" % h, 256, 256 + nl)
+        tt(EJ, EJ, R("dS", l0, l1), ALU.mult)
+        tt(first("nbrS", l0, l1), EJ, first("nbrS", l0, l1), ALU.add)
 
-        def dW(h, m):
-            l0, l1 = CH[h]
-            P = R("PD%d" % h, 0, l1 - l0)
-            if m == 0:
-                low(P, l1 - l0)
-            for q in range(4 * m, 4 * m + 4):
-                mm(P, sel("selm", q), E3d("DD", l0, l1, q=q), False, q == 15)
-
-        def dA(h, m):
-            l0, l1 = CH[h]
-            for p in range(4 * m, 4 * m + 4):
-                mm(R("PA", l0, l1), sel("sel1", p), E3d("DD", l0, l1, k=p), p == 0, p == 15)
-
-        def best(h):
-            l0, l1 = CH[h]
-            a, b, nl = l0 // 16, l1 // 16, l1 - l0
-            scan(R("SD", l0, l1), R("rneg", 0, nl), R("PD%d" % h, 0, nl), ALU.add, ALU.max)
-            cp(R("DI", a, b), R("SD", l0 + 15, l1, 16))
-            ts(R("DA", a, b), R("DI", a, b), 2047, None, ALU.bitwise_and)
-            po = R("pxU", a, b)
-            ts(po, R("DA", a, b), -1.0, 2047.0, ALU.mult, ALU.add)
-            tt(R("ZS", 0, nl), X("XC%d" % h, 0, 16 * nl, po), R(zb, l0, l1), ALU.add, off=[po])
-            ts(R("ZI", 0, nl), R("ZS", 0, nl), 0.5, -0.25, ALU.mult, ALU.add)
-            cp(R("zb1" if t == 0 else "zf", l0, l1), R("ZI", 0, nl))
-
-        compare(0, 0, [(0, 64), (64, 128)])
-        compare(0, 1, [(0, 128)])
-        compare(1, 0, [(128, 224)])
-        tail(0)
-        gx(0)
-        compare(1, 1, [(128, 224)])
-        tail(1)
-        gx(1)
-        ts(R("FF"), R("KI"), 8192.0, None, ALU.is_lt)
-        emit("V", lambda: g.vector.tensor_tensor_scan(T.Finc[:, :], T.FF[:, :], T.zer[:, 0:14], 0.0, ALU.add, ALU.add), [R("FF"), R("zer", 0, 14)], [R("Finc")])
-        mm(R("PZ", 224, 238), R("blk"), R("Finc"), True, False)
-        mm(R("PZ", 224, 238), R("trid"), R("FF"), False, True)
-        if t == 0:
-            mm(R("PZ", 240, 254), R("ones", 0, 128), R("FF"), True, True)
-        tt(R("HZ"), R("PM", 0, L), R("KwT"), ALU.mult)
-        mm(R("PZ", 0, L), R("l16", p=16), R("chh", p=16), True, False)
-        mm(R("PZ", 0, L), R("blkf"), R("HZ"), False, True)
-        ts(R("nd"), R("KI"), float(1 << 18), None, ALU.is_lt)
+    def sources(t):
+        ts(R("FF"), R("KS"), 8192.0, None, ALU.is_lt)
+        ts(R("nd"), R("KS"), float(1 << 18), None, ALU.is_lt)
+        scan(R("Finc"), R("FF"), R("zer", 0, 14), ALU.add, ALU.add)
         tt(R("bb"), R("nd"), R("FF"), ALU.subtract)
+        group(R("PM", 480, 494), (blk, R("Finc")), (R("trid"), R("FF")))
         if t == 0:
-            cp(R("nW"), R("SW", 15, L, 16))
-            ts(R("KK"), R("KA"), 15, None, ALU.bitwise_and)
-            cp(R("BnF"), R("Bn"))
-            ts(R("th"), R("KK"), 1.0, None, ALU.add)
-            tt(R("th"), R("th"), R("bb"), ALU.mult)
-            cp(R("cdU"), R("th"))
-            cp(R("cdR"), X("num", 0, 32, R("cdU")), off=[R("cdU")])
-            ts(R("mk"), R("cdR"), R("pk"), None, ALU.is_equal)
-            tt(R("YW"), R("mk"), R("BnF"), ALU.mult)
-            mm(R("PM", L, 2 * L), R("l16", p=16), R("chh", p=16), True, False)
-            mm(R("PM", L, 2 * L), R("blkf"), R("YW"), False, True)
-        scan(R("SH"), R("rneg"), R("PZ", 0, L), ALU.add, ALU.max)
-        ts(R("srv"), R("PZ", 224, 238), 48.0, None, ALU.is_le)
+            group(R("PM", 496, 497), (R("ones"), R("Finc", 13, 14)))
+        ts(R("srv"), R("PM", 480, 494), 48.0, None, ALU.is_le)
         if t == 0:
-            red(R("fc"), R("PZ", 240, 254), ALU.add)
-        cp(R("HI"), R("SH", 15, L, 16))
-        ts(R("HJ"), R("HI"), V - 1, None, ALU.bitwise_and)
-        ts(R("ths"), R("bb"), -8192.0, float(NXT), ALU.mult, ALU.add)
-        tt(R("sp"), R("cb"), R("KA"), ALU.subtract)
-        tt(R("ths"), R("ths"), R("HJ"), ALU.add)
-        tt(R("sp"), R("sp"), R("ths"), ALU.max)
-        cp(R("spU"), R("sp"))
-        landed(BIG, NXT, NXT + V, "xr%d" % t, "xl%d" % t, nxt)
-        if t == 0:
-            ts(R("nb"), R("bb"), -1.0, 1.0, ALU.mult, ALU.add)
-            scan(R("SV"), R("rneg"), R("PM", L, 2 * L), ALU.add, ALU.max)
-            tt(R("taB"), R("nb"), R("dW"), ALU.mult)
-            tt(R("thn"), R("nb"), R("nW"), ALU.mult)
-            tt(R("oB2"), R("taB"), R("vW0"), ALU.max)
-            tt(R("vW1"), R("SV", 15, L, 16), R("thn"), ALU.add)
-            cp(R("oBU"), R("oB2"))
-            cp(R("voff"), R("vW1"))
-        ac(R("NZ"), R("KwT"), AF.Sign)
-        dsub(0, 0)
-        dsub(0, 1)
-        ac(R("SRC"), X(BIG, 0, NXT + V, R("spU")), off=[R("spU")])
-        if t == 0:
-            ac(R("wR"), X("num", 0, V, R("voff")), off=[R("voff")])
-        tt(R("N1"), R("NZ"), R("ramp"), ALU.mult)
-        dsub(0, 2)
-        dA(0, 0)
-        dsub(0, 3)
-        dA(0, 1)
-        mm(R("PZ", 256, 256 + L), R("idn"), R("N1"), True, False)
-        mm(R("PZ", 256, 256 + L), R("idn"), R("KwT"), False, True)
-        tt(R("srv"), R("srv"), R("FF"), ALU.mult)
-        tt(R("srv"), R("srv"), R("bb"), ALU.add)
-        ts(R("ta"), R("srv"), -1.0, 1.0, ALU.mult, ALU.add)
-        tt(R("ta"), R("ta"), R("dW"), ALU.mult)
-        tt(R("oKf"), R("ta"), R(vW), ALU.max)
-        if t == 0:
-            tt(R("Bm"), R("nbrS", 0, 2008, 9), R("JM"), ALU.min)
-            cp(R("oKU", 0, 14), R("oKf"))
-            tt(R("FP"), R("hv"), R("SRC"), ALU.mult)
-            tt(R("Bs"), R("wR"), R("JM"), ALU.subtract)
-            tt(R("Bx"), R("Bm"), R("Bs"), ALU.max)
-            cp(X("nbrS", 0, V + L, R("oBU")), R("Bx"), off=[R("oBU")])
-            tt(X("ringS", 0, V + L, R("oKU", 0, 14)), R("KvT"), R("FP"), ALU.add, off=[R("oKU", 0, 14)])
-            cp(R("BvT"), X("nbrS", 0, V, R("voff")), off=[R("voff")])
-            cp(R("fi"), R("fc"))
+            cp(R("fi"), R("PM", 496, 497))
             ts(R("fj"), R("fi"), 15, None, ALU.bitwise_and)
             tt(R("thr1"), R("fj"), R("thr0"), ALU.add)
-        else:
-            cp(R("oBU"), R("oKf"))
-            cp(R("va"), X("num", 0, V + L, R("oBU")), off=[R("oBU")])
-            cp(R("vWp", 0, 14), R(vW))
-            cp(R("vh"), X("vWp", 0, 14, R("rp")), off=[R("rp")])
-            tt(R("eq"), R("va"), R("vh"), ALU.is_equal)
-            tt(R("eq"), R("eq"), R("tri"), ALU.mult)
-            scan(R("SE"), R("rmul"), R("eq"), ALU.mult, ALU.add)
-            ts(R("ta"), R("SE", 15, L, 16), 0.5, None, ALU.is_ge)
-            tt(R("FP"), R("hv"), R("SRC"), ALU.mult)
-            tt(R("ta"), R("ta"), R("dW"), ALU.mult)
-            tt(R("oKf"), R("oKf"), R("ta"), ALU.max)
-            cp(R("oKU", 0, 28, 2), R("oKf"))
-            for c in range(13, -1, -1):
-                o = R("oKU", 2 * c, 2 * c + 1)
-                tt(X("ringS", 0, V + L, o), R("KvT", 16 * c, 16 * c + 16), R("FP", 16 * c, 16 * c + 16), ALU.add, off=[o])
-            landed("come", 0, 1, "rr", "rl", prev)
+        tt(R("s1"), R("bb"), R("cA"), ALU.mult)
+        tt(R("srv"), R("srv"), R("FF"), ALU.mult)
+        tt(R("s2"), R("srv"), R("cB"), ALU.mult)
+        tt(R("s1"), R("s1"), R("s2"), ALU.add)
+        sp = R("spU")
+        ts(sp, R("s1"), float(L), None, ALU.add)
+        src, P = X("SRW%d" % t, 0, GIV + L, sp), R("PM", 0, L)
+        if t == 0:
+            ac(R("GA"), src, AF.Abs, off=[sp])
+            group(P, (R("n256"), R("KvT0")), (idn, R("GA")))
+            tt(R("ringS", *v0), P, R("KvT0"), ALU.max)
+            return
+        ac(R("GG"), src, off=[sp])
+        ac(R("GA"), R("GG"), AF.Abs)
+        rvn = R("SRW1", GIV + L, GIV + L + 1)
+        ts(R("eG"), R("GG"), rvn, rvn, ALU.is_equal, ALU.mult)
+        ts(R("eH"), R("GG"), R("nrv"), R("nrv"), ALU.is_equal, ALU.mult)
+        group(R("PM", 256, 256 + L), (idn, R("KvT1")), (idn, R("ev")))
+        ac(R("KvP"), R("PM", 256, 256 + L))
+        group(P, (R("n256"), R("KvT1")), (R("n128"), R("ev")), (idn, R("GA")), (nidn, R("eG")), (idn, R("eH")))
+        tt(R("fil"), P, R("KvP"), ALU.max)
+        ts(R("ne"), R("fil"), R("come", 0, 1), R("ncm"), ALU.is_equal, ALU.mult)
+        tt(R("s2"), R("srv"), R("bb"), ALU.add)
+        ts(R("na"), R("s2"), -1.0, 1.0, ALU.mult, ALU.add)
+        tt(R("s2"), R("s2"), R("vWi"), ALU.mult)
+        tt(R("okf", 0, 14), R("s2"), R("i1"), ALU.subtract)
+        ac(R("oh"), X("okf", 0, 16, R("rp")), off=[R("rp")])
+        group(P, (l16, R("tripen", p=16)), (blk, R("YW")), (blk, R("YY0")))
+        tt(R("eq"), P, R("oh"), ALU.is_equal)
+        group(R("PM", 480, 494), (idn, R("na")), *[(sel("sel1", q), R("eq", q, L, 16)) for q in range(16)])
+        ts(R("t1"), R("PM", 480, 494), 0.5, 4096.0, ALU.is_ge, ALU.mult)
+        tt(R("t1"), R("t1"), R("dW"), ALU.min)
+        tt(R("t1"), R("t1"), R("vW1"), ALU.max)
+        cp(R("oKU", 0, 28, 2), R("t1"))
+        for c in range(13, -1, -1):
+            o = R("oKU", 2 * c, 2 * c + 1)
+            tt(X("TT", 0, V + L, o), R("fil", 16 * c, 16 * c + 16), R("ne", 16 * c, 16 * c + 16), ALU.add, off=[o], scatter=True)
+
+    def distances(t, h):
+        l0, l1 = CH[h]
+        nl, nc, zb = l1 - l0, (l1 - l0) // 16, R("zb%d" % t, l0, l1)
+        group(R("PA", L + l0, L + l1), (R("ones", p=1), R("ramp", l0, l1, p=1)), (nidn, R("SRW%d" % t, l0, l1)))
+        PA = R("PA", l0, l1)
+        mm(PA, idn, R("hw", l0, l1), True, False)
+        if t == 1:
+            mm(PA, idn, R("nm", l0, l1), False, False)
+        for m in range(4):
+            bank = "PD%d" % (m & 1)
+            for p in range(4 * m, 4 * m + 4):
+                group(R(bank, (p & 3) * 128, (p & 3) * 128 + nl), (nidn, zb), (idn, R("XC%d" % h, p, 16 * nl, 16)))
+            for p in range(4 * m, 4 * m + 4):
+                ac(col3("DD", l0, l1, p), R(bank, (p & 3) * 128, (p & 3) * 128 + nl), AF.Abs)
+            for p in range(4 * m, 4 * m + 4):
+                mm(PA, sel("sel1", p), col3("DD", l0, l1, p), False, p == 15)
+            if m & 1:
+                j = m >> 1
+                P = R("PC%d" % h, 272 + 64 * j, 272 + 64 * j + 8 * nc)
+                group(P, (R("LA", p=1), R("r8", 0, 8 * nc, p=1)), (l16, R(("b8a", "b8b")[j], 0, 8 * nc, p=16)),
+                      *[(sel("selm", q), lane3("DD", l0, l1, q, 8 * j, 8 * j + 8)) for q in range(16)])
+                lo = 128 * h + 64 * j
+                scan(R("SD", lo, lo + 8 * nc), R("rneg8", 0, 8 * nc), P, ALU.add, ALU.max)
+        ts(R("cap", l0, l1), PA, R("thr%d" % t), None, ALU.is_lt)
+        tt(R("com", l0, l1), R("PA", L + l0, L + l1), R("cap", l0, l1), ALU.mult)
+
+    def best(t, h):
+        l0, l1 = CH[h]
+        a, b, nl, nc = l0 // 16, l1 // 16, l1 - l0, (l1 - l0) // 16
+        lo = 128 * h + 7
+        tt(R("DI", a, b), R("SD", lo, lo + 8 * nc - 7, 8), R("SD", lo + 64, lo + 64 + 8 * nc - 7, 8), ALU.max)
+        ts(R("DA", a, b), R("DI", a, b), 2047, None, ALU.bitwise_and)
+        po = R("pxU", a, b)
+        ts(po, R("DA", a, b), -1.0, 2047.0, ALU.mult, ALU.add)
+        tt(R("ZS", l0, l1), X("XC%d" % h, 0, 16 * nl, po), R("zb%d" % t, l0, l1), ALU.add, off=[po])
+        ts(R("z16", l0, l1), R("ZS", l0, l1), 0.5, ZOFF - 0.25, ALU.mult, ALU.add)
+        ts(R(("zb1", "zf")[t], l0, l1), R("z16", l0, l1), -ZOFF, None, ALU.add)
+
+    def revoked(t):
+        red(R("xr"), R("com"), ALU.max)
+        ts(R("hi"), R("xr"), 1.0 / 256, -0.498, ALU.mult, ALU.add)
+        ts(R("rv%d" % t), R("hi"), -256.0, R("xr"), ALU.mult, ALU.add)
+
+    ac(R("KvT0"), R("ringS", *v0))
+    for h in range(2):
+        step1(0, h)
+    for t in range(2):
+        for h in range(2):
+            around(t, h)
+        request(t)
+        for h in range(2):
+            choose(t, h)
+            if t == 0:
+                move(h)
+        sources(t)
+        if t == 0:
+            for h, (l0, l1) in enumerate(CH):
+                o = R("voff", l0 // 16, l1 // 16)
+                cp(R("BvT", l0, l1), X("nbrS", 0, V, o), off=[o])
+                ac(R("KvT1", l0, l1), X("ringS", 0, V, o), off=[o])
+            cp(R("vW1"), R("SV", 15, L, 16))
+            tt(R("vWi"), R("vW1"), R("i1"), ALU.add)
+        for h in range(2):
+            distances(t, h)
+            best(t, h)
+            if t == 0:
+                step1(1, h)
+            if t == 1 and h == 0:
+                last = ("PK0", "PK1", "PM", "PC0")
+                for m in range(4):
+                    mm(R(last[m]), idn, R("TT", 512 * m, 512 * m + 512), True, False)
+        revoked(t)
+        if t == 0:
+            rv = R("rv0")
+            ts(R("nrv"), rv, -1.0, None, ALU.mult)
+            ts(R("m2rv"), rv, -2.0, None, ALU.mult)
+            ts(R("krv"), rv, -1.0, 2048.0, ALU.mult, ALU.add)
             cm = R("come", 0, 1)
-            for m in range(4):
-                a, b = 512 * m, 512 * m + 512
-                ts(R("e1", a, b), R("ringS", a, b), cm, cm, ALU.is_equal, ALU.mult)
-        dA(0, 2)
-        for m in range(4):
-            dsub(1, m)
-            if m == 0:
-                dA(0, 3)
-            dW(0, m)
-            if t == 0 and m == 2:
-                ac(R("V21"), R("wR"), AF.Identity, bias=1.0, scale=2.0)
-        for m in range(4):
-            dA(1, m)
-        for m in range(4):
-            dW(1, m)
-        best(0)
-        ts(R("cap"), R("PA", 0, L), R("thr%d" % t), None, ALU.is_lt)
-        tt(R("com"), R("PZ", 256, 256 + L), R("cap"), ALU.mult)
-        if t == 0:
-            best(1)
-        red(R("rvc"), R("com"), ALU.max)
-        cp(R("rvi"), R("rvc"))
-        ts(R("rvj"), R("rvi"), 255, None, ALU.bitwise_and)
-        if t == 0:
-            cp(R("rv0", 0, 1), R("rvj"))
-            step1(1)
-            remote(T.come[:, 0:1], R("rv0", 0, 1), "rr", "rl", nxt)
-            revoke(0, R("rv0", 0, 1), "ringS", ("PC0", "PC1", "PK", "PD0"))
-            remote(T.BIG1[:, NXT:NXT + V], R("ringS", 0, V), "xr1", "xl1", prev)
-            ac(R("KvT"), X("ringS", 0, V, R("voff")), off=[R("voff")])
+            send(cm, rv, "rv", nxt, prev)
+            ts(R("TT", 0, V), R("ringS"), rv, R("nrv"), ALU.is_equal, ALU.mult)
+            dma("G", T.TT[:, 0:V], T.ringS[:, :], rd=[R("ringS"), R("TT", 0, V)], wr=[R("TT", 0, V)], lat=3.0, cost=1.0, accum_op=ALU.add)
+            ts(R("cm1"), cm, rv, None, ALU.not_equal)
+            ts(R("ncm"), cm, -1.0, None, ALU.mult)
+            tt(R("ncm2"), R("ncm"), R("cm1"), ALU.mult)
+            ts(R("e1"), R("ringS"), cm, R("ncm2"), ALU.is_equal, ALU.mult)
+            dma("G", T.TT[:, 0:V], T.e1[:, :], rd=[R("e1"), R("TT", 0, V)], wr=[R("TT", 0, V)], lat=3.0, cost=1.0, accum_op=ALU.add)
+    dma("S", T.yz[:, :], T.zf[:, :], rd=[R("zf")])
+    for m in range(4):
+        a, b = 512 * m, 512 * m + 512
+        ts(R("e1", a, b), R("TT", a, b), R("rv1"), R("rv1"), ALU.is_equal, ALU.mult)
+        mm(R(last[m]), nidn, R("e1", a, b), False, True)
+        if m == 3:
+            cp(R("ykS", a, b), R(last[m]))
         else:
-            cp(R("rv1", 0, 1), R("rvj"))
-            tt(R("tmpc"), R("rv1", 0, 1), cm, ALU.not_equal)
-            tt(R("rv1", 1, 2), R("rv1", 0, 1), R("tmpc"), ALU.mult)
-            revoke(1, R("rv1", 1, 2), "ykS", ("PC0", "PC1", "PK", "PA"))
-            best(1)
-            dma("Y", T.yz[:, :], T.zf[:, :], rd=[R("zf")])
+            ac(R("ykS", a, b), R(last[m]))
+        dma("Y", T.yk[:, a:b], T.ykS[:, a:b], rd=[R("ykS", a, b)])
     if not PLAN:
         PLAN.extend(order())
     for i in PLAN:

@@ -1,38 +1,41 @@
 from concourse.mybir import AluOpType as ALU, AxisListType, ActivationFunctionType as AF
 
 L, V = 224, 2048
-CH = [(0, 128), (128, 224)]
+CH = [(0, 96), (96, 224)]
+GATHER = [[[(0, 48, "V"), (48, 96, "S")], [(96, 224, "S")]], [[(0, 96, "S")], [(96, 224, "S")]]]
+PLACES = [[[(0, 48, "V"), (48, 96, "S")], [(96, 160, "V"), (160, 224, "S")]], [[(0, 96, "S")], [(96, 128, "V"), (128, 224, "S")]]]
+RUNS = [[[(0, 96)], [(96, 224)]], [[(0, 96)], [(96, 224)]]]
+COPY = "SSVV"
 GIV = 240
 ZOFF = 1025.0
 BIGN = float(1 << 24)
 NENG = 8
-PASSES = 2500
-FIRST = 4.0
-WAKE, PE, HOP = 0.15, 0.00045, 4.5
+PASSES = 12000
+WAKE, PWAKE, SWAKE, PE, HALF = 0.2, 0.15, 0.18, 0.00056, 4
+HOP, FIRST, TABLE, ISSUE = 6.0, 2.0, 11.5, 0.8
 SCRATCH, SMALL, PLAN, SPAN, GRAPH = {}, {}, [], [], []
 B16, F16, F32, I32, U16 = "bfloat16", "float16", "float32", "int32", "uint16"
 for _d, _list in (
         (B16, (("ringS", V), ("matS", 4096), ("BIG0", 17 * 128), ("BIG1", 17 * 128), ("XC0", 2048), ("XC1", 2048),
-               ("SRW0", 480), ("SRW1", 480), ("rsp0", 240), ("rsp1", 240), ("zb0", L), ("zb1", L),
+               ("SRW", GIV + V), ("snd", 240), ("dlt", 240), ("zb0", L), ("zb1", L),
                ("ones", 128), ("sel1", 144), ("selk", 144), ("selm", 144), ("blk", 128), ("blk16", 128), ("trid", 128),
                ("idn", 128), ("nidn", 128), ("n256", 128), ("n128", 128), ("l16", 128), ("pen", L), ("tripen", L), ("OH", 32),
-               ("LA", 128), ("r9", 72), ("r8", 64), ("b9", 72), ("b9n", 72), ("b8a", 64), ("b8b", 64), ("tpr0", 128), ("tpr1", 128),
+               ("LL", 128), ("r17", 136), ("b17", 136), ("b17n", 136), ("b16", 128), ("xs", L), ("tpr0", 128), ("tpr1", 128),
                ("c16", 128), ("ramp", L), ("col", 128), ("colg", 128), ("c15", L),
-               ("KvT0", L), ("KvT1", L), ("hv", L), ("ev", L), ("hn", L), ("hw", L), ("nm", L), ("mq", L), ("cap", L),
+               ("KvT0", L), ("KvT1", L), ("hv", L), ("ev", L), ("hn", L), ("hw", L), ("nm", L), ("mq", L),
                ("GG", L), ("GA", L), ("eG", L), ("eH", L), ("KvP", L), ("fil", L), ("ne", L), ("eq", L),
                ("TT", V + L), ("e1", V), ("ykS", V), ("FF", 14), ("Finc", 14), ("na", 14))),
-        (F16, (("YY0", L), ("YY1", L), ("en", L), ("BnD", L), ("YW", L), ("z16", L))),
-        (F32, (("zf", L), ("blkf", 128), ("rneg", L), ("rneg8", 64), ("V20", L), ("V21", L), ("M1", 272), ("MM", 272), ("S0", 144),
-               ("D0s", 128), ("PR", L), ("SD", 256), ("ZS", L), ("HZ", L), ("BnF", L), ("dS", L), ("SV", L), ("com", L), ("oh", L),
+        (F16, (("YY0", L), ("YY1", L), ("en", L), ("YW", L), ("z16", L))),
+        (F32, (("zf", L), ("blkf", 128), ("rneg", L), ("rneg17", 136), ("V20", L), ("V21", L), ("M1", 238), ("MM", 238),
+               ("PR", L), ("cap", L), ("ZS", L), ("HZ", L), ("BnF", L), ("Bm", L), ("wA", L), ("num", V), ("idnf", 128), ("SV", L), ("com", L), ("oh", L),
                ("come", 4), ("okf", 16), ("zer", 16),
-               ("pf", 1), ("gf", 1), ("qc", 1), ("q15", 1), ("pc0", 1), ("pc1", 1), ("thr0", 1), ("thr1", 1), ("rowc", 14), ("iW", 14),
-               ("nk", 14), ("dW", 14), ("cA", 14), ("cB", 14), ("i1", 14), ("vW1", 14), ("vWi", 14), ("x1", 14), ("nd", 14), ("bb", 14),
-               ("srv", 14), ("s1", 14), ("s2", 14), ("t1", 14), ("xr", 1), ("rv0", 1), ("rv1", 1), ("nrv", 1), ("m2rv", 1),
-               ("krv", 1), ("cm1", 1), ("cm2", 1), ("ncm", 1), ("ncm2", 1))),
-        (I32, (("nbrS", V), ("thrI", 1), ("RI", L), ("SW", L), ("SH", L), ("SK", 128), ("BvT", L), ("PI", L), ("PJ", L),
-               ("pI", 1), ("qI", 1), ("gI", 1), ("KA", 14), ("KS", 14), ("KK", 14), ("DI", 14), ("DA", 14), ("HJ", 14),
-               ("hi", 1), ("fi", 1), ("fj", 1))),
-        (U16, (("Bn", L), ("PL", L), ("hU0", 16), ("hU1", 16), ("req0", 16), ("req1", 16), ("oKU", 28),
+               ("pf", 1), ("gf", 1), ("qc", 1), ("q15", 1), ("pc0", 1), ("pc1", 1), ("thB0", 1), ("thB1", 1), ("m16", 1), ("n16", 1),
+               ("c16x", 1), ("rowc", 14), ("iW", 14), ("nk", 14), ("dW", 14), ("cA", 14), ("hW", 14), ("i1", 14), ("vW1", 14),
+               ("vWi", 14), ("x1", 14), ("nd", 14), ("bb", 14), ("srv", 14), ("s1", 14), ("s2", 14), ("s3", 14), ("t1", 14), ("xr", 1),
+               ("rv0", 1), ("rv1", 1), ("nrv", 1), ("m2rv", 1), ("krv", 1), ("cm1", 1), ("ncm", 1), ("ncm2", 1))),
+        (I32, (("nbrS", V), ("thrI", 1), ("RI", L), ("SW", L), ("SH", L), ("SK", 238), ("SD", L), ("BvT", L), ("PI", L), ("PJ", L),
+               ("pI", 1), ("qI", 1), ("gI", 1), ("KA", 14), ("KK", 14), ("DA", 14), ("HJ", 14), ("hi", 1), ("fi", 1), ("fj", 1))),
+        (U16, (("Bn", L), ("PL", L), ("oKU", 28),
                ("noff", 14), ("posU", 14), ("kU", 14), ("pxU", 14), ("voff", 14), ("spU", 14), ("rp", 14)))):
     for _n, _w in _list:
         if _w in (1, 14) and _n != "thrI":
@@ -47,7 +50,7 @@ BANKS = ("PK0", "PK1", "PC0", "PC1", "PD0", "PD1", "PA", "PM")
 for _n in BANKS:
     SCRATCH[_n] = ("psum", [128, 512], F32)
 SEMAPHORES = (["sV", "sS", "sP", "sG"] + ["d%d" % i for i in range(20)]
-              + [a + b for a in ("q0", "q1", "a0", "a1", "rv") for b in "rl"])
+              + [a + b for a in ("tb", "dl", "rv") for b in "rl"])
 
 
 def rank_program(g, core, T, topo):
@@ -126,13 +129,13 @@ def rank_program(g, core, T, topo):
         note(e, wr, True, s, total[s], snap)
 
     def order():
-        succ, chain, acc = [[] for _ in ops], [], {}
+        succ, chain, acc = [[] for _ in ops], {}, {}
         for i, (e, fn, rd, wr, s, inc, cost, lat) in enumerate(ops):
             before = {}
-            if e == "Y":
-                if chain:
-                    before[chain[-1]] = 0.0
-                chain.append(i)
+            if e in "YS" and s[0] == "d":
+                if e in chain:
+                    before[chain[e]] = 0.0
+                chain[e] = i
             for refs, write in ((rd, False), (wr, True)):
                 for name, lo, hi, tag in refs:
                     for (l2, h2, w2, j, t2) in acc.get(name, ()):
@@ -140,11 +143,11 @@ def rank_program(g, core, T, topo):
                         if name in BANKS:
                             if same and not (write or w2):
                                 continue
-                            d = 0.0 if same and e == "P" else ops[j][7]
-                        else:
-                            if not (write or w2) or not meet(lo, hi, tag, l2, h2, t2):
-                                continue
-                            d = ops[j][7]
+                        elif not (write or w2) or not meet(lo, hi, tag, l2, h2, t2):
+                            continue
+                        d = ops[j][7]
+                        if ops[j][4] == semof.get(ops[j][0]):
+                            d = (0.0 if e == "P" else SWAKE) if same else (PWAKE if e == "P" else WAKE)
                         before[j] = max(before.get(j, 0.0), d)
             for refs, write in ((rd, False), (wr, True)):
                 for name, lo, hi, tag in refs:
@@ -204,17 +207,21 @@ def rank_program(g, core, T, topo):
             return seed[0] / (1 << 31)
 
         best_ = cur = forwards([float(i) for i in range(n)])
-        for _ in range(PASSES):
-            size, shift, key = (0.2, 0.5, 1.5, 3.0)[int(4 * draw())], {}, []
+        for it in range(PASSES):
+            size, shift, key, mid = (0.2, 0.5, 1.5, 3.0)[int(4 * draw())], {}, [], draw() * cur[0]
             for i in range(n):
-                k = (kind[i], int(cur[1][i] / 4))
-                if k not in shift:
-                    shift[k] = size * (2 * draw() - 1) if draw() < 0.3 else 0.0
-                key.append(cur[1][i] - cost[i] + shift[k])
+                s = cur[1][i] - cost[i]
+                if abs(s - mid) < 6:
+                    k = (kind[i], int(s / 4))
+                    if k not in shift:
+                        shift[k] = size * (2 * draw() - 1) if draw() < 0.3 else 0.0
+                    s += shift[k]
+                key.append(s)
             a = forwards(key)
-            b = again(a[1])
-            a = a if a[0] < b[0] else b
-            if a[0] <= cur[0] + 0.05:
+            if draw() < 0.3:
+                b = again(a[1])
+                a = a if a[0] < b[0] else b
+            if a[0] <= cur[0] + 0.3 * (1 - it / PASSES) * draw() + 0.005:
                 cur = a
             if a[0] < best_[0]:
                 best_ = a
@@ -269,21 +276,22 @@ def rank_program(g, core, T, topo):
         c = 0.05 + 0.00083 * 1.56 * out[5] if off else vcost(out[5], 0.5 if wide(out, a) else 1)
         emit("V", lambda: g.vector.tensor_copy(out[0], a[0]), [a] + list(off), [out], cost=c)
 
-    def scan(out, d0, d1, op0, op1, first=0.0):
-        emit("V", lambda: g.vector.tensor_tensor_scan(out[0], d0[0], d1[0], first, op0, op1), [d0, d1], [out], cost=vcost(out[5], 1))
+    def scan(out, d0, d1, op0, op1):
+        emit("V", lambda: g.vector.tensor_tensor_scan(out[0], d0[0], d1[0], 0.0, op0, op1), [d0, d1], [out], cost=vcost(out[5], 1))
 
     def red(out, a, op):
         emit("V", lambda: g.vector.tensor_reduce(out[0], a[0], AxisListType.X, op), [a], [out], cost=vcost(a[5], 1))
 
     def ac(out, a, func=AF.Copy, off=(), **kw):
         c = 0.065 + 0.00083 * 1.56 * out[5] if off else vcost(out[5], 1)
-        emit("S", lambda: g.scalar.activation(out[0], a[0], func, **kw), [a] + list(off), [out], cost=c)
+        rd, kw = [a] + list(off) + cols(*kw.values()), {k: val(x) for k, x in kw.items()}
+        emit("S", lambda: g.scalar.activation(out[0], a[0], func, **kw), rd, [out], cost=c)
 
     def fill(out, c):
         emit("V", lambda: g.vector.memset(out[0], c), [], [out], cost=vcost(out[5], 0.5 if wide(out) else 1))
 
     def mm(out, lhsT, rhs, start, stop):
-        c = PE * max(64, out[5]) * (1 if wide(rhs) else 4)
+        c = PE * max(64, out[5]) * {B16: 1, F16: HALF, F32: 4}[SCRATCH[rhs[1]][2]]
         emit("P", lambda: g.tensor.matmul(out[0], lhsT[0], rhs[0], start, stop), [lhsT, rhs], [out], cost=c)
 
     def group(out, *terms):
@@ -295,7 +303,7 @@ def rank_program(g, core, T, topo):
 
     ndma = [0]
 
-    def dma(e, out, a, rd=(), wr=(), lat=2.0, cost=0.06, **kw):
+    def dma(e, out, a, rd=(), wr=(), lat=1.0, cost=ISSUE, **kw):
         s = "d%d" % ndma[0]
         ndma[0] += 1
         emit(e, lambda: queue[e].dma_start(out, a, **kw), list(rd), list(wr), s, 16, cost=cost, lat=lat)
@@ -307,28 +315,26 @@ def rank_program(g, core, T, topo):
         def call():
             g.remote_dma(out[0], src[0], T.sem[sem + "r"], T.sem[sem + "l"], pid, rid, mask)
         flag = (None, sem + "l", 0, 1, None)
-        emit("G", call, [src], [flag], sem + "l", NENG, 1.2 + FIRST * (sem == "q0"), HOP)
+        emit("G", call, [src], [flag], sem + "l", NENG, 0.8 + FIRST * (sem == "tb"), HOP + TABLE * (sem == "tb"))
         emit("R", None, [flag], [out], sem + "r", len(topo.engines(frm, core)[:NENG]), 0.0, 0.1)
 
     prev, nxt = T.cores[(rank - 1) % N], T.cores[(rank + 1) % N]
-    dma("Y", T.zb0[:, :], T.z0[:, :], wr=[R("zb0")], lat=1.5)
-    dma("Y", T.thrI[:, :], T.thr[:, :], wr=[R("thrI")], lat=1.5)
-    dma("Y", T.nbrS[:, :], T.nbr[:, :], wr=[R("nbrS")], lat=4.5)
-    dma("Y", T.ringS[:, :], T.ring[:, :], wr=[R("ringS")], lat=6.0)
-    dma("Y", T.matS[:, :], T.mat[:, :], wr=[R("matS")], lat=9.0)
+    dma("S", T.zb0[:, :], T.z0[:, :], wr=[R("zb0")], lat=0.5)
+    dma("Y", T.nbrS[:, :], T.nbr[:, :], wr=[R("nbrS")], lat=2.4)
+    dma("S", T.ringS[:, :], T.ring[:, :], wr=[R("ringS")], lat=2.2)
+    dma("Y", T.matS[:, :], T.mat[:, :], wr=[R("matS")], lat=4.2)
+    dma("Y", T.thrI[:, :], T.thr[:, :], wr=[R("thrI")], lat=3.2)
     iota(R("pI"), [[1, 1]], 0, 1)
     iota(R("colg"), [[1, 8], [0, 16]], 0, 0)
     iota(R("tpr0", p=1), [[0, 8], [-1, 16]], 0, 0)
     iota(R("c15"), [[0, 14], [1, 16]], 0, 0)
     iota(R("col"), [[1, 128]], 0, 0)
     iota(R("rowc"), [[16, 14]], 0, 0)
-    iota(R("LA", p=2), [[0, 128]], 256, -(1 << 19) - 256)
-    iota(R("r9", p=2), [[-1, 8], [0, 9]], 7, 0)
-    iota(R("r8", p=2), [[-1, 8], [0, 8]], 7, 0)
-    iota(R("b9", p=16), [[0, 8], [-1, 9]], 256, -16)
-    iota(R("b8a", p=16), [[0, 8], [-1, 8]], 255, -16)
+    iota(R("r17", p=32), [[-1, 8], [0, 17]], 7, 0)
+    iota(R("b17", p=32), [[0, 8], [-1, 17]], 256, -16)
     iota(R("V20"), [[18, L]], 1, 0)
     iota(R("ramp", p=1), [[-256, L]], 256 * L, 0)
+    iota(R("num"), [[1, V]], 0, 0)
     fill(R("ones"), 1.0)
     fill(R("c16", p=1), 1.0 / 16)
     ts(R("qI"), R("pI"), 15, None, ALU.bitwise_and)
@@ -337,67 +343,64 @@ def rank_program(g, core, T, topo):
     cp(R("gf"), R("gI"))
     cp(R("pf"), R("pI"))
     ts(R("blk"), R("colg"), R("gf"), None, ALU.is_equal)
-    ts(R("blk16"), R("blk"), 1.0 / 16, None, ALU.mult)
-    ts(R("tpr1", p=1), R("tpr0", p=1), 1.0, None, ALU.add)
     ts(R("l16"), R("c15", 0, 128), R("qc"), None, ALU.is_equal)
     ts(R("pen"), R("c15"), R("qc"), -BIGN, ALU.not_equal, ALU.mult)
     ts(R("tripen"), R("c15"), R("qc"), -4096.0, ALU.is_le, ALU.mult)
     ts(R("idn"), R("col"), R("pf"), None, ALU.is_equal)
-    for name, c in (("nidn", -1.0), ("n256", -256.0), ("n128", -128.0)):
-        ts(R(name), R("idn"), c, None, ALU.mult)
     ts(R("trid"), R("col"), R("pf"), -1.0, ALU.is_lt, ALU.mult)
     tt(R("trid"), R("trid"), R("blk"), ALU.mult)
-    cp(R("blkf"), R("blk"))
     fill(R("sel1"), 0.0)
-    cp(R("sel1", 15, 143, 16), R("blk", 0, 128, 16))
-    ts(R("selk"), R("sel1"), 4096.0, None, ALU.mult)
-    ts(R("selm"), R("sel1"), -2048.0, None, ALU.mult)
-    ts(R("q15"), R("qc"), -1.0, 15.0, ALU.mult, ALU.add)
+    ac(R("sel1", 15, 143, 16), R("blk", 0, 128, 16))
+    for name, of, c in (("blk16", "blk", 1.0 / 16), ("blkf", "blk", 1.0), ("idnf", "idn", 1.0), ("nidn", "idn", -1.0), ("n256", "idn", -256.0),
+                        ("n128", "idn", -128.0), ("selk", "sel1", 4096.0), ("selm", "sel1", -2048.0)):
+        ac(R(name), R(of), scale=c)
+    ac(R("tpr1", p=1), R("tpr0", p=1), AF.Identity, bias=1.0)
+    ac(R("q15"), R("qc"), AF.Identity, scale=-1.0, bias=15.0)
     fill(R("OH", 16, 32), 0.0)
     ts(R("OH", 0, 16), R("c15", 0, 16), R("q15"), None, ALU.is_equal)
-    fill(R("r9", 0, 72, 9, p=2), 0.0)
-    cp(R("b9n", p=16), R("b9", p=16))
-    fill(R("b9", 0, 72, 9, p=16), 0.0)
-    fill(R("b9n", 0, 72, 9, p=16), float(1 << 23))
-    ts(R("b8b", p=16), R("b8a", p=16), -8.0, None, ALU.add)
+    ts(R("m16"), R("pf"), 16.0, None, ALU.is_equal)
+    ts(R("n16"), R("pf"), 16.0, None, ALU.not_equal)
+    ac(R("c16x"), R("m16"), scale=256.0)
+    ac(R("LL"), R("l16"), AF.Identity, scale=R("n16"), bias=R("c16x"))
+    ac(R("b17", p=32), R("b17", p=32), AF.Identity, scale=R("n16", p=32))
+    ac(R("r17", p=32), R("r17", p=32), AF.Identity, scale=R("m16", p=32))
+    tt(R("b17", p=32), R("b17", p=32), R("r17", p=32), ALU.add)
+    for c in range(8):
+        ac(R("b16", 16 * c, 16 * c + 16, p=32), R("b17", 17 * c + 1, 17 * c + 17, p=32))
+    fill(R("b17", 0, 136, 17, p=32), 0.0)
+    ac(R("b17n", p=32), R("b17", p=32))
+    fill(R("b17n", 0, 136, 17, p=16), float(1 << 23))
     for t in range(2):
-        ts(R("pc%d" % t), R("qc"), 811.0, t - 0.375, ALU.mult, ALU.add)
-        fill(R("SRW%d" % t, L, GIV), 0.0)
+        ac(R("pc%d" % t), R("qc"), AF.Identity, scale=811.0, bias=t - 0.375)
+    fill(R("SRW", L, GIV), 0.0)
     fill(R("rneg"), 0.0)
     fill(R("rneg", 0, L, 16), -BIGN)
-    fill(R("rneg8"), 0.0)
-    fill(R("rneg8", 0, 64, 8), -BIGN)
-    fill(R("D0s"), -BIGN / 2)
+    fill(R("rneg17"), 0.0)
+    fill(R("rneg17", 0, 136, 17), -BIGN)
     fill(R("zer"), 0.0)
     fill(R("okf"), 0.0)
     fill(col3("E2", 0, L, 0), 0.0)
-    ts(R("iW"), R("rowc"), R("qc"), None, ALU.add)
+    ac(R("iW"), R("rowc"), AF.Identity, bias=R("qc"))
     for h, (l0, l1) in enumerate(CH):
-        a, b = l0 // 16, l1 // 16
-        ts(R("x1", a, b), R("rowc", a, b), float(1 << 15), -float((1 << 19) * (7 + a)), ALU.mult, ALU.add)
-        ts(R("nk", a, b), R("iW", a, b), -1.0, float(4096 + 2047 + l1), ALU.mult, ALU.add)
-    tt(R("nk"), R("nk"), R("x1"), ALU.add)
-    ts(R("dW"), R("iW"), float(V), None, ALU.add)
-    ts(R("cA"), R("iW"), -float(L), None, ALU.add)
-    ts(R("cB"), R("iW"), float(GIV - L), None, ALU.add)
-    ts(R("i1"), R("iW"), 1.0, None, ALU.add)
+        ac(R("nk", l0 // 16, l1 // 16), R("iW", l0 // 16, l1 // 16), AF.Identity, scale=-1.0, bias=float(4096 + 2047 + l1))
+    for name, c in (("dW", V), ("cA", -L), ("i1", 1)):
+        ac(R(name), R("iW"), AF.Identity, bias=float(c))
     ts(R("rp"), R("rowc"), 1.0 / 16, None, ALU.mult)
-    cp(R("thr0"), R("thrI"))
+    ts(R("thB0"), R("thrI"), 65536.0, None, ALU.mult)
 
     idn, nidn, blk, l16 = R("idn"), R("nidn"), R("blk"), R("l16", p=16)
-    v0 = (0, 9 * (L - 1) + 1, 9)
 
     def sel(name, q):
         return R(name, 15 - q, 143 - q)
 
-    def first(name, l0, l1):
-        return R(name, 9 * l0, 9 * (l1 - 1) + 1, 9)
+    def first(name, l0=0, l1=L, base=0):
+        return R(name, base + 9 * l0, base + 9 * (l1 - 1) + 1, 9)
 
     def step1(t, h):
         l0, l1 = CH[h]
         a, b, nl, PK = l0 // 16, l1 // 16, l1 - l0, "PK%d" % h
         u, EJ, YY = R(PK, 384, 384 + nl), R(PK, 256, 256 + nl), R("YY%d" % t, l0, l1)
-        group(u, (R("tpr%d" % t, p=1), R("c16", 0, nl, p=1)), (R("blk16"), R("zb0" if t == 0 else "z16", l0, l1)))
+        group(u, (R("tpr%d" % t, p=1), R("c16", 0, nl, p=1)), (R("blk16"), R("zb%d" % t, l0, l1)))
         cp(R("RI", l0, l1), u)
         tt(EJ, u, R("RI", l0, l1), ALU.is_equal)
         tt(YY, EJ, first("nbrS", l0, l1) if t == 0 else R("BvT", l0, l1), ALU.mult)
@@ -410,10 +413,10 @@ def rank_program(g, core, T, topo):
         a, b, nl, PK, BIG = l0 // 16, l1 // 16, l1 - l0, "PK%d" % h, "BIG%d" % h
         no, Kv, Kn = R("noff", a, b), R("KvT%d" % t, l0, l1), R(BIG, 0, nl)
         cp(R("Bn", l0, l1), X("nbrS", 0, V, no), off=[no])
-        ac(Kn, X("ringS", 0, V, no), off=[no])
-        for x, y in parts(h):
+        (ac if t or h else cp)(Kn, X("ringS", 0, V, no), off=[no])
+        for x, y, e in GATHER[t][h]:
             o = R("Bn", x, y)
-            ac(R(BIG, nl + 16 * (x - l0), nl + 16 * (y - l0)), X("ringS", 0, V, o), off=[o])
+            (ac if e == "S" else cp)(R(BIG, nl + 16 * (x - l0), nl + 16 * (y - l0)), X("ringS", 0, V, o), off=[o])
         ts(R("hv", l0, l1), Kv, 0.0, -1.0, ALU.is_equal, ALU.mult)
         ts(R("hn", l0, l1), Kn, 0.0, 2048.0, ALU.is_equal, ALU.mult)
         tv, tn = [(idn, Kv), (idn, R("hv", l0, l1))], [(idn, Kn), (idn, R("hn", l0, l1))]
@@ -427,83 +430,62 @@ def rank_program(g, core, T, topo):
         tt(R("HZ", l0, l1), R(PK, 128, 128 + nl), R("zb%d" % t, l0, l1), ALU.mult)
         tt(col3("E1", l0, l1, 0), R(PK, 0, nl), Kn, ALU.is_equal)
         if t == 0:
-            P = R("PD%d" % h, 0, nl)
-            group(P, (blk, R("YY0", l0, l1)))
             cp(R("BnF", l0, l1), R("Bn", l0, l1))
-            tt(R("BnD", l0, l1), R("BnF", l0, l1), P, ALU.subtract)
-
-    def parts(h):
-        l0, l1 = CH[h]
-        return [(l0, l0 + 64), (l0 + 64, l1)] if l1 - l0 == 128 else [(l0, l1)]
 
     def request(t):
         P = R("PD0", 256, 256 + L)
         group(P, (l16, R("pen", p=16)), (R("blkf"), R("HZ")))
         scan(R("SH"), R("rneg"), P, ALU.add, ALU.max)
         ts(R("HJ"), R("SH", 15, L, 16), V - 1, None, ALU.bitwise_and)
-        cp(R("hU%d" % t, 0, 14), R("HJ"))
-        rq = R("req%d" % t, 0, 14)
-        send(rq, R("hU%d" % t, 0, 14), "q%d" % t, nxt, prev)
-        ac(R("rsp%d" % t, 0, L), X("ringS", 0, V, rq), off=[rq])
-        if t == 1:
-            cp(R("rsp1", L, L + 1), R("rv0"))
-        send(R("SRW%d" % t, GIV, GIV + L + t), R("rsp%d" % t, 0, L + t), "a%d" % t, prev, nxt)
+        ts(R("hW"), R("HJ"), float(GIV - L), None, ALU.add)
 
-    def compare(h, which, k0, k1, runs):
+    def compare(h, which, runs):
         l0, l1 = CH[h]
         nl, En = l1 - l0, "E%d" % (which + 1)
         for x, y in runs:
             lo = nl + 16 * (x - l0)
-            for k in range(k0, k1):
+            for k in range(16):
                 tt(col3(En, x, y, k + 1), R("PK%d" % h, 128 * which + x - l0, 128 * which + y - l0),
                    R("BIG%d" % h, lo + k, lo + 16 * (y - x), 16), ALU.is_equal)
 
-    def count(h, which, half):
+    def count(h, which):
         l0, l1 = CH[h]
-        nc = (l1 - l0) // 16
-        w, lo = (9, 136 * which) if half == 0 else (8, 136 * which + 72)
-        P = R("PC%d" % h, lo, lo + w * nc)
-        low = ("b9", "b9n")[which] if half == 0 else "b8b"
-        group(P, (R("LA", p=2), R("r%d" % w, 0, w * nc, p=2)), (l16, R(low, 0, w * nc, p=16)),
-              *[(sel("selk", q), lane3("E%d" % (which + 1), l0, l1, q, 9 * half, 9 + 8 * half)) for q in range(16)])
+        w = 17 * (l1 - l0) // 16
+        P = R("PC%d" % h, 136 * which, 136 * which + w)
+        group(P, (R("LL", p=17), R(("b17", "b17n")[which], 0, w, p=17)),
+              *[(sel("selk", q), lane3("E%d" % (which + 1), l0, l1, q, 0, 17)) for q in range(16)])
         return P
 
     def choose(t, h):
         l0, l1 = CH[h]
-        a, b, nl, nc = l0 // 16, l1 // 16, l1 - l0, (l1 - l0) // 16
-        BIG, m0 = "BIG%d" % h, 136 * h
-        compare(h, 0, 0, 16, parts(h) if t == 0 else [(l0, l1)])
-        ac(R("M1", m0, m0 + 9 * nc), count(h, 0, 0))
-        ac(R("M1", m0 + 72, m0 + 72 + 8 * nc), count(h, 0, 1))
-        mn = R("M1", m0, m0 + 9 * nc, 9)
+        a, b, nl = l0 // 16, l1 // 16, l1 - l0
+        BIG, m0, m1 = "BIG%d" % h, 17 * a, 17 * b
+        compare(h, 0, RUNS[t][h])
+        ac(R("M1", m0, m1), count(h, 0))
+        mn = R("M1", m0, m1, 17)
         ts(R("x1", a, b), mn, 8192.0, float(1 << 18), ALU.is_ge, ALU.mult)
         tt(mn, R("x1", a, b), R("nk", a, b), ALU.add)
-        compare(h, 1, 0, 8, [(l0, l1)])
-        MM = R("MM", m0, m0 + 9 * nc)
-        tt(MM, count(h, 1, 0), R("M1", m0, m0 + 9 * nc), ALU.min)
-        scan(R("S0", 72 * h, 72 * h + 9 * nc), MM, MM, ALU.max, ALU.max, -BIGN / 2)
-        cp(R("D0s", 64 * h, 64 * h + 8 * nc, 8), R("S0", 72 * h + 8, 72 * h + 9 * nc, 9))
-        compare(h, 1, 8, 16, [(l0, l1)])
-        MM = R("MM", m0 + 72, m0 + 72 + 8 * nc)
-        tt(MM, count(h, 1, 1), R("M1", m0 + 72, m0 + 72 + 8 * nc), ALU.min)
-        scan(R("SK", 64 * h, 64 * h + 8 * nc), R("D0s", 64 * h, 64 * h + 8 * nc), MM, ALU.max, ALU.max, -BIGN / 2)
-        top = R("SK", 64 * h + 7, 64 * h + 8 * nc, 8)
-        ts(R("KA", a, b), top, 4095, None, ALU.bitwise_and)
+        compare(h, 1, [(l0, l1)])
+        tt(R("MM", m0, m1), count(h, 1), R("M1", m0, m1), ALU.min)
+        scan(R("SK", m0, m1), R("rneg17", 0, m1 - m0), R("MM", m0, m1), ALU.add, ALU.max)
+        ts(R("KA", a, b), R("SK", m0 + 16, m1, 17), 4095, None, ALU.bitwise_and)
         po = R("posU", a, b)
         ts(po, R("KA", a, b), -1.0, float(2047 + nl), ALU.mult, ALU.add)
-        w, PR = X(BIG, 0, 17 * nl, po), R("PR", l0, l1)
-        tt(PR, w, R("V2%d" % t, l0, l1), ALU.mult, off=[po])
-        if t == 1:
-            ts(R("mq", l0, l1), w, R("rv0"), None, ALU.not_equal, off=[po])
-            tt(PR, PR, R("mq", l0, l1), ALU.mult)
-        Kw = R("SRW%d" % t, l0, l1)
+        w, PR, Kw, V2 = X(BIG, 0, 17 * nl, po), R("PR", l0, l1), R("SRW", l0, l1), R("V2%d" % t, l0, l1)
         ac(Kw, w, off=[po], scale=-1.0)
+        if t == 0:
+            tt(PR, w, V2, ALU.mult, off=[po])
+        else:
+            P = R("PK%d" % h, 384, 384 + nl)
+            ts(R("mq", l0, l1), Kw, R("nrv"), R("nrv"), ALU.is_equal, ALU.mult)
+            group(P, (nidn, Kw), (idn, R("mq", l0, l1)))
+            tt(PR, P, V2, ALU.mult)
         ts(R("PI", l0, l1), PR, 0.25, R("pc%d" % t), ALU.mult, ALU.add)
         ts(R("PJ", l0, l1), R("PI", l0, l1), 4095, None, ALU.bitwise_and)
         cp(R("PL", l0, l1), R("PJ", l0, l1))
-        o = R("PL", l0, l1)
-        ac(R("XC%d" % h, 0, 16 * nl), X("matS", 0, 4096, o), off=[o])
-        ts(R("KS", a, b), top, (1 << 19) - 1, None, ALU.bitwise_and)
+        for x, y, e in PLACES[t][h]:
+            o = R("PL", x, y)
+            (ac if e == "S" else cp)(R("XC%d" % h, 16 * (x - l0), 16 * (y - l0)), X("matS", 0, 4096, o), off=[o])
         ts(R("hw", l0, l1), Kw, 0.0, 8192.0, ALU.is_equal, ALU.mult)
         if t == 1:
             ts(R("nm", l0, l1), Kw, R("nrv"), 8192.0, ALU.is_equal, ALU.mult)
@@ -514,21 +496,27 @@ def rank_program(g, core, T, topo):
         ts(R("KK", a, b), R("KA", a, b), 2048 + 15, None, ALU.bitwise_and)
         ko, YW, YY = R("kU", a, b), R("YW", l0, l1), R("YY0", l0, l1)
         ts(ko, R("KK", a, b), 16.0, None, ALU.min)
-        tt(YW, X("OH", 0, 32, ko), R("BnD", l0, l1), ALU.mult, off=[ko])
-        group(R("PM", 0, nl), (blk, YW))
-        group(R("PM", 128, 128 + nl), (blk, YW), (blk, YY))
-        group(R("PM", 256, 256 + nl), (l16, R("pen", 0, nl, p=16)), (blk, YY), (blk, YW))
+        tt(YW, X("OH", 0, 32, ko), R("BnF", l0, l1), ALU.mult, off=[ko])
+        group(R("PM", 256, 256 + nl), (l16, R("pen", 0, nl, p=16)), (blk, YW))
         scan(R("SV", l0, l1), R("rneg", 0, nl), R("PM", 256, 256 + nl), ALU.add, ALU.max)
-        ac(R("dS", l0, l1), R("PM", 0, nl))
-        ac(R("V21", l0, l1), R("PM", 128, 128 + nl), AF.Identity, bias=1.0, scale=2.0)
-        cp(R("voff", a, b), R("SV", l0 + 15, l1, 16))
+        th, vo, wA = R("t1", a, b), R("voff", a, b), R("wA", l0, l1)
+        ts(th, R("KK", a, b), 16.0, None, ALU.is_ge)
+        tt(th, th, R("SW", l0 + 15, l1, 16), ALU.mult)
+        tt(R("vW1", a, b), R("SV", l0 + 15, l1, 16), th, ALU.add)
+        cp(vo, R("vW1", a, b))
+        ac(wA, X("num", 0, V, vo), off=[vo])
+        ac(R("V21", l0, l1), wA, AF.Identity, bias=1.0, scale=2.0)
         EJ = R("PK%d" % h, 256, 256 + nl)
-        tt(EJ, EJ, R("dS", l0, l1), ALU.mult)
-        tt(first("nbrS", l0, l1), EJ, first("nbrS", l0, l1), ALU.add)
+        tt(R("Bm", l0, l1), first("nbrS", l0, l1), YY, ALU.subtract)
+        tt(EJ, EJ, wA, ALU.mult)
+        tt(first("nbrS", l0, l1), EJ, R("Bm", l0, l1), ALU.add)
 
     def sources(t):
-        ts(R("FF"), R("KS"), 8192.0, None, ALU.is_lt)
-        ts(R("nd"), R("KS"), float(1 << 18), None, ALU.is_lt)
+        if t == 1:
+            group(R("PM", 256, 256 + L), (idn, R("KvT1")), (idn, R("ev")))
+            ac(R("KvP"), R("PM", 256, 256 + L))
+        ts(R("FF"), R("SK", 16, 238, 17), 8192.0, None, ALU.is_lt)
+        ts(R("nd"), R("SK", 16, 238, 17), float(1 << 18), None, ALU.is_lt)
         scan(R("Finc"), R("FF"), R("zer", 0, 14), ALU.add, ALU.add)
         tt(R("bb"), R("nd"), R("FF"), ALU.subtract)
         group(R("PM", 480, 494), (blk, R("Finc")), (R("trid"), R("FF")))
@@ -538,38 +526,38 @@ def rank_program(g, core, T, topo):
         if t == 0:
             cp(R("fi"), R("PM", 496, 497))
             ts(R("fj"), R("fi"), 15, None, ALU.bitwise_and)
-            tt(R("thr1"), R("fj"), R("thr0"), ALU.add)
+            ts(R("thB1"), R("fj"), 65536.0, R("thB0"), ALU.mult, ALU.add)
         tt(R("s1"), R("bb"), R("cA"), ALU.mult)
         tt(R("srv"), R("srv"), R("FF"), ALU.mult)
-        tt(R("s2"), R("srv"), R("cB"), ALU.mult)
+        tt(R("s2"), R("srv"), R("hW"), ALU.mult)
         tt(R("s1"), R("s1"), R("s2"), ALU.add)
         sp = R("spU")
         ts(sp, R("s1"), float(L), None, ALU.add)
-        src, P = X("SRW%d" % t, 0, GIV + L, sp), R("PM", 0, L)
+        src, P = X("SRW", 0, GIV + V, sp), R("PM", 0, L)
         if t == 0:
             ac(R("GA"), src, AF.Abs, off=[sp])
             group(P, (R("n256"), R("KvT0")), (idn, R("GA")))
-            tt(R("ringS", *v0), P, R("KvT0"), ALU.max)
+            tt(first("ringS"), P, R("KvT0"), ALU.max)
+            ac(R("snd", 0, L), first("ringS"))
             return
         ac(R("GG"), src, off=[sp])
         ac(R("GA"), R("GG"), AF.Abs)
-        rvn = R("SRW1", GIV + L, GIV + L + 1)
+        rvn = R("dlt", L, L + 1)
         ts(R("eG"), R("GG"), rvn, rvn, ALU.is_equal, ALU.mult)
         ts(R("eH"), R("GG"), R("nrv"), R("nrv"), ALU.is_equal, ALU.mult)
-        group(R("PM", 256, 256 + L), (idn, R("KvT1")), (idn, R("ev")))
-        ac(R("KvP"), R("PM", 256, 256 + L))
         group(P, (R("n256"), R("KvT1")), (R("n128"), R("ev")), (idn, R("GA")), (nidn, R("eG")), (idn, R("eH")))
         tt(R("fil"), P, R("KvP"), ALU.max)
         ts(R("ne"), R("fil"), R("come", 0, 1), R("ncm"), ALU.is_equal, ALU.mult)
-        tt(R("s2"), R("srv"), R("bb"), ALU.add)
-        ts(R("na"), R("s2"), -1.0, 1.0, ALU.mult, ALU.add)
-        tt(R("s2"), R("s2"), R("vWi"), ALU.mult)
-        tt(R("okf", 0, 14), R("s2"), R("i1"), ALU.subtract)
+        tt(R("s3"), R("srv"), R("bb"), ALU.add)
+        ts(R("na"), R("s3"), -1.0, 1.0, ALU.mult, ALU.add)
+        tt(R("s3"), R("s3"), R("vWi"), ALU.mult)
+        tt(R("okf", 0, 14), R("s3"), R("i1"), ALU.subtract)
         ac(R("oh"), X("okf", 0, 16, R("rp")), off=[R("rp")])
-        group(P, (l16, R("tripen", p=16)), (blk, R("YW")), (blk, R("YY0")))
+        P, Q = R("PK0", 0, L), R("PK0", 256, 270)
+        group(P, (l16, R("tripen", p=16)), (R("idnf"), R("wA")))
         tt(R("eq"), P, R("oh"), ALU.is_equal)
-        group(R("PM", 480, 494), (idn, R("na")), *[(sel("sel1", q), R("eq", q, L, 16)) for q in range(16)])
-        ts(R("t1"), R("PM", 480, 494), 0.5, 4096.0, ALU.is_ge, ALU.mult)
+        group(Q, (idn, R("na")), *[(sel("sel1", q), R("eq", q, L, 16)) for q in range(16)])
+        ts(R("t1"), Q, 0.5, 4096.0, ALU.is_ge, ALU.mult)
         tt(R("t1"), R("t1"), R("dW"), ALU.min)
         tt(R("t1"), R("t1"), R("vW1"), ALU.max)
         cp(R("oKU", 0, 28, 2), R("t1"))
@@ -579,8 +567,8 @@ def rank_program(g, core, T, topo):
 
     def distances(t, h):
         l0, l1 = CH[h]
-        nl, nc, zb = l1 - l0, (l1 - l0) // 16, R("zb%d" % t, l0, l1)
-        group(R("PA", L + l0, L + l1), (R("ones", p=1), R("ramp", l0, l1, p=1)), (nidn, R("SRW%d" % t, l0, l1)))
+        nl, zb = l1 - l0, R("zb%d" % t, l0, l1)
+        group(R("PA", L + l0, L + l1), (R("ones", p=1), R("ramp", l0, l1, p=1)), (nidn, R("SRW", l0, l1)))
         PA = R("PA", l0, l1)
         mm(PA, idn, R("hw", l0, l1), True, False)
         if t == 1:
@@ -588,39 +576,46 @@ def rank_program(g, core, T, topo):
         for m in range(4):
             bank = "PD%d" % (m & 1)
             for p in range(4 * m, 4 * m + 4):
-                group(R(bank, (p & 3) * 128, (p & 3) * 128 + nl), (nidn, zb), (idn, R("XC%d" % h, p, 16 * nl, 16)))
-            for p in range(4 * m, 4 * m + 4):
-                ac(col3("DD", l0, l1, p), R(bank, (p & 3) * 128, (p & 3) * 128 + nl), AF.Abs)
+                group(R(bank, p & 3, 4 * nl, 4), (nidn, zb), (idn, R("XC%d" % h, p, 16 * nl, 16)))
+            ac((T.DD[:, l0:l1, 4 * m:4 * m + 4], "DD", l0, l1, ("k", 4 * m, 4 * m + 4), 4 * nl), R(bank, 0, 4 * nl), AF.Abs)
             for p in range(4 * m, 4 * m + 4):
                 mm(PA, sel("sel1", p), col3("DD", l0, l1, p), False, p == 15)
-            if m & 1:
-                j = m >> 1
-                P = R("PC%d" % h, 272 + 64 * j, 272 + 64 * j + 8 * nc)
-                group(P, (R("LA", p=1), R("r8", 0, 8 * nc, p=1)), (l16, R(("b8a", "b8b")[j], 0, 8 * nc, p=16)),
-                      *[(sel("selm", q), lane3("DD", l0, l1, q, 8 * j, 8 * j + 8)) for q in range(16)])
-                lo = 128 * h + 64 * j
-                scan(R("SD", lo, lo + 8 * nc), R("rneg8", 0, 8 * nc), P, ALU.add, ALU.max)
-        ts(R("cap", l0, l1), PA, R("thr%d" % t), None, ALU.is_lt)
-        tt(R("com", l0, l1), R("PA", L + l0, L + l1), R("cap", l0, l1), ALU.mult)
+        P = R("PC%d" % h, 272, 272 + nl)
+        group(P, (R("LL", p=17), R("b16", 0, nl, p=17)), *[(sel("selm", q), lane3("DD", l0, l1, q, 0, 16)) for q in range(16)])
+        scan(R("SD", l0, l1), R("rneg", 0, nl), P, ALU.add, ALU.max)
+        ac(R("cap", l0, l1), PA, AF.Identity, scale=-65536.0, bias=R("thB%d" % t))
+        tt(R("com", l0, l1), R("PA", L + l0, L + l1), R("cap", l0, l1), ALU.min)
 
     def best(t, h):
         l0, l1 = CH[h]
-        a, b, nl, nc = l0 // 16, l1 // 16, l1 - l0, (l1 - l0) // 16
-        lo = 128 * h + 7
-        tt(R("DI", a, b), R("SD", lo, lo + 8 * nc - 7, 8), R("SD", lo + 64, lo + 64 + 8 * nc - 7, 8), ALU.max)
-        ts(R("DA", a, b), R("DI", a, b), 2047, None, ALU.bitwise_and)
-        po = R("pxU", a, b)
+        a, b, nl = l0 // 16, l1 // 16, l1 - l0
+        ts(R("DA", a, b), R("SD", l0 + 15, l1, 16), 2047, None, ALU.bitwise_and)
+        po, ZS = R("pxU", a, b), R("ZS", l0, l1)
         ts(po, R("DA", a, b), -1.0, 2047.0, ALU.mult, ALU.add)
-        tt(R("ZS", l0, l1), X("XC%d" % h, 0, 16 * nl, po), R("zb%d" % t, l0, l1), ALU.add, off=[po])
-        ts(R("z16", l0, l1), R("ZS", l0, l1), 0.5, ZOFF - 0.25, ALU.mult, ALU.add)
+        x, zb = X("XC%d" % h, 0, 16 * nl, po), R("zb%d" % t, l0, l1)
+        if t == 0:
+            tt(ZS, x, zb, ALU.add, off=[po])
+        else:
+            ZS = R("PC%d" % h, 0, nl)
+            ac(R("xs", l0, l1), x, off=[po])
+            group(ZS, (idn, zb), (idn, R("xs", l0, l1)))
+        ts(R("z16", l0, l1), ZS, 0.5, ZOFF - 0.25, ALU.mult, ALU.add)
         ts(R(("zb1", "zf")[t], l0, l1), R("z16", l0, l1), -ZOFF, None, ALU.add)
+
+    def thin():
+        K, TT = R("ringS"), R("TT", 0, V)
+        ts(TT, K, R("rv0"), R("nrv"), ALU.is_equal, ALU.mult)
+        dma("G", TT[0], K[0], rd=[K, TT], wr=[TT], lat=5.0, cost=3.5, accum_op=ALU.add)
+        ts(R("e1"), K, R("come", 0, 1), R("ncm2"), ALU.is_equal, ALU.mult)
+        dma("G", TT[0], R("e1")[0], rd=[R("e1"), TT], wr=[TT], lat=5.0, cost=1.5, accum_op=ALU.add)
 
     def revoked(t):
         red(R("xr"), R("com"), ALU.max)
         ts(R("hi"), R("xr"), 1.0 / 256, -0.498, ALU.mult, ALU.add)
         ts(R("rv%d" % t), R("hi"), -256.0, R("xr"), ALU.mult, ALU.add)
 
-    ac(R("KvT0"), R("ringS", *v0))
+    send(R("SRW", GIV, GIV + V), R("ringS"), "tb", prev, nxt)
+    cp(R("KvT0"), first("ringS"))
     for h in range(2):
         step1(0, h)
     for t in range(2):
@@ -631,13 +626,14 @@ def rank_program(g, core, T, topo):
             choose(t, h)
             if t == 0:
                 move(h)
+        if t == 1:
+            thin()
         sources(t)
         if t == 0:
             for h, (l0, l1) in enumerate(CH):
                 o = R("voff", l0 // 16, l1 // 16)
                 cp(R("BvT", l0, l1), X("nbrS", 0, V, o), off=[o])
                 ac(R("KvT1", l0, l1), X("ringS", 0, V, o), off=[o])
-            cp(R("vW1"), R("SV", 15, L, 16))
             tt(R("vWi"), R("vW1"), R("i1"), ALU.add)
         for h in range(2):
             distances(t, h)
@@ -650,29 +646,25 @@ def rank_program(g, core, T, topo):
                     mm(R(last[m]), idn, R("TT", 512 * m, 512 * m + 512), True, False)
         revoked(t)
         if t == 0:
-            rv = R("rv0")
+            rv, cm = R("rv0"), R("come", 0, 1)
             ts(R("nrv"), rv, -1.0, None, ALU.mult)
             ts(R("m2rv"), rv, -2.0, None, ALU.mult)
             ts(R("krv"), rv, -1.0, 2048.0, ALU.mult, ALU.add)
-            cm = R("come", 0, 1)
             send(cm, rv, "rv", nxt, prev)
-            ts(R("TT", 0, V), R("ringS"), rv, R("nrv"), ALU.is_equal, ALU.mult)
-            dma("G", T.TT[:, 0:V], T.ringS[:, :], rd=[R("ringS"), R("TT", 0, V)], wr=[R("TT", 0, V)], lat=3.0, cost=1.0, accum_op=ALU.add)
+            ac(R("snd", L, L + 1), rv)
+            send(R("dlt", 0, L + 1), R("snd", 0, L + 1), "dl", prev, nxt)
+            ac(first("SRW", base=GIV), R("dlt", 0, L))
             ts(R("cm1"), cm, rv, None, ALU.not_equal)
-            ts(R("ncm"), cm, -1.0, None, ALU.mult)
+            ac(R("ncm"), cm, scale=-1.0)
             tt(R("ncm2"), R("ncm"), R("cm1"), ALU.mult)
-            ts(R("e1"), R("ringS"), cm, R("ncm2"), ALU.is_equal, ALU.mult)
-            dma("G", T.TT[:, 0:V], T.e1[:, :], rd=[R("e1"), R("TT", 0, V)], wr=[R("TT", 0, V)], lat=3.0, cost=1.0, accum_op=ALU.add)
-    dma("S", T.yz[:, :], T.zf[:, :], rd=[R("zf")])
     for m in range(4):
         a, b = 512 * m, 512 * m + 512
         ts(R("e1", a, b), R("TT", a, b), R("rv1"), R("rv1"), ALU.is_equal, ALU.mult)
         mm(R(last[m]), nidn, R("e1", a, b), False, True)
-        if m == 3:
-            cp(R("ykS", a, b), R(last[m]))
-        else:
-            ac(R("ykS", a, b), R(last[m]))
-        dma("Y", T.yk[:, a:b], T.ykS[:, a:b], rd=[R("ykS", a, b)])
+        (ac if COPY[m] == "S" else cp)(R("ykS", a, b), R(last[m]))
+        if m & 1:
+            dma("YS"[m >> 1], T.yk[:, a - 512:b], T.ykS[:, a - 512:b], rd=[R("ykS", a - 512, b)])
+    dma("Y", T.yz[:, :], T.zf[:, :], rd=[R("zf")])
     if not PLAN:
         PLAN.extend(order())
     for i in PLAN:

from concourse.mybir import AluOpType as ALU, AxisListType, ActivationFunctionType as AF

L, V = 224, 2048
CH = [(0, 96), (96, 224)]
GATHER = [[[(0, 48, "V"), (48, 96, "S")], [(96, 224, "S")]], [[(0, 96, "S")], [(96, 224, "S")]]]
PLACES = [[[(0, 48, "V"), (48, 96, "S")], [(96, 160, "V"), (160, 224, "S")]], [[(0, 96, "S")], [(96, 128, "V"), (128, 224, "S")]]]
RUNS = [[[(0, 96)], [(96, 224)]], [[(0, 96)], [(96, 224)]]]
COPY = "SSVV"
GIV = 240
ZOFF = 1025.0
BIGN = float(1 << 24)
NENG = 8
PASSES = 12000
WAKE, PWAKE, SWAKE, PE, HALF = 0.2, 0.15, 0.18, 0.00056, 4
HOP, FIRST, TABLE, ISSUE = 6.0, 2.0, 11.5, 0.8
SCRATCH, SMALL, PLAN, SPAN, GRAPH = {}, {}, [], [], []
B16, F16, F32, I32, U16 = "bfloat16", "float16", "float32", "int32", "uint16"
for _d, _list in (
        (B16, (("ringS", V), ("matS", 4096), ("BIG0", 17 * 128), ("BIG1", 17 * 128), ("XC0", 2048), ("XC1", 2048),
               ("SRW", GIV + V), ("snd", 240), ("dlt", 240), ("zb0", L), ("zb1", L),
               ("ones", 128), ("sel1", 144), ("selk", 144), ("selm", 144), ("blk", 128), ("blk16", 128), ("trid", 128),
               ("idn", 128), ("nidn", 128), ("n256", 128), ("n128", 128), ("l16", 128), ("pen", L), ("tripen", L), ("OH", 32),
               ("LL", 128), ("r17", 136), ("b17", 136), ("b17n", 136), ("b16", 128), ("xs", L), ("tpr0", 128), ("tpr1", 128),
               ("c16", 128), ("ramp", L), ("col", 128), ("colg", 128), ("c15", L),
               ("KvT0", L), ("KvT1", L), ("hv", L), ("ev", L), ("hn", L), ("hw", L), ("nm", L), ("mq", L),
               ("GG", L), ("GA", L), ("eG", L), ("eH", L), ("KvP", L), ("fil", L), ("ne", L), ("eq", L),
               ("TT", V + L), ("e1", V), ("ykS", V), ("FF", 14), ("Finc", 14), ("na", 14))),
        (F16, (("YY0", L), ("YY1", L), ("en", L), ("YW", L), ("z16", L))),
        (F32, (("zf", L), ("blkf", 128), ("rneg", L), ("rneg17", 136), ("V20", L), ("V21", L), ("M1", 238), ("MM", 238),
               ("PR", L), ("cap", L), ("ZS", L), ("HZ", L), ("BnF", L), ("Bm", L), ("wA", L), ("num", V), ("idnf", 128), ("SV", L), ("com", L), ("oh", L),
               ("come", 4), ("okf", 16), ("zer", 16),
               ("pf", 1), ("gf", 1), ("qc", 1), ("q15", 1), ("pc0", 1), ("pc1", 1), ("thB0", 1), ("thB1", 1), ("m16", 1), ("n16", 1),
               ("c16x", 1), ("rowc", 14), ("iW", 14), ("nk", 14), ("dW", 14), ("cA", 14), ("hW", 14), ("i1", 14), ("vW1", 14),
               ("vWi", 14), ("x1", 14), ("nd", 14), ("bb", 14), ("srv", 14), ("s1", 14), ("s2", 14), ("s3", 14), ("t1", 14), ("xr", 1),
               ("rv0", 1), ("rv1", 1), ("nrv", 1), ("m2rv", 1), ("krv", 1), ("cm1", 1), ("ncm", 1), ("ncm2", 1))),
        (I32, (("nbrS", V), ("thrI", 1), ("RI", L), ("SW", L), ("SH", L), ("SK", 238), ("SD", L), ("BvT", L), ("PI", L), ("PJ", L),
               ("pI", 1), ("qI", 1), ("gI", 1), ("KA", 14), ("KK", 14), ("DA", 14), ("HJ", 14), ("hi", 1), ("fi", 1), ("fj", 1))),
        (U16, (("Bn", L), ("PL", L), ("oKU", 28),
               ("noff", 14), ("posU", 14), ("kU", 14), ("pxU", 14), ("voff", 14), ("spU", 14), ("rp", 14)))):
    for _n, _w in _list:
        if _w in (1, 14) and _n != "thrI":
            _k = sum(1 for _v in SMALL.values() if _v[0] == "small" + _d)
            SMALL[_n] = ("small" + _d, 16 * _k, _w)
            SCRATCH["small" + _d] = ("sbuf", [128, 16 * _k + 16], _d)
        else:
            SCRATCH[_n] = ("sbuf", [128, _w], _d)
SCRATCH["E1"] = SCRATCH["E2"] = ("sbuf", [128, L, 17], B16)
SCRATCH["DD"] = ("sbuf", [128, L, 16], B16)
BANKS = ("PK0", "PK1", "PC0", "PC1", "PD0", "PD1", "PA", "PM")
for _n in BANKS:
    SCRATCH[_n] = ("psum", [128, 512], F32)
SEMAPHORES = (["sV", "sS", "sP", "sG"] + ["d%d" % i for i in range(20)]
              + [a + b for a in ("tb", "dl", "rv") for b in "rl"])


def rank_program(g, core, T, topo):
    rank = T.rank_of(core)
    if rank is None:
        return
    N = len(T.cores)
    queue = {"V": g.vector, "S": g.scalar, "P": g.tensor, "G": g, "Y": g.sync}
    semof = {"V": "sV", "S": "sS", "P": "sP", "G": "sG"}
    total = {}
    known = {e: {} for e in queue}
    log = {}

    def meet(lo, hi, tag, l2, h2, t2):
        if not (l2 < hi and lo < h2):
            return False
        if tag and t2 and tag[0] == t2[0]:
            if tag[0] == "k":
                return t2[1] < tag[2] and tag[1] < t2[2]
            return tag[1] == t2[1]
        return True

    def need(e, refs, write):
        out = []
        for name, lo, hi, tag in refs:
            for (l2, h2, w2, e2, s2, c2, k2, t2) in log.get(name, ()):
                if name in BANKS:
                    if e2 == e and (e == "P" or not (write or w2)):
                        continue
                elif not (write or w2) or not meet(lo, hi, tag, l2, h2, t2):
                    continue
                out.append((s2, c2, k2))
        return out

    def note(e, refs, write, s, c, snap):
        for name, lo, hi, tag in refs:
            acc = log.setdefault(name, [])
            if name in BANKS:
                acc[:] = [a for a in acc if not (a[3] == e and a[2] == write)]
            elif write:
                acc[:] = [a for a in acc if not (lo <= a[0] and a[1] <= hi and tag in (None, a[7]))]
            else:
                acc[:] = [a for a in acc if a[2] or not (a[3] == e and a[4] == s and lo <= a[0] and a[1] <= hi and tag in (None, a[7]))]
            acc.append((lo, hi, write, e, s, c, snap, tag))

    def waits(e, deps):
        todo = {}
        for s, c, k in deps:
            if known[e].get(s, 0) < c and todo.get(s, (0,))[0] < c:
                todo[s] = (c, k)
        for s in list(todo):
            c = todo[s][0]
            if any(o != s and todo[o][1].get(s, 0) >= c for o in todo):
                del todo[s]
        for s, (c, k) in todo.items():
            queue[e].wait_ge(T.sem[s], c)
            for a, b in k.items():
                known[e][a] = max(known[e].get(a, 0), b)
            known[e][s] = max(known[e].get(s, 0), c)

    ops = []

    def emit(e, fn, reads, writes, sem=None, inc=1, cost=0.06, lat=WAKE):
        ops.append((e, fn, [r[1:5] for r in reads], [r[1:5] for r in writes], sem or semof[e], inc, cost, lat))

    def issue(e, fn, rd, wr, s, inc, cost, lat):
        if e != "R":
            waits(e, need(e, rd, False) + need(e, wr, True))
            ins = fn()
            if ins is not None:
                ins.then_inc(T.sem[s], inc)
        total[s] = total.get(s, 0) + inc
        snap = dict(known[e]) if e != "R" else {}
        snap[s] = total[s]
        note(e, rd, False, s, total[s], snap)
        note(e, wr, True, s, total[s], snap)

    def order():
        succ, chain, acc = [[] for _ in ops], {}, {}
        for i, (e, fn, rd, wr, s, inc, cost, lat) in enumerate(ops):
            before = {}
            if e in "YS" and s[0] == "d":
                if e in chain:
                    before[chain[e]] = 0.0
                chain[e] = i
            for refs, write in ((rd, False), (wr, True)):
                for name, lo, hi, tag in refs:
                    for (l2, h2, w2, j, t2) in acc.get(name, ()):
                        same = ops[j][0] == e
                        if name in BANKS:
                            if same and not (write or w2):
                                continue
                        elif not (write or w2) or not meet(lo, hi, tag, l2, h2, t2):
                            continue
                        d = ops[j][7]
                        if ops[j][4] == semof.get(ops[j][0]):
                            d = (0.0 if e == "P" else SWAKE) if same else (PWAKE if e == "P" else WAKE)
                        before[j] = max(before.get(j, 0.0), d)
            for refs, write in ((rd, False), (wr, True)):
                for name, lo, hi, tag in refs:
                    a = acc.setdefault(name, [])
                    if write and name in BANKS:
                        a[:] = []
                    elif name in BANKS:
                        a[:] = [x for x in a if x[2] or ops[x[3]][0] == e]
                    elif write:
                        a[:] = [x for x in a if not (lo <= x[0] and x[1] <= hi and tag in (None, x[4]))]
                    a.append((lo, hi, write, i, tag))
            for j, d in before.items():
                if j != i:
                    succ[j].append((i, d))
        n = len(ops)
        pred = [[] for _ in ops]
        for j in range(n):
            for i, d in succ[j]:
                pred[i].append((j, d))
        eng, cost, tail = [o[0] for o in ops], [o[6] for o in ops], [o[7] for o in ops]
        kind = [o[3][0][0] if o[3] else "" for o in ops]
        GRAPH.append((succ, list(zip(eng, cost, tail, kind))))

        def place(seq, links, lead):
            end, busy = [0.0] * n, {e: [] for e in eng}
            for i in seq:
                t, c, line = lead[i], cost[i], busy[eng[i]]
                for j, d in links[i]:
                    if end[j] + d > t:
                        t = end[j] + d
                k = len(line)
                while k and line[k - 1][1] > t:
                    k -= 1
                while k < len(line) and line[k][0] < t + c:
                    t = max(t, line[k][1])
                    k += 1
                line.insert(k, (t, t + c))
                end[i] = t + c
            return end

        def forwards(key):
            for i in range(n):
                for j, d in pred[i]:
                    if key[j] > key[i]:
                        key[i] = key[j]
            end = place(sorted(range(n), key=lambda i: (key[i], i)), pred, [0.0] * n)
            return max(e + x for e, x in zip(end, tail)), end

        def again(end):
            back = place(sorted(range(n), key=lambda i: (-end[i], -i)), succ, tail)
            return forwards([-b for b in back])

        seed = [1]

        def draw():
            seed[0] = (seed[0] * 1103515245 + 12345) % (1 << 31)
            return seed[0] / (1 << 31)

        best_ = cur = forwards([float(i) for i in range(n)])
        for it in range(PASSES):
            size, shift, key, mid = (0.2, 0.5, 1.5, 3.0)[int(4 * draw())], {}, [], draw() * cur[0]
            for i in range(n):
                s = cur[1][i] - cost[i]
                if abs(s - mid) < 6:
                    k = (kind[i], int(s / 4))
                    if k not in shift:
                        shift[k] = size * (2 * draw() - 1) if draw() < 0.3 else 0.0
                    s += shift[k]
                key.append(s)
            a = forwards(key)
            if draw() < 0.3:
                b = again(a[1])
                a = a if a[0] < b[0] else b
            if a[0] <= cur[0] + 0.3 * (1 - it / PASSES) * draw() + 0.005:
                cur = a
            if a[0] < best_[0]:
                best_ = a
        SPAN.append(best_[0])
        return sorted(range(n), key=lambda i: (round(best_[1][i] - cost[i], 6), i))

    def wide(*refs):
        return all(SCRATCH[r[1]][0] == "sbuf" and SCRATCH[r[1]][2] in (B16, F16, U16) for r in refs)

    def vcost(n, per):
        return 0.00083 * max(64, n * per)

    def R(name, lo=0, hi=None, step=1, p=None):
        if name in SMALL:
            name, off, w = SMALL[name]
            lo, hi = lo + off, off + (w if hi is None else hi)
        hi = T[name].shape[1] if hi is None else hi
        ps = slice(None) if p is None else slice(0, p)
        ap = T[name][ps, lo:hi] if step == 1 else T[name][ps, lo:hi:step]
        return (ap, name, lo, hi, None if step == 1 else (step, lo % step), (hi - lo + step - 1) // step)

    def X(name, lo, hi, off):
        return (T[name][:, lo:hi].indirect(off[0]), name, lo, hi, None, 16 * off[5])

    def col3(name, l0, l1, k):
        return (T[name][:, l0:l1, k], name, l0, l1, ("k", k, k + 1), l1 - l0)

    def lane3(name, l0, l1, q, k0, k1):
        return (T[name][:, l0 + q:l1:16, k0:k1], name, l0, l1, ("k", k0, k1), (l1 - l0) // 16 * (k1 - k0))

    def cols(*xs):
        return [x for x in xs if isinstance(x, tuple)]

    def val(x):
        return x[0] if isinstance(x, tuple) else x

    def ts(out, a, s1, s2, op0, op1=None, off=()):
        rd = [a] + cols(s1, s2) + list(off)
        c = 0.05 + 0.00083 * 1.56 * out[5] if off else vcost(out[5], 0.5 if wide(out, a) else 1)
        if op1 is None:
            emit("V", lambda: g.vector.tensor_scalar(out[0], a[0], val(s1), None, op0), rd, [out], cost=c)
        else:
            emit("V", lambda: g.vector.tensor_scalar(out[0], a[0], val(s1), val(s2), op0, op1), rd, [out], cost=c)

    def tt(out, a, b, op, off=(), scatter=False):
        c = vcost(b[5], 1 if a[1] in BANKS or b[1] in BANKS else 2)
        if off:
            c = 0.05 + 0.00083 * b[5] * (3.8 if scatter else 1.56)
        emit("V", lambda: g.vector.tensor_tensor(out[0], a[0], b[0], op), [a, b] + list(off), [out], cost=c)

    def cp(out, a, off=()):
        c = 0.05 + 0.00083 * 1.56 * out[5] if off else vcost(out[5], 0.5 if wide(out, a) else 1)
        emit("V", lambda: g.vector.tensor_copy(out[0], a[0]), [a] + list(off), [out], cost=c)

    def scan(out, d0, d1, op0, op1):
        emit("V", lambda: g.vector.tensor_tensor_scan(out[0], d0[0], d1[0], 0.0, op0, op1), [d0, d1], [out], cost=vcost(out[5], 1))

    def red(out, a, op):
        emit("V", lambda: g.vector.tensor_reduce(out[0], a[0], AxisListType.X, op), [a], [out], cost=vcost(a[5], 1))

    def ac(out, a, func=AF.Copy, off=(), **kw):
        c = 0.065 + 0.00083 * 1.56 * out[5] if off else vcost(out[5], 1)
        rd, kw = [a] + list(off) + cols(*kw.values()), {k: val(x) for k, x in kw.items()}
        emit("S", lambda: g.scalar.activation(out[0], a[0], func, **kw), rd, [out], cost=c)

    def fill(out, c):
        emit("V", lambda: g.vector.memset(out[0], c), [], [out], cost=vcost(out[5], 0.5 if wide(out) else 1))

    def mm(out, lhsT, rhs, start, stop):
        c = PE * max(64, out[5]) * {B16: 1, F16: HALF, F32: 4}[SCRATCH[rhs[1]][2]]
        emit("P", lambda: g.tensor.matmul(out[0], lhsT[0], rhs[0], start, stop), [lhsT, rhs], [out], cost=c)

    def group(out, *terms):
        for i, (lhsT, rhs) in enumerate(terms):
            mm(out, lhsT, rhs, i == 0, i == len(terms) - 1)

    def iota(out, pattern, base, cm):
        emit("G", lambda: g.iota(out[0], pattern, base, cm, allow_small_or_imprecise_dtypes=True), [], [out], cost=0.13 + 0.00166 * out[5])

    ndma = [0]

    def dma(e, out, a, rd=(), wr=(), lat=1.0, cost=ISSUE, **kw):
        s = "d%d" % ndma[0]
        ndma[0] += 1
        emit(e, lambda: queue[e].dma_start(out, a, **kw), list(rd), list(wr), s, 16, cost=cost, lat=lat)

    def send(out, src, sem, dst, frm):
        rid, pid, _ = topo.addr(dst)
        mask = sum(1 << e for e in topo.engines(core, dst)[:NENG])

        def call():
            g.remote_dma(out[0], src[0], T.sem[sem + "r"], T.sem[sem + "l"], pid, rid, mask)
        flag = (None, sem + "l", 0, 1, None)
        emit("G", call, [src], [flag], sem + "l", NENG, 0.8 + FIRST * (sem == "tb"), HOP + TABLE * (sem == "tb"))
        emit("R", None, [flag], [out], sem + "r", len(topo.engines(frm, core)[:NENG]), 0.0, 0.1)

    prev, nxt = T.cores[(rank - 1) % N], T.cores[(rank + 1) % N]
    dma("S", T.zb0[:, :], T.z0[:, :], wr=[R("zb0")], lat=0.5)
    dma("Y", T.nbrS[:, :], T.nbr[:, :], wr=[R("nbrS")], lat=2.4)
    dma("S", T.ringS[:, :], T.ring[:, :], wr=[R("ringS")], lat=2.2)
    dma("Y", T.matS[:, :], T.mat[:, :], wr=[R("matS")], lat=4.2)
    dma("Y", T.thrI[:, :], T.thr[:, :], wr=[R("thrI")], lat=3.2)
    iota(R("pI"), [[1, 1]], 0, 1)
    iota(R("colg"), [[1, 8], [0, 16]], 0, 0)
    iota(R("tpr0", p=1), [[0, 8], [-1, 16]], 0, 0)
    iota(R("c15"), [[0, 14], [1, 16]], 0, 0)
    iota(R("col"), [[1, 128]], 0, 0)
    iota(R("rowc"), [[16, 14]], 0, 0)
    iota(R("r17", p=32), [[-1, 8], [0, 17]], 7, 0)
    iota(R("b17", p=32), [[0, 8], [-1, 17]], 256, -16)
    iota(R("V20"), [[18, L]], 1, 0)
    iota(R("ramp", p=1), [[-256, L]], 256 * L, 0)
    iota(R("num"), [[1, V]], 0, 0)
    fill(R("ones"), 1.0)
    fill(R("c16", p=1), 1.0 / 16)
    ts(R("qI"), R("pI"), 15, None, ALU.bitwise_and)
    ts(R("gI"), R("pI"), 4, None, ALU.arith_shift_right)
    cp(R("qc"), R("qI"))
    cp(R("gf"), R("gI"))
    cp(R("pf"), R("pI"))
    ts(R("blk"), R("colg"), R("gf"), None, ALU.is_equal)
    ts(R("l16"), R("c15", 0, 128), R("qc"), None, ALU.is_equal)
    ts(R("pen"), R("c15"), R("qc"), -BIGN, ALU.not_equal, ALU.mult)
    ts(R("tripen"), R("c15"), R("qc"), -4096.0, ALU.is_le, ALU.mult)
    ts(R("idn"), R("col"), R("pf"), None, ALU.is_equal)
    ts(R("trid"), R("col"), R("pf"), -1.0, ALU.is_lt, ALU.mult)
    tt(R("trid"), R("trid"), R("blk"), ALU.mult)
    fill(R("sel1"), 0.0)
    ac(R("sel1", 15, 143, 16), R("blk", 0, 128, 16))
    for name, of, c in (("blk16", "blk", 1.0 / 16), ("blkf", "blk", 1.0), ("idnf", "idn", 1.0), ("nidn", "idn", -1.0), ("n256", "idn", -256.0),
                        ("n128", "idn", -128.0), ("selk", "sel1", 4096.0), ("selm", "sel1", -2048.0)):
        ac(R(name), R(of), scale=c)
    ac(R("tpr1", p=1), R("tpr0", p=1), AF.Identity, bias=1.0)
    ac(R("q15"), R("qc"), AF.Identity, scale=-1.0, bias=15.0)
    fill(R("OH", 16, 32), 0.0)
    ts(R("OH", 0, 16), R("c15", 0, 16), R("q15"), None, ALU.is_equal)
    ts(R("m16"), R("pf"), 16.0, None, ALU.is_equal)
    ts(R("n16"), R("pf"), 16.0, None, ALU.not_equal)
    ac(R("c16x"), R("m16"), scale=256.0)
    ac(R("LL"), R("l16"), AF.Identity, scale=R("n16"), bias=R("c16x"))
    ac(R("b17", p=32), R("b17", p=32), AF.Identity, scale=R("n16", p=32))
    ac(R("r17", p=32), R("r17", p=32), AF.Identity, scale=R("m16", p=32))
    tt(R("b17", p=32), R("b17", p=32), R("r17", p=32), ALU.add)
    for c in range(8):
        ac(R("b16", 16 * c, 16 * c + 16, p=32), R("b17", 17 * c + 1, 17 * c + 17, p=32))
    fill(R("b17", 0, 136, 17, p=32), 0.0)
    ac(R("b17n", p=32), R("b17", p=32))
    fill(R("b17n", 0, 136, 17, p=16), float(1 << 23))
    for t in range(2):
        ac(R("pc%d" % t), R("qc"), AF.Identity, scale=811.0, bias=t - 0.375)
    fill(R("SRW", L, GIV), 0.0)
    fill(R("rneg"), 0.0)
    fill(R("rneg", 0, L, 16), -BIGN)
    fill(R("rneg17"), 0.0)
    fill(R("rneg17", 0, 136, 17), -BIGN)
    fill(R("zer"), 0.0)
    fill(R("okf"), 0.0)
    fill(col3("E2", 0, L, 0), 0.0)
    ac(R("iW"), R("rowc"), AF.Identity, bias=R("qc"))
    for h, (l0, l1) in enumerate(CH):
        ac(R("nk", l0 // 16, l1 // 16), R("iW", l0 // 16, l1 // 16), AF.Identity, scale=-1.0, bias=float(4096 + 2047 + l1))
    for name, c in (("dW", V), ("cA", -L), ("i1", 1)):
        ac(R(name), R("iW"), AF.Identity, bias=float(c))
    ts(R("rp"), R("rowc"), 1.0 / 16, None, ALU.mult)
    ts(R("thB0"), R("thrI"), 65536.0, None, ALU.mult)

    idn, nidn, blk, l16 = R("idn"), R("nidn"), R("blk"), R("l16", p=16)

    def sel(name, q):
        return R(name, 15 - q, 143 - q)

    def first(name, l0=0, l1=L, base=0):
        return R(name, base + 9 * l0, base + 9 * (l1 - 1) + 1, 9)

    def step1(t, h):
        l0, l1 = CH[h]
        a, b, nl, PK = l0 // 16, l1 // 16, l1 - l0, "PK%d" % h
        u, EJ, YY = R(PK, 384, 384 + nl), R(PK, 256, 256 + nl), R("YY%d" % t, l0, l1)
        group(u, (R("tpr%d" % t, p=1), R("c16", 0, nl, p=1)), (R("blk16"), R("zb%d" % t, l0, l1)))
        cp(R("RI", l0, l1), u)
        tt(EJ, u, R("RI", l0, l1), ALU.is_equal)
        tt(YY, EJ, first("nbrS", l0, l1) if t == 0 else R("BvT", l0, l1), ALU.mult)
        group(u, (l16, R("pen", 0, nl, p=16)), (blk, YY))
        scan(R("SW", l0, l1), R("rneg", 0, nl), u, ALU.add, ALU.max)
        cp(R("noff", a, b), R("SW", l0 + 15, l1, 16))

    def around(t, h):
        l0, l1 = CH[h]
        a, b, nl, PK, BIG = l0 // 16, l1 // 16, l1 - l0, "PK%d" % h, "BIG%d" % h
        no, Kv, Kn = R("noff", a, b), R("KvT%d" % t, l0, l1), R(BIG, 0, nl)
        cp(R("Bn", l0, l1), X("nbrS", 0, V, no), off=[no])
        (ac if t or h else cp)(Kn, X("ringS", 0, V, no), off=[no])
        for x, y, e in GATHER[t][h]:
            o = R("Bn", x, y)
            (ac if e == "S" else cp)(R(BIG, nl + 16 * (x - l0), nl + 16 * (y - l0)), X("ringS", 0, V, o), off=[o])
        ts(R("hv", l0, l1), Kv, 0.0, -1.0, ALU.is_equal, ALU.mult)
        ts(R("hn", l0, l1), Kn, 0.0, 2048.0, ALU.is_equal, ALU.mult)
        tv, tn = [(idn, Kv), (idn, R("hv", l0, l1))], [(idn, Kn), (idn, R("hn", l0, l1))]
        if t == 1:
            ts(R("ev", l0, l1), Kv, R("rv0"), R("m2rv"), ALU.is_equal, ALU.mult)
            ts(R("en", l0, l1), Kn, R("rv0"), R("krv"), ALU.is_equal, ALU.mult)
            tv.append((idn, R("ev", l0, l1)))
            tn.append((idn, R("en", l0, l1)))
        group(R(PK, 0, nl), *tv)
        group(R(PK, 128, 128 + nl), *tn)
        tt(R("HZ", l0, l1), R(PK, 128, 128 + nl), R("zb%d" % t, l0, l1), ALU.mult)
        tt(col3("E1", l0, l1, 0), R(PK, 0, nl), Kn, ALU.is_equal)
        if t == 0:
            cp(R("BnF", l0, l1), R("Bn", l0, l1))

    def request(t):
        P = R("PD0", 256, 256 + L)
        group(P, (l16, R("pen", p=16)), (R("blkf"), R("HZ")))
        scan(R("SH"), R("rneg"), P, ALU.add, ALU.max)
        ts(R("HJ"), R("SH", 15, L, 16), V - 1, None, ALU.bitwise_and)
        ts(R("hW"), R("HJ"), float(GIV - L), None, ALU.add)

    def compare(h, which, runs):
        l0, l1 = CH[h]
        nl, En = l1 - l0, "E%d" % (which + 1)
        for x, y in runs:
            lo = nl + 16 * (x - l0)
            for k in range(16):
                tt(col3(En, x, y, k + 1), R("PK%d" % h, 128 * which + x - l0, 128 * which + y - l0),
                   R("BIG%d" % h, lo + k, lo + 16 * (y - x), 16), ALU.is_equal)

    def count(h, which):
        l0, l1 = CH[h]
        w = 17 * (l1 - l0) // 16
        P = R("PC%d" % h, 136 * which, 136 * which + w)
        group(P, (R("LL", p=17), R(("b17", "b17n")[which], 0, w, p=17)),
              *[(sel("selk", q), lane3("E%d" % (which + 1), l0, l1, q, 0, 17)) for q in range(16)])
        return P

    def choose(t, h):
        l0, l1 = CH[h]
        a, b, nl = l0 // 16, l1 // 16, l1 - l0
        BIG, m0, m1 = "BIG%d" % h, 17 * a, 17 * b
        compare(h, 0, RUNS[t][h])
        ac(R("M1", m0, m1), count(h, 0))
        mn = R("M1", m0, m1, 17)
        ts(R("x1", a, b), mn, 8192.0, float(1 << 18), ALU.is_ge, ALU.mult)
        tt(mn, R("x1", a, b), R("nk", a, b), ALU.add)
        compare(h, 1, [(l0, l1)])
        tt(R("MM", m0, m1), count(h, 1), R("M1", m0, m1), ALU.min)
        scan(R("SK", m0, m1), R("rneg17", 0, m1 - m0), R("MM", m0, m1), ALU.add, ALU.max)
        ts(R("KA", a, b), R("SK", m0 + 16, m1, 17), 4095, None, ALU.bitwise_and)
        po = R("posU", a, b)
        ts(po, R("KA", a, b), -1.0, float(2047 + nl), ALU.mult, ALU.add)
        w, PR, Kw, V2 = X(BIG, 0, 17 * nl, po), R("PR", l0, l1), R("SRW", l0, l1), R("V2%d" % t, l0, l1)
        ac(Kw, w, off=[po], scale=-1.0)
        if t == 0:
            tt(PR, w, V2, ALU.mult, off=[po])
        else:
            P = R("PK%d" % h, 384, 384 + nl)
            ts(R("mq", l0, l1), Kw, R("nrv"), R("nrv"), ALU.is_equal, ALU.mult)
            group(P, (nidn, Kw), (idn, R("mq", l0, l1)))
            tt(PR, P, V2, ALU.mult)
        ts(R("PI", l0, l1), PR, 0.25, R("pc%d" % t), ALU.mult, ALU.add)
        ts(R("PJ", l0, l1), R("PI", l0, l1), 4095, None, ALU.bitwise_and)
        cp(R("PL", l0, l1), R("PJ", l0, l1))
        for x, y, e in PLACES[t][h]:
            o = R("PL", x, y)
            (ac if e == "S" else cp)(R("XC%d" % h, 16 * (x - l0), 16 * (y - l0)), X("matS", 0, 4096, o), off=[o])
        ts(R("hw", l0, l1), Kw, 0.0, 8192.0, ALU.is_equal, ALU.mult)
        if t == 1:
            ts(R("nm", l0, l1), Kw, R("nrv"), 8192.0, ALU.is_equal, ALU.mult)

    def move(h):
        l0, l1 = CH[h]
        a, b, nl = l0 // 16, l1 // 16, l1 - l0
        ts(R("KK", a, b), R("KA", a, b), 2048 + 15, None, ALU.bitwise_and)
        ko, YW, YY = R("kU", a, b), R("YW", l0, l1), R("YY0", l0, l1)
        ts(ko, R("KK", a, b), 16.0, None, ALU.min)
        tt(YW, X("OH", 0, 32, ko), R("BnF", l0, l1), ALU.mult, off=[ko])
        group(R("PM", 256, 256 + nl), (l16, R("pen", 0, nl, p=16)), (blk, YW))
        scan(R("SV", l0, l1), R("rneg", 0, nl), R("PM", 256, 256 + nl), ALU.add, ALU.max)
        th, vo, wA = R("t1", a, b), R("voff", a, b), R("wA", l0, l1)
        ts(th, R("KK", a, b), 16.0, None, ALU.is_ge)
        tt(th, th, R("SW", l0 + 15, l1, 16), ALU.mult)
        tt(R("vW1", a, b), R("SV", l0 + 15, l1, 16), th, ALU.add)
        cp(vo, R("vW1", a, b))
        ac(wA, X("num", 0, V, vo), off=[vo])
        ac(R("V21", l0, l1), wA, AF.Identity, bias=1.0, scale=2.0)
        EJ = R("PK%d" % h, 256, 256 + nl)
        tt(R("Bm", l0, l1), first("nbrS", l0, l1), YY, ALU.subtract)
        tt(EJ, EJ, wA, ALU.mult)
        tt(first("nbrS", l0, l1), EJ, R("Bm", l0, l1), ALU.add)

    def sources(t):
        if t == 1:
            group(R("PM", 256, 256 + L), (idn, R("KvT1")), (idn, R("ev")))
            ac(R("KvP"), R("PM", 256, 256 + L))
        ts(R("FF"), R("SK", 16, 238, 17), 8192.0, None, ALU.is_lt)
        ts(R("nd"), R("SK", 16, 238, 17), float(1 << 18), None, ALU.is_lt)
        scan(R("Finc"), R("FF"), R("zer", 0, 14), ALU.add, ALU.add)
        tt(R("bb"), R("nd"), R("FF"), ALU.subtract)
        group(R("PM", 480, 494), (blk, R("Finc")), (R("trid"), R("FF")))
        if t == 0:
            group(R("PM", 496, 497), (R("ones"), R("Finc", 13, 14)))
        ts(R("srv"), R("PM", 480, 494), 48.0, None, ALU.is_le)
        if t == 0:
            cp(R("fi"), R("PM", 496, 497))
            ts(R("fj"), R("fi"), 15, None, ALU.bitwise_and)
            ts(R("thB1"), R("fj"), 65536.0, R("thB0"), ALU.mult, ALU.add)
        tt(R("s1"), R("bb"), R("cA"), ALU.mult)
        tt(R("srv"), R("srv"), R("FF"), ALU.mult)
        tt(R("s2"), R("srv"), R("hW"), ALU.mult)
        tt(R("s1"), R("s1"), R("s2"), ALU.add)
        sp = R("spU")
        ts(sp, R("s1"), float(L), None, ALU.add)
        src, P = X("SRW", 0, GIV + V, sp), R("PM", 0, L)
        if t == 0:
            ac(R("GA"), src, AF.Abs, off=[sp])
            group(P, (R("n256"), R("KvT0")), (idn, R("GA")))
            tt(first("ringS"), P, R("KvT0"), ALU.max)
            ac(R("snd", 0, L), first("ringS"))
            return
        ac(R("GG"), src, off=[sp])
        ac(R("GA"), R("GG"), AF.Abs)
        rvn = R("dlt", L, L + 1)
        ts(R("eG"), R("GG"), rvn, rvn, ALU.is_equal, ALU.mult)
        ts(R("eH"), R("GG"), R("nrv"), R("nrv"), ALU.is_equal, ALU.mult)
        group(P, (R("n256"), R("KvT1")), (R("n128"), R("ev")), (idn, R("GA")), (nidn, R("eG")), (idn, R("eH")))
        tt(R("fil"), P, R("KvP"), ALU.max)
        ts(R("ne"), R("fil"), R("come", 0, 1), R("ncm"), ALU.is_equal, ALU.mult)
        tt(R("s3"), R("srv"), R("bb"), ALU.add)
        ts(R("na"), R("s3"), -1.0, 1.0, ALU.mult, ALU.add)
        tt(R("s3"), R("s3"), R("vWi"), ALU.mult)
        tt(R("okf", 0, 14), R("s3"), R("i1"), ALU.subtract)
        ac(R("oh"), X("okf", 0, 16, R("rp")), off=[R("rp")])
        P, Q = R("PK0", 0, L), R("PK0", 256, 270)
        group(P, (l16, R("tripen", p=16)), (R("idnf"), R("wA")))
        tt(R("eq"), P, R("oh"), ALU.is_equal)
        group(Q, (idn, R("na")), *[(sel("sel1", q), R("eq", q, L, 16)) for q in range(16)])
        ts(R("t1"), Q, 0.5, 4096.0, ALU.is_ge, ALU.mult)
        tt(R("t1"), R("t1"), R("dW"), ALU.min)
        tt(R("t1"), R("t1"), R("vW1"), ALU.max)
        cp(R("oKU", 0, 28, 2), R("t1"))
        for c in range(13, -1, -1):
            o = R("oKU", 2 * c, 2 * c + 1)
            tt(X("TT", 0, V + L, o), R("fil", 16 * c, 16 * c + 16), R("ne", 16 * c, 16 * c + 16), ALU.add, off=[o], scatter=True)

    def distances(t, h):
        l0, l1 = CH[h]
        nl, zb = l1 - l0, R("zb%d" % t, l0, l1)
        group(R("PA", L + l0, L + l1), (R("ones", p=1), R("ramp", l0, l1, p=1)), (nidn, R("SRW", l0, l1)))
        PA = R("PA", l0, l1)
        mm(PA, idn, R("hw", l0, l1), True, False)
        if t == 1:
            mm(PA, idn, R("nm", l0, l1), False, False)
        for m in range(4):
            bank = "PD%d" % (m & 1)
            for p in range(4 * m, 4 * m + 4):
                group(R(bank, p & 3, 4 * nl, 4), (nidn, zb), (idn, R("XC%d" % h, p, 16 * nl, 16)))
            ac((T.DD[:, l0:l1, 4 * m:4 * m + 4], "DD", l0, l1, ("k", 4 * m, 4 * m + 4), 4 * nl), R(bank, 0, 4 * nl), AF.Abs)
            for p in range(4 * m, 4 * m + 4):
                mm(PA, sel("sel1", p), col3("DD", l0, l1, p), False, p == 15)
        P = R("PC%d" % h, 272, 272 + nl)
        group(P, (R("LL", p=17), R("b16", 0, nl, p=17)), *[(sel("selm", q), lane3("DD", l0, l1, q, 0, 16)) for q in range(16)])
        scan(R("SD", l0, l1), R("rneg", 0, nl), P, ALU.add, ALU.max)
        ac(R("cap", l0, l1), PA, AF.Identity, scale=-65536.0, bias=R("thB%d" % t))
        tt(R("com", l0, l1), R("PA", L + l0, L + l1), R("cap", l0, l1), ALU.min)

    def best(t, h):
        l0, l1 = CH[h]
        a, b, nl = l0 // 16, l1 // 16, l1 - l0
        ts(R("DA", a, b), R("SD", l0 + 15, l1, 16), 2047, None, ALU.bitwise_and)
        po, ZS = R("pxU", a, b), R("ZS", l0, l1)
        ts(po, R("DA", a, b), -1.0, 2047.0, ALU.mult, ALU.add)
        x, zb = X("XC%d" % h, 0, 16 * nl, po), R("zb%d" % t, l0, l1)
        if t == 0:
            tt(ZS, x, zb, ALU.add, off=[po])
        else:
            ZS = R("PC%d" % h, 0, nl)
            ac(R("xs", l0, l1), x, off=[po])
            group(ZS, (idn, zb), (idn, R("xs", l0, l1)))
        ts(R("z16", l0, l1), ZS, 0.5, ZOFF - 0.25, ALU.mult, ALU.add)
        ts(R(("zb1", "zf")[t], l0, l1), R("z16", l0, l1), -ZOFF, None, ALU.add)

    def thin():
        K, TT = R("ringS"), R("TT", 0, V)
        ts(TT, K, R("rv0"), R("nrv"), ALU.is_equal, ALU.mult)
        dma("G", TT[0], K[0], rd=[K, TT], wr=[TT], lat=5.0, cost=3.5, accum_op=ALU.add)
        ts(R("e1"), K, R("come", 0, 1), R("ncm2"), ALU.is_equal, ALU.mult)
        dma("G", TT[0], R("e1")[0], rd=[R("e1"), TT], wr=[TT], lat=5.0, cost=1.5, accum_op=ALU.add)

    def revoked(t):
        red(R("xr"), R("com"), ALU.max)
        ts(R("hi"), R("xr"), 1.0 / 256, -0.498, ALU.mult, ALU.add)
        ts(R("rv%d" % t), R("hi"), -256.0, R("xr"), ALU.mult, ALU.add)

    send(R("SRW", GIV, GIV + V), R("ringS"), "tb", prev, nxt)
    cp(R("KvT0"), first("ringS"))
    for h in range(2):
        step1(0, h)
    for t in range(2):
        for h in range(2):
            around(t, h)
        request(t)
        for h in range(2):
            choose(t, h)
            if t == 0:
                move(h)
        if t == 1:
            thin()
        sources(t)
        if t == 0:
            for h, (l0, l1) in enumerate(CH):
                o = R("voff", l0 // 16, l1 // 16)
                cp(R("BvT", l0, l1), X("nbrS", 0, V, o), off=[o])
                ac(R("KvT1", l0, l1), X("ringS", 0, V, o), off=[o])
            tt(R("vWi"), R("vW1"), R("i1"), ALU.add)
        for h in range(2):
            distances(t, h)
            best(t, h)
            if t == 0:
                step1(1, h)
            if t == 1 and h == 0:
                last = ("PK0", "PK1", "PM", "PC0")
                for m in range(4):
                    mm(R(last[m]), idn, R("TT", 512 * m, 512 * m + 512), True, False)
        revoked(t)
        if t == 0:
            rv, cm = R("rv0"), R("come", 0, 1)
            ts(R("nrv"), rv, -1.0, None, ALU.mult)
            ts(R("m2rv"), rv, -2.0, None, ALU.mult)
            ts(R("krv"), rv, -1.0, 2048.0, ALU.mult, ALU.add)
            send(cm, rv, "rv", nxt, prev)
            ac(R("snd", L, L + 1), rv)
            send(R("dlt", 0, L + 1), R("snd", 0, L + 1), "dl", prev, nxt)
            ac(first("SRW", base=GIV), R("dlt", 0, L))
            ts(R("cm1"), cm, rv, None, ALU.not_equal)
            ac(R("ncm"), cm, scale=-1.0)
            tt(R("ncm2"), R("ncm"), R("cm1"), ALU.mult)
    for m in range(4):
        a, b = 512 * m, 512 * m + 512
        ts(R("e1", a, b), R("TT", a, b), R("rv1"), R("rv1"), ALU.is_equal, ALU.mult)
        mm(R(last[m]), nidn, R("e1", a, b), False, True)
        (ac if COPY[m] == "S" else cp)(R("ykS", a, b), R(last[m]))
        if m & 1:
            dma("YS"[m >> 1], T.yk[:, a - 512:b], T.ykS[:, a - 512:b], rd=[R("ykS", a - 512, b)])
    dma("Y", T.yz[:, :], T.zf[:, :], rd=[R("zf")])
    if not PLAN:
        PLAN.extend(order())
    for i in PLAN:
        issue(*ops[i])
    for s, c in total.items():
        if known["Y"].get(s, 0) < c:
            g.sync.wait_ge(T.sem[s], c)
